import numpy as np
import ml_dtypes


def mxq(x, axis, fmt="e4m3"):
    dtype, down = {"e4m3": (ml_dtypes.float8_e4m3fn, 7), "e5m2": (ml_dtypes.float8_e5m2, 14)}[fmt]
    v = np.moveaxis(np.asarray(x, np.float32).astype(ml_dtypes.bfloat16).astype(np.float64), axis, -1)
    blocks = v.reshape(v.shape[:-1] + (-1, 32))
    amax = np.abs(blocks).max(-1, keepdims=True)
    byte = np.maximum(np.where(amax > 0, np.frexp(amax)[1] - 1 + 127, 0) - down, 1)
    scale = np.exp2(byte - 127.0)
    codes = (blocks / scale).astype(np.float32).astype(dtype).astype(np.float64)
    return np.moveaxis((codes * scale).reshape(v.shape), -1, axis)


WIDE = False


def mx_kscale(k):
    if not WIDE:
        return np.ones(k)
    levels = np.array([10, -10, 5, -5, 0])
    if k % 512:
        return np.exp2(np.random.permutation(np.resize(levels, k // 32))).repeat(32)
    a = np.empty((k // 512, 16))
    for p in range(k // 512):
        a[p, :8] = np.random.permutation(np.resize(levels, 8))
        for g in range(8):
            far = levels[np.abs(levels - a[p, g]) >= 10]
            a[p, g + 8] = far[np.random.randint(len(far))]
    return np.exp2(a.ravel()).repeat(32)


def f64(x):
    return np.asarray(x).astype(np.float64)


def striped(idx):
    return np.tile(idx.reshape(-1, 16).T, (8, 1)).astype(np.uint16)


def unstriped(offs):
    return offs[:16].T.reshape(-1).astype(np.int64)


E2M1 = np.array([0.0, 0.5, 1.0, 1.5, 2.0, 3.0, 4.0, 6.0, -0.0, -0.5, -1.0, -1.5, -2.0, -3.0, -4.0, -6.0])


def pack_weight(w, fmt):
    k, n = w.shape
    w = f64(np.asarray(w, np.float32).astype(ml_dtypes.bfloat16)).reshape(k // 32, 32, n)
    amax = np.abs(w).max(1)
    if fmt == "e4m3":
        byte = np.frexp(amax)[1] - 1 + 127 - 7
    else:
        mant, ex = np.frexp(amax / 6.0)
        byte = np.where(mant > 0.5, ex, ex - 1) + 127
    byte = np.clip(np.where(amax > 0, byte, 1), 1, 254)
    scaled = (w * np.exp2(127.0 - byte)[:, None, :]).reshape(k, n).astype(np.float32)
    by_word = np.ascontiguousarray(scaled.reshape(k // 512, 128, 4, n).transpose(0, 1, 3, 2))
    if fmt == "e4m3":
        words = by_word.astype(ml_dtypes.float8_e4m3fn).view(np.uint8)
    else:
        c = by_word.astype(ml_dtypes.float4_e2m1fn).view(np.uint8) & 0xF
        words = (c[..., 0::2] | (c[..., 1::2] << 4)).reshape(k // 512, 128, 2 * n)
    return np.ascontiguousarray(words), np.ascontiguousarray(byte.astype(np.uint8).reshape(k // 512, 16, n))


def unpack_weight(words, scales, fmt):
    g, _, n = scales.shape
    words = np.ascontiguousarray(words).reshape(g, 128, n, -1)
    if fmt == "e4m3":
        vals = words.view(ml_dtypes.float8_e4m3fn).astype(np.float64)
    else:
        nib = np.empty((g, 128, n, 4), np.uint8)
        nib[..., 0::2] = words & 0xF
        nib[..., 1::2] = words >> 4
        vals = E2M1[nib]
    vals = vals * np.repeat(np.exp2(scales.astype(np.float64) - 127.0), 8, axis=1)[..., None]
    return vals.transpose(0, 1, 3, 2).reshape(g * 512, n)


def d_relu2(v):
    return 2.0 * np.maximum(v, 0.0)


K, T, E, C, H, N = 512, 768, 6, 256, 512, 1024


def by_expert(wq, xq):
    return np.concatenate([wq[e].T @ xq[:, e * C:(e + 1) * C] for e in range(E)], axis=1)


def setup_inputs():
    n = np.random.standard_normal
    s = mx_kscale(N)[:, None]
    u = mx_kscale(H)
    first = np.random.permutation(np.repeat(np.arange(E), T // E))
    second = (first + 1 + np.random.permutation(np.repeat(np.arange(E - 1), -(-T // (E - 1)))[:T])) % E
    while np.bincount(second, minlength=E).max() != T // E:
        load = np.bincount(second, minlength=E); hi, lo = int(load.argmax()), int(load.argmin())
        t = np.flatnonzero((second == hi) & (first != lo))[0]; second[t] = lo
    slot_token = np.empty(E * C, np.int64); pos = np.empty((2, T), np.int64); fill = np.zeros(E, np.int64)
    place = np.stack([np.random.permutation(C) for _ in range(E)])
    for r, deal in enumerate((first, second)):
        for t in np.random.permutation(T):
            e = deal[t]; j = e * C + place[e, fill[e]]; fill[e] += 1; slot_token[j] = t; pos[r, t] = j
    g = np.random.uniform(0.2, 0.8, T)
    w_slot = np.empty(E * C); w_slot[pos[0]] = g; w_slot[pos[1]] = 1.0 - g
    w2 = [pack_weight(m, "e2m1") for m in n((E, N, H)) / np.sqrt(N) / s[None] * u[None, None, :]]
    w1 = [pack_weight(m, "e2m1") for m in n((E, H, K)) / np.sqrt(H) / u[None, :, None]]
    return {
        "dyT": (n((N, T)) * s).astype(np.float32),
        "a": n((H, E * C)).astype(np.float32),
        "w2_words": np.stack([m[0] for m in w2]),
        "w2_scales": np.stack([m[1] for m in w2]),
        "w1_words": np.stack([m[0] for m in w1]),
        "w1_scales": np.stack([m[1] for m in w1]),
        "gate": np.tile(w_slot, (N, 1)).astype(np.float32),
        "offs": striped(slot_token),
        "pos1": striped(pos[0]),
        "pos2": striped(pos[1]),
    }


def reference(dyT, a, w2_words, w2_scales, w1_words, w1_scales, gate, offs, pos1, pos2):
    idx = unstriped(offs)
    w2 = np.stack([unpack_weight(w2_words[e], w2_scales[e], "e2m1") for e in range(E)])
    w1 = np.stack([unpack_weight(w1_words[e], w1_scales[e], "e2m1") for e in range(E)])
    gq = mxq(f64(gate) * f64(dyT)[:, idx], 0, "e4m3")
    dh = by_expert(w2, gq)
    da = dh * d_relu2(f64(a))
    dx = by_expert(w1, mxq(da, 0, "e4m3"))
    return dx[:, unstriped(pos1)] + dx[:, unstriped(pos2)]

@@ -1,0 +1,270 @@
+from contextlib import ExitStack
+
+import concourse.mybir as mybir
+from concourse.masks import make_identity
+
+N, T, E, C, H, K = 1024, 768, 6, 256, 512, 512
+S = E * C
+P = 128
+PACK = 4
+FLOPS = 2 * S * (N * H + H * K)
+
+F32 = mybir.dt.float32
+BF16 = mybir.dt.bfloat16
+I32 = mybir.dt.int32
+U32 = mybir.dt.uint32
+U16 = mybir.dt.uint16
+U8 = mybir.dt.uint8
+FP8X4 = mybir.dt.float8_e4m3fn_x4
+FP4X4 = mybir.dt.float4_e2m1fn_x4
+MULT = mybir.AluOpType.mult
+ADD = mybir.AluOpType.add
+MAX = mybir.AluOpType.max
+RELU = mybir.ActivationFunctionType.Relu
+COPY = mybir.ActivationFunctionType.Copy
+
+CHUNKS = ((0, 384), (384, 384), (768, 384), (1152, 256), (1408, 128))
+ON_GPSIMD = (0, 1)
+
+
+def tile_moe_bdx_mlp_relu2_kernel(
+    tc, dyT, a, w2_words, w2_scales, w1_words, w1_scales, gate, offs, pos1, pos2, out
+):
+    nc = tc.nc
+    with ExitStack() as ctx:
+        lists = ctx.enter_context(tc.tile_pool(name="lists", bufs=1))
+        keep = ctx.enter_context(tc.tile_pool(name="keep", bufs=1))
+        stage = ctx.enter_context(tc.tile_pool(name="stage", bufs=3))
+        ps_dh = ctx.enter_context(tc.psum_pool(name="ps_dh", bufs=3))
+        ps_turn = ctx.enter_context(tc.psum_pool(name="ps_turn", bufs=2))
+        ps_dx = ctx.enter_context(tc.psum_pool(name="ps_dx", bufs=3))
+
+        offs_sb = lists.tile([P, S // 16], U16, name="offs_sb")
+        pos1_sb = lists.tile([P, T // 16], U16, name="pos1_sb")
+        pos2_sb = lists.tile([P, T // 16], U16, name="pos2_sb")
+
+        ident = keep.tile([P, P], F32, name="ident")
+        w2_sc = keep.tile([P, 2 * E, H], U8, name="w2_sc", align_bytes=64)
+        w1_sc = keep.tile([P, E, K], U8, name="w1_sc", align_bytes=64)
+        w2 = [keep.tile([P, 2, 2 * H], U8, name=f"w2_{e}", align_bytes=64) for e in range(E)]
+        w1 = [keep.tile([P, 2 * K], U8, name=f"w1_{e}", align_bytes=64) for e in range(E)]
+        dy = [keep.tile([P, T], F32, name=f"dy_{m}") for m in range(N // P)]
+        gates = [keep.tile([P, n], F32, name=f"gate_{c0}") for c0, n in CHUNKS]
+        saved = [keep.tile([P, PACK, 2 * C], F32, name=f"saved_{b}") for b in range(3)]
+        da_codes = [keep.tile([P, C], U32, name=f"da_codes_{e}", align_bytes=64) for e in range(E)]
+        da_scales = [keep.tile([P, C], U8, name=f"da_scales_{e}", align_bytes=64) for e in range(E)]
+        relu_a = [keep.tile([P, C, PACK], F32, name=f"relu_a_{e}") for e in ON_GPSIMD]
+        dh_copy = [keep.tile([P, C, PACK], F32, name=f"dh_copy_{e}") for e in ON_GPSIMD]
+        dx = keep.tile([P, K // P, S], F32, name="dx")
+
+        nc.gpsimd.memset(w2_sc[:].rearrange("p g i -> p (g i)").bitcast(I32), 0)
+        nc.gpsimd.memset(w1_sc[:].rearrange("p g i -> p (g i)").bitcast(I32), 0)
+        make_identity(nc, ident[:])
+
+        dy_rows = dyT.rearrange("(s p j) t -> s j p t", s=2, j=PACK)
+        a_rows = a.rearrange("(p t) c -> p t c", t=PACK)
+        w2_rows = w2_scales.bitcast(I32).rearrange("e s f i -> f (e s) i")
+        w1_rows = w1_scales.bitcast(I32).rearrange("e s f i -> f (e s) i")
+
+        def load_gate(c):
+            c0, n = CHUNKS[c]
+            nc.sync.dma_start(out=gates[c][:], in_=gate[0:P, c0 : c0 + n])
+
+        def load_saved(b):
+            nc.sync.dma_start(out=saved[b][:], in_=a_rows[:, :, 2 * C * b : 2 * C * (b + 1)])
+
+        def load_w2(e):
+            nc.sync.dma_start(out=w2[e][:].bitcast(I32), in_=w2_words[e].rearrange("s p b -> p s b").bitcast(I32))
+
+        def load_w1(e):
+            nc.sync.dma_start(out=w1[e][:].bitcast(I32), in_=w1_words[e, 0].bitcast(I32))
+
+        nc.sync.dma_start(offs_sb[:], offs)
+        load_gate(0)
+        for m in range(N // P):
+            nc.sync.dma_start(out=dy[m][:], in_=dy_rows[m // PACK, m % PACK])
+        load_gate(1)
+        for q in range(4):
+            nc.sync.dma_start(out=w2_sc[32 * q : 32 * q + 4].bitcast(I32), in_=w2_rows[4 * q : 4 * q + 4])
+        load_w2(0)
+        load_w2(1)
+        load_saved(0)
+        load_gate(2)
+        load_w2(2)
+        load_w2(3)
+        load_gate(3)
+        load_gate(4)
+        load_w2(4)
+        load_w2(5)
+        load_saved(1)
+        for q in range(4):
+            nc.sync.dma_start(out=w1_sc[32 * q : 32 * q + 4].bitcast(I32), in_=w1_rows[4 * q : 4 * q + 4])
+        load_saved(2)
+        for e in range(E):
+            load_w1(e)
+        nc.sync.dma_start(pos1_sb[:], pos1)
+        nc.sync.dma_start(pos2_sb[:], pos2)
+
+        rounded = {}
+        g_codes = {}
+        turned = {}
+        products = {}
+
+        def gather(c, s, meanwhile=None):
+            c0, n = CHUNKS[c]
+            g = stage.tile([P, PACK, n], F32, name="g", align_bytes=64)
+            for j in range(PACK):
+                if j == PACK - 1 and meanwhile:
+                    meanwhile()
+                nc.vector.tensor_tensor(
+                    g[:, j, :], dy[PACK * s + j][:].indirect(offs_sb[:, c0 // 16 : (c0 + n) // 16]), gates[c][:], MULT
+                )
+            rounded[c, s] = stage.tile([P, n, PACK], BF16, name="g_bf16", align_bytes=64)
+            nc.scalar.copy(
+                out=rounded[c, s][:].rearrange("p (c i) j -> p c j i", i=4), in_=g[:].rearrange("p j (c i) -> p c j i", i=4)
+            )
+
+        def quantise(c, s):
+            c0, n = CHUNKS[c]
+            codes = stage.tile([P, n], U32, name=f"g_codes_{s}", align_bytes=64)
+            scales = stage.tile([P, n], U8, name=f"g_scales_{s}", align_bytes=64)
+            flat = rounded[c, s][:].rearrange("p c j -> p (c j)")
+            done = 0
+            for width in (512, 256, 128):
+                if n - done >= width:
+                    cols = slice(done, done + width)
+                    nc.vector.quantize_mx(
+                        out=codes[:, cols].bitcast(FP8X4),
+                        scales=scales[:, cols],
+                        in_=flat[:, PACK * done : PACK * (done + width)],
+                    )
+                    done += width
+            for b in range(n // P):
+                cols = slice(b * P, (b + 1) * P)
+                g_codes[c0 // P + b, s] = (codes[:, cols], scales[:, cols])
+
+        def product_dh(b):
+            e = b * P // C
+            acc = ps_dh.tile([P, H], F32, name="dh")
+            for s in range(2):
+                codes, scales = g_codes[b, s]
+                nc.tensor.matmul_mx(
+                    out=acc[:],
+                    lhsT=codes.bitcast(FP8X4),
+                    lhsT_scale=scales,
+                    rhs=w2[e][:, s, :].bitcast(FP4X4),
+                    rhs_scale=w2_sc[:, 2 * e + s, :],
+                    start=(s == 0),
+                    stop=(s == 1),
+                )
+            dh = stage.tile([P, PACK, P], F32, name="dh_sb")
+            nc.scalar.copy(out=dh[:], in_=acc[:].rearrange("p (m t) -> p t m", t=PACK))
+            return dh
+
+        def turn(b, dh):
+            turned[b] = ps_turn.tile([P, PACK, P], F32, name="turned")
+            for t in range(PACK):
+                nc.tensor.transpose(turned[b][:, t, :], dh[:, t, :], ident[:])
+
+        def first_layer(c):
+            quantise(c, 1)
+            c0, n = CHUNKS[c]
+            blocks = range(c0 // P, (c0 + n) // P)
+            dh = product_dh(blocks[0])
+            for b in blocks[1:]:
+                following = product_dh(b)
+                turn(b - 1, dh)
+                dh = following
+            turn(blocks[-1], dh)
+            for b in blocks:
+                e, h = divmod(b, C // P)
+                if e in ON_GPSIMD:
+                    nc.scalar.copy(
+                        out=dh_copy[e][:, h * P : (h + 1) * P, :], in_=turned[b][:].rearrange("p t c -> p c t")
+                    )
+
+        def slots_of(b):
+            cols = slice(b * P % (2 * C), b * P % (2 * C) + P)
+            return saved[b * P // (2 * C)][:, :, cols].rearrange("p t c -> p c t")
+
+        def make_relu(e):
+            nc.scalar.activation(
+                out=relu_a[e][:].rearrange("p (c i) t -> p c t i", i=4),
+                in_=saved[0][:, :, e * C : (e + 1) * C].rearrange("p t (c i) -> p c t i", i=4),
+                func=RELU,
+            )
+
+        def make_da(e):
+            da = stage.tile([P, C, PACK], BF16, name="g" if e == len(ON_GPSIMD) else "da", align_bytes=64)
+            for h in range(C // P):
+                b = e * C // P + h
+                nc.vector.scalar_tensor_tensor(
+                    out=da[:, h * P : (h + 1) * P, :],
+                    in0=slots_of(b),
+                    scalar=0.0,
+                    in1=turned[b][:].rearrange("p t c -> p c t"),
+                    op0=MAX,
+                    op1=MULT,
+                )
+            products[e] = da[:].rearrange("p c t -> p (c t)")
+
+        def quantise_da(e):
+            nc.vector.quantize_mx(out=da_codes[e][:].bitcast(FP8X4), scales=da_scales[e][:], in_=products[e])
+
+        def product_dx(e, k0, k1, on_vector=False):
+            acc = ps_dx.tile([P, k1 - k0, C], F32, name="dx_acc")
+            for k in range(k0, k1):
+                nc.tensor.matmul_mx(
+                    out=acc[:, k - k0, :],
+                    lhsT=w1[e][:, 2 * k * P : 2 * (k + 1) * P].bitcast(FP4X4),
+                    lhsT_scale=w1_sc[:, e, k * P : (k + 1) * P],
+                    rhs=da_codes[e][:].bitcast(FP8X4),
+                    rhs_scale=da_scales[e][:],
+                    start=True,
+                    stop=True,
+                )
+            slots = dx[:, k0:k1, e * C : (e + 1) * C]
+            if on_vector:
+                nc.vector.tensor_scalar(slots, acc[:], 2.0, None, MULT)
+            else:
+                nc.scalar.activation(out=slots, in_=acc[:], func=COPY, scale=2.0)
+
+        last = len(CHUNKS) - 1
+        for c in range(last + 1):
+            gather(c, 0)
+            if c:
+                first_layer(c - 1)
+            if c == 1:
+                for e in ON_GPSIMD:
+                    make_relu(e)
+            gather(c, 1, lambda: quantise(c, 0))
+        make_da(2)
+        shared = stage.tile([P, len(ON_GPSIMD), C, PACK], BF16, name="g", align_bytes=64)
+        for e in ON_GPSIMD:
+            for h in range(C // P):
+                part = slice(h * P, (h + 1) * P)
+                nc.gpsimd.tensor_tensor(shared[:, e, part, :], dh_copy[e][:, part, :], relu_a[e][:, part, :], MULT)
+            products[e] = shared[:, e, :, :].rearrange("p c t -> p (c t)")
+        first_layer(last)
+        for e in (2, 0, 3, 1, 4, 5):
+            if e > 2:
+                make_da(e)
+            quantise_da(e)
+            if e < E - 1:
+                product_dx(e, 0, 2)
+            else:
+                product_dx(e, 0, 1, on_vector=True)
+                product_dx(e, 1, 2)
+        for e in (2, 0, 3, 1, 4, 5):
+            product_dx(e, 2, 4)
+
+        for k in range(K // P):
+            x1 = stage.tile([P, T], F32, name="x1")
+            x2 = stage.tile([P, T], F32, name="x2")
+            total = stage.tile([P, T], F32, name="total")
+            nc.vector.tensor_copy(x1[:], dx[:, k, :].indirect(pos1_sb[:]))
+            for c0, c1 in ((0, T),) if k < K // P - 1 else ((0, T // 2), (T // 2, T)):
+                nc.vector.tensor_copy(x2[:, c0:c1], dx[:, k, :].indirect(pos2_sb[:, c0 // 16 : c1 // 16]))
+                adder = nc.vector if c0 else nc.gpsimd
+                adder.tensor_tensor(total[:, c0:c1], x1[:, c0:c1], x2[:, c0:c1], ADD)
+                nc.sync.dma_start(out=out[k * P : (k + 1) * P, c0:c1], in_=total[:, c0:c1])

@@ -55,7 +55,7 @@ def tile_moe_bdx_mlp_relu2_kernel(
         da_scales = [keep.tile([P, C], U8, name=f"da_scales_{e}", align_bytes=64) for e in range(E)]
         relu_a = [keep.tile([P, C, PACK], F32, name=f"relu_a_{e}") for e in ON_GPSIMD]
         dh_copy = [keep.tile([P, C, PACK], F32, name=f"dh_copy_{e}") for e in ON_GPSIMD]
-        dx = keep.tile([P, K // P, S], F32, name="dx")
+        dx = [keep.tile([P, S], F32, name=f"dx_{k}") for k in range(K // P)]
 
         nc.gpsimd.memset(w2_sc[:].rearrange("p g i -> p (g i)").bitcast(I32), 0)
         nc.gpsimd.memset(w1_sc[:].rearrange("p g i -> p (g i)").bitcast(I32), 0)
@@ -223,11 +223,12 @@ def tile_moe_bdx_mlp_relu2_kernel(
                     start=True,
                     stop=True,
                 )
-            slots = dx[:, k0:k1, e * C : (e + 1) * C]
-            if on_vector:
-                nc.vector.tensor_scalar(slots, acc[:], 2.0, None, MULT)
-            else:
-                nc.scalar.activation(out=slots, in_=acc[:], func=COPY, scale=2.0)
+            for k in range(k0, k1):
+                slots = dx[k][:, e * C : (e + 1) * C]
+                if on_vector:
+                    nc.vector.tensor_scalar(slots, acc[:, k - k0, :], 2.0, None, MULT)
+                else:
+                    nc.scalar.activation(out=slots, in_=acc[:, k - k0, :], func=COPY, scale=2.0)
 
         last = len(CHUNKS) - 1
         for c in range(last + 1):
@@ -260,11 +261,10 @@ def tile_moe_bdx_mlp_relu2_kernel(
 
         for k in range(K // P):
             x1 = stage.tile([P, T], F32, name="x1")
-            x2 = stage.tile([P, T], F32, name="x2")
             total = stage.tile([P, T], F32, name="total")
-            nc.vector.tensor_copy(x1[:], dx[:, k, :].indirect(pos1_sb[:]))
+            nc.vector.tensor_copy(x1[:], dx[k][:].indirect(pos1_sb[:]))
             for c0, c1 in ((0, T),) if k < K // P - 1 else ((0, T // 2), (T // 2, T)):
-                nc.vector.tensor_copy(x2[:, c0:c1], dx[:, k, :].indirect(pos2_sb[:, c0 // 16 : c1 // 16]))
-                adder = nc.vector if c0 else nc.gpsimd
-                adder.tensor_tensor(total[:, c0:c1], x1[:, c0:c1], x2[:, c0:c1], ADD)
+                nc.vector.tensor_tensor(
+                    total[:, c0:c1], dx[k][:].indirect(pos2_sb[:, c0 // 16 : c1 // 16]), x1[:, c0:c1], ADD
+                )
                 nc.sync.dma_start(out=out[k * P : (k + 1) * P, c0:c1], in_=total[:, c0:c1])

@@ -23,8 +23,20 @@ MAX = mybir.AluOpType.max
 RELU = mybir.ActivationFunctionType.Relu
 COPY = mybir.ActivationFunctionType.Copy
 
-CHUNKS = ((0, 384), (384, 384), (768, 384), (1152, 256), (1408, 128))
-ON_GPSIMD = (0, 1)
+GATES = ((0, 384), (384, 384), (768, 384), (1152, 384))
+GROUPS = ((0, 384, 0), (0, 384, 1), (384, 384, 0), (384, 384, 1), (768, 384, 0), (768, 384, 1), (1152, 384, 0), (1152, 256, 1), (1408, 128, 1))
+KB = 1024
+EDGE = 64
+G_AT = {1: 0, 2: 41 * KB, 4: EDGE, 8: 5 * KB + EDGE, 3: 10 * KB, 6: 10 * KB + EDGE, 5: 20 * KB, 7: 31 * KB}
+ROUNDED_AT = {0: 41 * KB, 2: 6 * KB, 6: 6 * KB + EDGE, 1: 10 * KB, 4: 16 * KB, 3: 20 * KB, 5: 30 * KB}
+SLOPE_AT = {0: 0, 1: 2 * KB, 2: 4 * KB, 3: 10 * KB, 4: 12 * KB, 5: 14 * KB, 6: 4 * KB + EDGE, 7: EDGE, 8: 2 * KB + EDGE, 9: 20 * KB, 10: 22 * KB, 11: 24 * KB}
+PACKED_AT = 34 * KB
+FIRST_DA_AT = 23 * KB + EDGE
+SECOND_GATE_AT = 26 * KB
+CODES_AT = {0: 13 * KB, 2: SECOND_GATE_AT + 4 * 384 - EDGE}
+DA_AT = {5: 33 * KB}
+BANK = 2 * KB
+BLOCKS = S // P
 
 
 def tile_moe_bdx_mlp_relu2_kernel(
@@ -35,9 +47,9 @@ def tile_moe_bdx_mlp_relu2_kernel(
         lists = ctx.enter_context(tc.tile_pool(name="lists", bufs=1))
         keep = ctx.enter_context(tc.tile_pool(name="keep", bufs=1))
         stage = ctx.enter_context(tc.tile_pool(name="stage", bufs=3))
-        ps_dh = ctx.enter_context(tc.psum_pool(name="ps_dh", bufs=3))
-        ps_turn = ctx.enter_context(tc.psum_pool(name="ps_turn", bufs=2))
-        ps_dx = ctx.enter_context(tc.psum_pool(name="ps_dx", bufs=3))
+        rooms = ctx.enter_context(tc.tile_pool(name="rooms", bufs=1))
+        pair = ctx.enter_context(tc.tile_pool(name="pair", bufs=2))
+        psum = ctx.enter_context(tc.psum_pool(name="psum", bufs=1))
 
         offs_sb = lists.tile([P, S // 16], U16, name="offs_sb")
         pos1_sb = lists.tile([P, T // 16], U16, name="pos1_sb")
@@ -49,12 +61,18 @@ def tile_moe_bdx_mlp_relu2_kernel(
         w2 = [keep.tile([P, 2, 2 * H], U8, name=f"w2_{e}", align_bytes=64) for e in range(E)]
         w1 = [keep.tile([P, 2 * K], U8, name=f"w1_{e}", align_bytes=64) for e in range(E)]
         dy = [keep.tile([P, T], F32, name=f"dy_{m}") for m in range(N // P)]
-        gates = [keep.tile([P, n], F32, name=f"gate_{c0}") for c0, n in CHUNKS]
-        saved = [keep.tile([P, PACK, 2 * C], F32, name=f"saved_{b}") for b in range(3)]
-        da_codes = [keep.tile([P, C], U32, name=f"da_codes_{e}", align_bytes=64) for e in range(E)]
-        da_scales = [keep.tile([P, C], U8, name=f"da_scales_{e}", align_bytes=64) for e in range(E)]
-        relu_a = [keep.tile([P, C, PACK], F32, name=f"relu_a_{e}") for e in ON_GPSIMD]
-        dh_copy = [keep.tile([P, C, PACK], F32, name=f"dh_copy_{e}") for e in ON_GPSIMD]
+        gates = [keep.tile([P, n], F32, name=f"gate_{c0}", align_bytes=64) for c0, n in GATES if c0 != 384]
+        gates[1:1] = [rooms.tile([P, 384], F32, name="second_gate", align_bytes=64, offset=SECOND_GATE_AT)]
+        saved = [keep.tile([P, PACK, n], F32, name=f"saved_{c0}") for c0, n in GATES]
+
+        slope = {}
+        da_packed = [
+            rooms.tile([P, 2 * C, 2], F32, name="da_packed_0", align_bytes=64, offset=PACKED_AT),
+            keep.tile([P, 2 * C, 2], F32, name="da_packed_1", align_bytes=64),
+            keep.tile([P, 2 * C, 2], F32, name="da_packed_2", align_bytes=64),
+        ]
+        da_codes = [keep.tile([P, 2 * C], U32, name=f"da_codes_{e}", align_bytes=64) for e in range(3)]
+        da_scales = [keep.tile([P, 2 * C], U8, name=f"da_scales_{e}", align_bytes=64) for e in range(3)]
         dx = [keep.tile([P, S], F32, name=f"dx_{k}") for k in range(K // P)]
 
         nc.gpsimd.memset(w2_sc[:].rearrange("p g i -> p (g i)").bitcast(I32), 0)
@@ -62,16 +80,17 @@ def tile_moe_bdx_mlp_relu2_kernel(
         make_identity(nc, ident[:])
 
         dy_rows = dyT.rearrange("(s p j) t -> s j p t", s=2, j=PACK)
-        a_rows = a.rearrange("(p t) c -> p t c", t=PACK)
+        a_rows = a.rearrange("(t p) c -> p t c", p=P)
         w2_rows = w2_scales.bitcast(I32).rearrange("e s f i -> f (e s) i")
         w1_rows = w1_scales.bitcast(I32).rearrange("e s f i -> f (e s) i")
 
         def load_gate(c):
-            c0, n = CHUNKS[c]
+            c0, n = GATES[c]
             nc.sync.dma_start(out=gates[c][:], in_=gate[0:P, c0 : c0 + n])
 
-        def load_saved(b):
-            nc.sync.dma_start(out=saved[b][:], in_=a_rows[:, :, 2 * C * b : 2 * C * (b + 1)])
+        def load_saved(c):
+            c0, n = GATES[c]
+            nc.sync.dma_start(out=saved[c][:], in_=a_rows[:, :, c0 : c0 + n])
 
         def load_w2(e):
             nc.sync.dma_start(out=w2[e][:].bitcast(I32), in_=w2_words[e].rearrange("s p b -> p s b").bitcast(I32))
@@ -84,51 +103,66 @@ def tile_moe_bdx_mlp_relu2_kernel(
         for m in range(N // P):
             nc.sync.dma_start(out=dy[m][:], in_=dy_rows[m // PACK, m % PACK])
         load_gate(1)
+        load_saved(0)
         for q in range(4):
             nc.sync.dma_start(out=w2_sc[32 * q : 32 * q + 4].bitcast(I32), in_=w2_rows[4 * q : 4 * q + 4])
         load_w2(0)
         load_w2(1)
-        load_saved(0)
-        load_gate(2)
-        load_w2(2)
-        load_w2(3)
-        load_gate(3)
-        load_gate(4)
-        load_w2(4)
-        load_w2(5)
         load_saved(1)
+        load_saved(2)
+        load_w2(2)
+        load_gate(2)
+        load_saved(3)
         for q in range(4):
             nc.sync.dma_start(out=w1_sc[32 * q : 32 * q + 4].bitcast(I32), in_=w1_rows[4 * q : 4 * q + 4])
-        load_saved(2)
-        for e in range(E):
+        load_w1(0)
+        load_w1(1)
+        load_w2(3)
+        load_w2(4)
+        load_gate(3)
+        load_w2(5)
+        for e in range(2, E):
             load_w1(e)
         nc.sync.dma_start(pos1_sb[:], pos1)
         nc.sync.dma_start(pos2_sb[:], pos2)
 
         rounded = {}
         g_codes = {}
-        turned = {}
-        products = {}
+        dh = {}
+        first_da = []
 
-        def gather(c, s, meanwhile=None):
-            c0, n = CHUNKS[c]
-            g = stage.tile([P, PACK, n], F32, name="g", align_bytes=64)
+        def gather(k):
+            c0, n, s = GROUPS[k]
+            if k < 1:
+                g = keep.tile([P, PACK, n], F32, name=f"g_{k}", align_bytes=64)
+            else:
+                g = rooms.tile([P, PACK, n], F32, name=f"g_{k}", align_bytes=64, offset=G_AT[k])
+            first = c0 % 384
             for j in range(PACK):
-                if j == PACK - 1 and meanwhile:
-                    meanwhile()
                 nc.vector.tensor_tensor(
-                    g[:, j, :], dy[PACK * s + j][:].indirect(offs_sb[:, c0 // 16 : (c0 + n) // 16]), gates[c][:], MULT
+                    g[:, j, :],
+                    dy[PACK * s + j][:].indirect(offs_sb[:, c0 // 16 : (c0 + n) // 16]),
+                    gates[c0 // 384][:, first : first + n],
+                    MULT,
                 )
-            rounded[c, s] = stage.tile([P, n, PACK], BF16, name="g_bf16", align_bytes=64)
+            if k + 2 < len(GROUPS):
+                rounded[k] = rooms.tile([P, n, PACK], BF16, name=f"g_bf16_{k}", align_bytes=64, offset=ROUNDED_AT[k])
+            else:
+                rounded[k] = keep.tile([P, n, PACK], BF16, name=f"g_bf16_{k}", align_bytes=64)
             nc.scalar.copy(
-                out=rounded[c, s][:].rearrange("p (c i) j -> p c j i", i=4), in_=g[:].rearrange("p j (c i) -> p c j i", i=4)
+                out=rounded[k][:].rearrange("p (c i) j -> p c j i", i=4), in_=g[:].rearrange("p j (c i) -> p c j i", i=4)
             )
 
-        def quantise(c, s):
-            c0, n = CHUNKS[c]
-            codes = stage.tile([P, n], U32, name=f"g_codes_{s}", align_bytes=64)
-            scales = stage.tile([P, n], U8, name=f"g_scales_{s}", align_bytes=64)
-            flat = rounded[c, s][:].rearrange("p c j -> p (c j)")
+        def quantise(k):
+            c0, n, s = GROUPS[k]
+            if k in CODES_AT:
+                codes = rooms.tile([P, n], U32, name=f"codes_{k}", align_bytes=64, offset=CODES_AT[k])
+            elif k == 4:
+                codes = keep.tile([P, n], U32, name=f"gate_{GATES[k // 2][0]}", align_bytes=64)
+            else:
+                codes = stage.tile([P, n], U32, name="g_codes", align_bytes=64)
+            scales = stage.tile([P, n], U8, name="g_scales", align_bytes=64)
+            flat = rounded[k][:].rearrange("p c j -> p (c j)")
             done = 0
             for width in (512, 256, 128):
                 if n - done >= width:
@@ -143,125 +177,134 @@ def tile_moe_bdx_mlp_relu2_kernel(
                 cols = slice(b * P, (b + 1) * P)
                 g_codes[c0 // P + b, s] = (codes[:, cols], scales[:, cols])
 
-        def product_dh(b):
-            e = b * P // C
-            acc = ps_dh.tile([P, H], F32, name="dh")
-            for s in range(2):
-                codes, scales = g_codes[b, s]
-                nc.tensor.matmul_mx(
-                    out=acc[:],
-                    lhsT=codes.bitcast(FP8X4),
-                    lhsT_scale=scales,
-                    rhs=w2[e][:, s, :].bitcast(FP4X4),
-                    rhs_scale=w2_sc[:, 2 * e + s, :],
-                    start=(s == 0),
-                    stop=(s == 1),
-                )
-            dh = stage.tile([P, PACK, P], F32, name="dh_sb")
-            nc.scalar.copy(out=dh[:], in_=acc[:].rearrange("p (m t) -> p t m", t=PACK))
-            return dh
-
-        def turn(b, dh):
-            turned[b] = ps_turn.tile([P, PACK, P], F32, name="turned")
+        def make_slope(b):
+            slope[b] = rooms.tile([P, H], F32, name=f"slope_{b}", align_bytes=64, offset=SLOPE_AT[b])[:]
+            turned = psum.tile([P, PACK, P], F32, name=f"a_turned_{b}", offset=(3 + b % 3) * BANK)
+            col = b % 3 * P
             for t in range(PACK):
-                nc.tensor.transpose(turned[b][:, t, :], dh[:, t, :], ident[:])
-
-        def first_layer(c):
-            quantise(c, 1)
-            c0, n = CHUNKS[c]
-            blocks = range(c0 // P, (c0 + n) // P)
-            dh = product_dh(blocks[0])
-            for b in blocks[1:]:
-                following = product_dh(b)
-                turn(b - 1, dh)
-                dh = following
-            turn(blocks[-1], dh)
-            for b in blocks:
-                e, h = divmod(b, C // P)
-                if e in ON_GPSIMD:
-                    nc.scalar.copy(
-                        out=dh_copy[e][:, h * P : (h + 1) * P, :], in_=turned[b][:].rearrange("p t c -> p c t")
-                    )
-
-        def slots_of(b):
-            cols = slice(b * P % (2 * C), b * P % (2 * C) + P)
-            return saved[b * P // (2 * C)][:, :, cols].rearrange("p t c -> p c t")
-
-        def make_relu(e):
+                nc.tensor.transpose(turned[:, t, :], saved[b // 3][:, t, col : col + P], ident[:])
             nc.scalar.activation(
-                out=relu_a[e][:].rearrange("p (c i) t -> p c t i", i=4),
-                in_=saved[0][:, :, e * C : (e + 1) * C].rearrange("p t (c i) -> p c t i", i=4),
+                out=slope[b].rearrange("s (u p e) -> s u p e", u=2, e=2),
+                in_=turned[:].rearrange("s t q -> s (t q)").rearrange("s (p u e) -> s u p e", u=2, e=2),
                 func=RELU,
+                scale=2.0,
             )
 
-        def make_da(e):
-            da = stage.tile([P, C, PACK], BF16, name="g" if e == len(ON_GPSIMD) else "da", align_bytes=64)
-            for h in range(C // P):
-                b = e * C // P + h
-                nc.vector.scalar_tensor_tensor(
-                    out=da[:, h * P : (h + 1) * P, :],
-                    in0=slots_of(b),
-                    scalar=0.0,
-                    in1=turned[b][:].rearrange("p t c -> p c t"),
-                    op0=MAX,
-                    op1=MULT,
-                )
-            products[e] = da[:].rearrange("p c t -> p (c t)")
+        def product_dh(b, s):
+            e = b * P // C
+            if s == 0:
+                dh[b] = psum.tile([P, H], F32, name=f"dh_{b}", offset=(b % 3 if b < 9 else b - 6) * BANK)
+            codes, scales = g_codes[b, s]
+            nc.tensor.matmul_mx(
+                out=dh[b][:],
+                lhsT=codes.bitcast(FP8X4),
+                lhsT_scale=scales,
+                rhs=w2[e][:, s, :].bitcast(FP4X4),
+                rhs_scale=w2_sc[:, 2 * e + s, :],
+                start=(s == 0),
+                stop=(s == 1),
+            )
 
-        def quantise_da(e):
-            nc.vector.quantize_mx(out=da_codes[e][:].bitcast(FP8X4), scales=da_scales[e][:], in_=products[e])
+        def make_da(b):
+            e, h = divmod(b, 4)
+            if b == 0:
+                first_da.append(rooms.tile([P, 3 * H], BF16, name="first_da", align_bytes=64, offset=FIRST_DA_AT))
+            if b < 3:
+                da = first_da[0][:, b * H : (b + 1) * H]
+            elif b in DA_AT:
+                da = rooms.tile([P, H], BF16, name=f"da_{b}", align_bytes=64, offset=DA_AT[b])[:]
+            else:
+                da = stage.tile([P, H], BF16, name="da", align_bytes=64)[:]
+            nc.vector.tensor_tensor(
+                da.rearrange("s (u p e) -> s u p e", u=2, e=2),
+                dh[b][:].rearrange("s (p u e) -> s u p e", u=2, e=2),
+                slope[b].rearrange("s (u p e) -> s u p e", u=2, e=2),
+                MULT,
+            )
+            pairs = da.bitcast(F32)
+            turned = psum.tile([P, 2, P], F32, name=f"da_turned_{b}", offset=(6 + b % 2) * BANK)
+            for u in range(2):
+                nc.tensor.transpose(turned[:, u, :], pairs[:, u * P : (u + 1) * P], ident[:])
+            nc.scalar.copy(out=da_packed[e][:, h * P : (h + 1) * P, :], in_=turned[:].rearrange("p u s -> p s u"))
 
-        def product_dx(e, k0, k1, on_vector=False):
-            acc = ps_dx.tile([P, k1 - k0, C], F32, name="dx_acc")
-            for k in range(k0, k1):
+        def quantise_da(c0, c1):
+            m, c0, c1 = c0 // (2 * C), c0 % (2 * C), (c1 - 1) % (2 * C) + 1
+            flat = da_packed[m][:].rearrange("p c u -> p (c u)").bitcast(BF16)
+            nc.vector.quantize_mx(
+                out=da_codes[m][:, c0:c1].bitcast(FP8X4), scales=da_scales[m][:, c0:c1], in_=flat[:, PACK * c0 : PACK * c1]
+            )
+
+        def product_dx(experts, k, bank):
+            acc = psum.tile([P, len(experts), C], F32, name=f"dx_{experts[0]}_{k}", offset=bank * BANK)
+            for h, e in enumerate(experts):
+                cols = slice(e % 2 * C, (e % 2 + 1) * C)
                 nc.tensor.matmul_mx(
-                    out=acc[:, k - k0, :],
+                    out=acc[:, h, :],
                     lhsT=w1[e][:, 2 * k * P : 2 * (k + 1) * P].bitcast(FP4X4),
                     lhsT_scale=w1_sc[:, e, k * P : (k + 1) * P],
-                    rhs=da_codes[e][:].bitcast(FP8X4),
-                    rhs_scale=da_scales[e][:],
+                    rhs=da_codes[e // 2][:, cols].bitcast(FP8X4),
+                    rhs_scale=da_scales[e // 2][:, cols],
                     start=True,
                     stop=True,
                 )
-            for k in range(k0, k1):
-                slots = dx[k][:, e * C : (e + 1) * C]
-                if on_vector:
-                    nc.vector.tensor_scalar(slots, acc[:, k - k0, :], 2.0, None, MULT)
-                else:
-                    nc.scalar.activation(out=slots, in_=acc[:, k - k0, :], func=COPY, scale=2.0)
+            nc.scalar.copy(
+                out=dx[k][:, experts[0] * C : (experts[-1] + 1) * C], in_=acc[:].rearrange("p h c -> p (h c)")
+            )
 
-        last = len(CHUNKS) - 1
-        for c in range(last + 1):
-            gather(c, 0)
-            if c:
-                first_layer(c - 1)
-            if c == 1:
-                for e in ON_GPSIMD:
-                    make_relu(e)
-            gather(c, 1, lambda: quantise(c, 0))
-        make_da(2)
-        shared = stage.tile([P, len(ON_GPSIMD), C, PACK], BF16, name="g", align_bytes=64)
-        for e in ON_GPSIMD:
-            for h in range(C // P):
-                part = slice(h * P, (h + 1) * P)
-                nc.gpsimd.tensor_tensor(shared[:, e, part, :], dh_copy[e][:, part, :], relu_a[e][:, part, :], MULT)
-            products[e] = shared[:, e, :, :].rearrange("p c t -> p (c t)")
-        first_layer(last)
-        for e in (2, 0, 3, 1, 4, 5):
-            if e > 2:
-                make_da(e)
-            quantise_da(e)
-            if e < E - 1:
-                product_dx(e, 0, 2)
-            else:
-                product_dx(e, 0, 1, on_vector=True)
-                product_dx(e, 1, 2)
-        for e in (2, 0, 3, 1, 4, 5):
-            product_dx(e, 2, 4)
+        def first_layer(k, after=()):
+            quantise(k)
+            c0, n, s = GROUPS[k]
+            for b in after:
+                make_da(b)
+            for b in range(c0 // P, (c0 + n) // P):
+                product_dh(b, s)
+
+        gather(0)
+        gather(1)
+        first_layer(0)
+        gather(2)
+        first_layer(1)
+        for b in range(0, 3):
+            make_slope(b)
+        gather(3)
+        first_layer(2, (0, 1, 2))
+        for b in range(3, 6):
+            make_slope(b)
+        gather(4)
+        first_layer(3)
+        for b in range(6, 9):
+            make_slope(b)
+        gather(5)
+        first_layer(4, (3, 4, 5))
+        for b in range(9, 12):
+            make_slope(b)
+        gather(6)
+        first_layer(5)
+        quantise_da(0, 2 * C)
+        for k in range(2):
+            product_dx((0, 1), k, 6 + k)
+        gather(7)
+        first_layer(6, (6,))
+        gather(8)
+        first_layer(7)
+        first_layer(8)
+        for b in range(7, 12):
+            make_da(b)
+        quantise_da(2 * C, 4 * C)
+        product_dx((2, 3), 0, 0)
+        quantise_da(4 * C, 5 * C)
+        product_dx((4,), 0, 1)
+        quantise_da(5 * C, 6 * C)
+        product_dx((5,), 0, 2)
+        product_dx((2, 3), 1, 3)
+        product_dx((4, 5), 1, 4)
+        for k in range(2, 4):
+            for m, experts in enumerate(((0, 1), (2, 3), (4, 5))):
+                product_dx(experts, k, (5 + 3 * (k - 2) + m) % 8)
 
         for k in range(K // P):
-            x1 = stage.tile([P, T], F32, name="x1")
-            total = stage.tile([P, T], F32, name="total")
+            x1 = pair.tile([P, T], F32, name="x1")
+            total = pair.tile([P, T], F32, name="total")
             nc.vector.tensor_copy(x1[:], dx[k][:].indirect(pos1_sb[:]))
             for c0, c1 in ((0, T),) if k < K // P - 1 else ((0, T // 2), (T // 2, T)):
                 nc.vector.tensor_tensor(

@@ -23,18 +23,19 @@ MAX = mybir.AluOpType.max
 RELU = mybir.ActivationFunctionType.Relu
 COPY = mybir.ActivationFunctionType.Copy
 
-GATES = ((0, 384), (384, 384), (768, 384), (1152, 384))
-GROUPS = ((0, 384, 0), (0, 384, 1), (384, 384, 0), (384, 384, 1), (768, 384, 0), (768, 384, 1), (1152, 384, 0), (1152, 256, 1), (1408, 128, 1))
+GATES = ((0, 512), (512, 512), (1024, 512))
+GROUPS = ((0, 512, 0), (0, 512, 1), (512, 512, 0), (512, 512, 1), (1024, 512, 0), (1024, 384, 1), (1408, 128, 1))
+ON_GPSIMD = (0, 1)
 KB = 1024
-EDGE = 64
-G_AT = {1: 0, 2: 41 * KB, 4: EDGE, 8: 5 * KB + EDGE, 3: 10 * KB, 6: 10 * KB + EDGE, 5: 20 * KB, 7: 31 * KB}
-ROUNDED_AT = {0: 41 * KB, 2: 6 * KB, 6: 6 * KB + EDGE, 1: 10 * KB, 4: 16 * KB, 3: 20 * KB, 5: 30 * KB}
-SLOPE_AT = {0: 0, 1: 2 * KB, 2: 4 * KB, 3: 10 * KB, 4: 12 * KB, 5: 14 * KB, 6: 4 * KB + EDGE, 7: EDGE, 8: 2 * KB + EDGE, 9: 20 * KB, 10: 22 * KB, 11: 24 * KB}
-PACKED_AT = 34 * KB
-FIRST_DA_AT = 23 * KB + EDGE
-SECOND_GATE_AT = 26 * KB
-CODES_AT = {0: 13 * KB, 2: SECOND_GATE_AT + 4 * 384 - EDGE}
-DA_AT = {5: 33 * KB}
+G_AT = {0: 0, 5: 7 * KB, 6: 17 * KB, 2: 21 * KB, 3: 30 * KB, 4: 38 * KB, 1: 52 * KB}
+ROUNDED_AT = {3: 8 * KB, 4: 14 * KB, 0: 24 * KB, 1: 30 * KB, 2: 38 * KB, 6: 46 * KB}
+SLOPE_AT = {0: 0, 1: 2, 2: 4, 3: 6, 4: 18, 7: 52, 8: 54, 9: 56, 10: 58, 11: 60}
+DH_COPY_AT = 24 * KB
+SHARED_DA_AT = 46 * KB
+DY3_AT = 49 * KB
+DY2_AT = 62 * KB
+DH_BANK = (0, 1, 2, 3, 0, 1, 2, 3, 4, 5, 0, 1)
+TURN_BANK = {2: 6, 3: 7, 4: 6, 5: 7, 6: 6, 7: 7, 8: 6, 0: 7, 9: 3, 10: 6, 1: 7, 11: 4}
 BANK = 2 * KB
 BLOCKS = S // P
 
@@ -60,19 +61,19 @@ def tile_moe_bdx_mlp_relu2_kernel(
         w1_sc = keep.tile([P, E, K], U8, name="w1_sc", align_bytes=64)
         w2 = [keep.tile([P, 2, 2 * H], U8, name=f"w2_{e}", align_bytes=64) for e in range(E)]
         w1 = [keep.tile([P, 2 * K], U8, name=f"w1_{e}", align_bytes=64) for e in range(E)]
-        dy = [keep.tile([P, T], F32, name=f"dy_{m}") for m in range(N // P)]
-        gates = [keep.tile([P, n], F32, name=f"gate_{c0}", align_bytes=64) for c0, n in GATES if c0 != 384]
-        gates[1:1] = [rooms.tile([P, 384], F32, name="second_gate", align_bytes=64, offset=SECOND_GATE_AT)]
+        dy = [keep.tile([P, T], F32, name=f"dy_{m}") for m in range(N // P) if m not in (2, 3)]
+        dy[2:2] = [
+            rooms.tile([P, T], F32, name="dy_2", offset=DY2_AT),
+            rooms.tile([P, T], F32, name="dy_3", offset=DY3_AT),
+        ]
+        gates = [keep.tile([P, n], F32, name=f"gate_{c0}") for c0, n in GATES]
         saved = [keep.tile([P, PACK, n], F32, name=f"saved_{c0}") for c0, n in GATES]
 
         slope = {}
-        da_packed = [
-            rooms.tile([P, 2 * C, 2], F32, name="da_packed_0", align_bytes=64, offset=PACKED_AT),
-            keep.tile([P, 2 * C, 2], F32, name="da_packed_1", align_bytes=64),
-            keep.tile([P, 2 * C, 2], F32, name="da_packed_2", align_bytes=64),
-        ]
-        da_codes = [keep.tile([P, 2 * C], U32, name=f"da_codes_{e}", align_bytes=64) for e in range(3)]
-        da_scales = [keep.tile([P, 2 * C], U8, name=f"da_scales_{e}", align_bytes=64) for e in range(3)]
+        da_packed = [keep.tile([P, C, 2], F32, name=f"da_packed_{e}", align_bytes=64) for e in range(E)]
+        da_codes = {e: keep.tile([P, C], U32, name=f"da_codes_{e}", align_bytes=64) for e in range(E) if e != 3}
+        dh_copy = {}
+        da_scales = [keep.tile([P, C], U8, name=f"da_scales_{e}", align_bytes=64) for e in range(E)]
         dx = [keep.tile([P, S], F32, name=f"dx_{k}") for k in range(K // P)]
 
         nc.gpsimd.memset(w2_sc[:].rearrange("p g i -> p (g i)").bitcast(I32), 0)
@@ -109,19 +110,15 @@ def tile_moe_bdx_mlp_relu2_kernel(
         load_w2(0)
         load_w2(1)
         load_saved(1)
-        load_saved(2)
         load_w2(2)
+        load_w2(3)
         load_gate(2)
-        load_saved(3)
+        load_saved(2)
+        load_w2(4)
+        load_w2(5)
         for q in range(4):
             nc.sync.dma_start(out=w1_sc[32 * q : 32 * q + 4].bitcast(I32), in_=w1_rows[4 * q : 4 * q + 4])
-        load_w1(0)
-        load_w1(1)
-        load_w2(3)
-        load_w2(4)
-        load_gate(3)
-        load_w2(5)
-        for e in range(2, E):
+        for e in range(E):
             load_w1(e)
         nc.sync.dma_start(pos1_sb[:], pos1)
         nc.sync.dma_start(pos2_sb[:], pos2)
@@ -129,23 +126,21 @@ def tile_moe_bdx_mlp_relu2_kernel(
         rounded = {}
         g_codes = {}
         dh = {}
-        first_da = []
+        shared_da = []
+        early_da = []
 
         def gather(k):
             c0, n, s = GROUPS[k]
-            if k < 1:
-                g = keep.tile([P, PACK, n], F32, name=f"g_{k}", align_bytes=64)
-            else:
-                g = rooms.tile([P, PACK, n], F32, name=f"g_{k}", align_bytes=64, offset=G_AT[k])
-            first = c0 % 384
+            g = rooms.tile([P, PACK, n], F32, name=f"g_{k}", align_bytes=64, offset=G_AT[k])
+            first = c0 % 512
             for j in range(PACK):
                 nc.vector.tensor_tensor(
                     g[:, j, :],
                     dy[PACK * s + j][:].indirect(offs_sb[:, c0 // 16 : (c0 + n) // 16]),
-                    gates[c0 // 384][:, first : first + n],
+                    gates[c0 // 512][:, first : first + n],
                     MULT,
                 )
-            if k + 2 < len(GROUPS):
+            if k in ROUNDED_AT:
                 rounded[k] = rooms.tile([P, n, PACK], BF16, name=f"g_bf16_{k}", align_bytes=64, offset=ROUNDED_AT[k])
             else:
                 rounded[k] = keep.tile([P, n, PACK], BF16, name=f"g_bf16_{k}", align_bytes=64)
@@ -155,10 +150,8 @@ def tile_moe_bdx_mlp_relu2_kernel(
 
         def quantise(k):
             c0, n, s = GROUPS[k]
-            if k in CODES_AT:
-                codes = rooms.tile([P, n], U32, name=f"codes_{k}", align_bytes=64, offset=CODES_AT[k])
-            elif k == 4:
-                codes = keep.tile([P, n], U32, name=f"gate_{GATES[k // 2][0]}", align_bytes=64)
+            if k == 3:
+                codes = rooms.tile([P, n], U32, name="g_codes_3", align_bytes=64, offset=DY2_AT)
             else:
                 codes = stage.tile([P, n], U32, name="g_codes", align_bytes=64)
             scales = stage.tile([P, n], U8, name="g_scales", align_bytes=64)
@@ -178,11 +171,15 @@ def tile_moe_bdx_mlp_relu2_kernel(
                 g_codes[c0 // P + b, s] = (codes[:, cols], scales[:, cols])
 
         def make_slope(b):
-            slope[b] = rooms.tile([P, H], F32, name=f"slope_{b}", align_bytes=64, offset=SLOPE_AT[b])[:]
-            turned = psum.tile([P, PACK, P], F32, name=f"a_turned_{b}", offset=(3 + b % 3) * BANK)
-            col = b % 3 * P
+            if b == 4:
+                slopes = rooms.tile([P, 3, H], F32, name="slope_4", align_bytes=64, offset=SLOPE_AT[b] * KB)
+                slope.update({4 + h: slopes[:, h, :] for h in range(3)})
+            elif b in SLOPE_AT:
+                slope[b] = rooms.tile([P, H], F32, name=f"slope_{b}", align_bytes=64, offset=SLOPE_AT[b] * KB)[:]
+            turned = psum.tile([P, PACK, P], F32, name=f"a_turned_{b}", offset=(4 + b % 4) * BANK)
+            col = b % 4 * P
             for t in range(PACK):
-                nc.tensor.transpose(turned[:, t, :], saved[b // 3][:, t, col : col + P], ident[:])
+                nc.tensor.transpose(turned[:, t, :], saved[b // 4][:, t, col : col + P], ident[:])
             nc.scalar.activation(
                 out=slope[b].rearrange("s (u p e) -> s u p e", u=2, e=2),
                 in_=turned[:].rearrange("s t q -> s (t q)").rearrange("s (p u e) -> s u p e", u=2, e=2),
@@ -193,7 +190,7 @@ def tile_moe_bdx_mlp_relu2_kernel(
         def product_dh(b, s):
             e = b * P // C
             if s == 0:
-                dh[b] = psum.tile([P, H], F32, name=f"dh_{b}", offset=(b % 3 if b < 9 else b - 6) * BANK)
+                dh[b] = psum.tile([P, H], F32, name=f"dh_{b}", offset=DH_BANK[b] * BANK)
             codes, scales = g_codes[b, s]
             nc.tensor.matmul_mx(
                 out=dh[b][:],
@@ -204,52 +201,66 @@ def tile_moe_bdx_mlp_relu2_kernel(
                 start=(s == 0),
                 stop=(s == 1),
             )
+            if s == 1 and b in ON_GPSIMD:
+                if not dh_copy:
+                    copies = rooms.tile([P, len(ON_GPSIMD), H], F32, name="dh_copy", align_bytes=64, offset=DH_COPY_AT)
+                    dh_copy.update({h: copies[:, h, :] for h in ON_GPSIMD})
+                nc.scalar.copy(
+                    out=dh_copy[b].rearrange("s (u p e) -> s u p e", u=2, e=2),
+                    in_=dh[b][:].rearrange("s (p u e) -> s u p e", u=2, e=2),
+                )
 
         def make_da(b):
-            e, h = divmod(b, 4)
-            if b == 0:
-                first_da.append(rooms.tile([P, 3 * H], BF16, name="first_da", align_bytes=64, offset=FIRST_DA_AT))
-            if b < 3:
-                da = first_da[0][:, b * H : (b + 1) * H]
-            elif b in DA_AT:
-                da = rooms.tile([P, H], BF16, name=f"da_{b}", align_bytes=64, offset=DA_AT[b])[:]
+            e, h = divmod(b, C // P)
+            if b in ON_GPSIMD:
+                if not shared_da:
+                    shared_da.append(
+                        rooms.tile([P, len(ON_GPSIMD) * H], BF16, name="shared_da", align_bytes=64, offset=SHARED_DA_AT)
+                    )
+                da = shared_da[0][:, b * H : (b + 1) * H]
+                nc.gpsimd.tensor_tensor(da, dh_copy[b], slope[b], MULT)
             else:
-                da = stage.tile([P, H], BF16, name="da", align_bytes=64)[:]
-            nc.vector.tensor_tensor(
-                da.rearrange("s (u p e) -> s u p e", u=2, e=2),
-                dh[b][:].rearrange("s (p u e) -> s u p e", u=2, e=2),
-                slope[b].rearrange("s (u p e) -> s u p e", u=2, e=2),
-                MULT,
-            )
+                if b == 2:
+                    early_da.append(rooms.tile([P, 2 * H], BF16, name="early_da", align_bytes=64, offset=DY3_AT))
+                if b < 4:
+                    da = early_da[0][:, (b - 2) * H : (b - 1) * H]
+                else:
+                    da = stage.tile([P, H], BF16, name="da", align_bytes=64)[:]
+                nc.vector.tensor_tensor(
+                    da.rearrange("s (u p e) -> s u p e", u=2, e=2),
+                    dh[b][:].rearrange("s (p u e) -> s u p e", u=2, e=2),
+                    slope[b].rearrange("s (u p e) -> s u p e", u=2, e=2),
+                    MULT,
+                )
             pairs = da.bitcast(F32)
-            turned = psum.tile([P, 2, P], F32, name=f"da_turned_{b}", offset=(6 + b % 2) * BANK)
+            turned = psum.tile([P, 2, P], F32, name=f"da_turned_{b}", offset=TURN_BANK[b] * BANK)
             for u in range(2):
                 nc.tensor.transpose(turned[:, u, :], pairs[:, u * P : (u + 1) * P], ident[:])
             nc.scalar.copy(out=da_packed[e][:, h * P : (h + 1) * P, :], in_=turned[:].rearrange("p u s -> p s u"))
 
-        def quantise_da(c0, c1):
-            m, c0, c1 = c0 // (2 * C), c0 % (2 * C), (c1 - 1) % (2 * C) + 1
-            flat = da_packed[m][:].rearrange("p c u -> p (c u)").bitcast(BF16)
-            nc.vector.quantize_mx(
-                out=da_codes[m][:, c0:c1].bitcast(FP8X4), scales=da_scales[m][:, c0:c1], in_=flat[:, PACK * c0 : PACK * c1]
-            )
+        def quantise_da(e):
+            if e == 3:
+                da_codes[e] = rooms.tile([P, C], U32, name="da_codes_3", align_bytes=64, offset=SLOPE_AT[10] * KB)
+            flat = da_packed[e][:].rearrange("p c u -> p (c u)").bitcast(BF16)
+            nc.vector.quantize_mx(out=da_codes[e][:].bitcast(FP8X4), scales=da_scales[e][:], in_=flat)
 
-        def product_dx(experts, k, bank):
+        def product_dx(experts, k, bank, on_vector=False):
             acc = psum.tile([P, len(experts), C], F32, name=f"dx_{experts[0]}_{k}", offset=bank * BANK)
             for h, e in enumerate(experts):
-                cols = slice(e % 2 * C, (e % 2 + 1) * C)
                 nc.tensor.matmul_mx(
                     out=acc[:, h, :],
                     lhsT=w1[e][:, 2 * k * P : 2 * (k + 1) * P].bitcast(FP4X4),
                     lhsT_scale=w1_sc[:, e, k * P : (k + 1) * P],
-                    rhs=da_codes[e // 2][:, cols].bitcast(FP8X4),
-                    rhs_scale=da_scales[e // 2][:, cols],
+                    rhs=da_codes[e][:].bitcast(FP8X4),
+                    rhs_scale=da_scales[e][:],
                     start=True,
                     stop=True,
                 )
-            nc.scalar.copy(
-                out=dx[k][:, experts[0] * C : (experts[-1] + 1) * C], in_=acc[:].rearrange("p h c -> p (h c)")
-            )
+            slots = dx[k][:, experts[0] * C : (experts[-1] + 1) * C]
+            if on_vector:
+                nc.vector.tensor_copy(slots, acc[:].rearrange("p h c -> p (h c)"))
+            else:
+                nc.scalar.copy(out=slots, in_=acc[:].rearrange("p h c -> p (h c)"))
 
         def first_layer(k, after=()):
             quantise(k)
@@ -262,52 +273,63 @@ def tile_moe_bdx_mlp_relu2_kernel(
         gather(0)
         gather(1)
         first_layer(0)
+        for b in range(0, 4):
+            make_slope(b)
         gather(2)
         first_layer(1)
-        for b in range(0, 3):
-            make_slope(b)
         gather(3)
-        first_layer(2, (0, 1, 2))
-        for b in range(3, 6):
+        quantise(2)
+        for b in range(4, 6):
+            product_dh(b, 0)
+        for b in range(4, 12):
             make_slope(b)
         gather(4)
-        first_layer(3)
-        for b in range(6, 9):
-            make_slope(b)
+        quantise(3)
+        make_da(2)
+        make_da(3)
+        product_dh(6, 0)
+        product_dh(7, 0)
+        for b in range(4, 8):
+            product_dh(b, 1)
         gather(5)
-        first_layer(4, (3, 4, 5))
-        for b in range(9, 12):
-            make_slope(b)
+        first_layer(4, (4, 5, 6))
+        quantise_da(1)
         gather(6)
         first_layer(5)
-        quantise_da(0, 2 * C)
-        for k in range(2):
-            product_dx((0, 1), k, 6 + k)
-        gather(7)
-        first_layer(6, (6,))
-        gather(8)
-        first_layer(7)
-        first_layer(8)
-        for b in range(7, 12):
+        first_layer(6)
+        quantise_da(2)
+        for b in (7, 8, 0, 9, 10, 1, 11):
             make_da(b)
-        quantise_da(2 * C, 4 * C)
-        product_dx((2, 3), 0, 0)
-        quantise_da(4 * C, 5 * C)
-        product_dx((4,), 0, 1)
-        quantise_da(5 * C, 6 * C)
-        product_dx((5,), 0, 2)
-        product_dx((2, 3), 1, 3)
-        product_dx((4, 5), 1, 4)
-        for k in range(2, 4):
-            for m, experts in enumerate(((0, 1), (2, 3), (4, 5))):
-                product_dx(experts, k, (5 + 3 * (k - 2) + m) % 8)
+        product_dx((1, 2), 0, 2)
+        quantise_da(3)
+        product_dx((3,), 0, 5)
+        quantise_da(0)
+        product_dx((0,), 0, 0)
+        quantise_da(4)
+        product_dx((4,), 0, 3)
+        quantise_da(5)
+        product_dx((5,), 0, 1, on_vector=True)
+        for k in range(1, 4):
+            for m, experts in enumerate(((1, 2), (3, 4), (0,), (5,))):
+                product_dx(experts, k, (2, 6, 7, 4, 5, 0, 3, 1)[(4 * (k - 1) + m) % 8])
 
-        for k in range(K // P):
-            x1 = pair.tile([P, T], F32, name="x1")
-            total = pair.tile([P, T], F32, name="total")
-            nc.vector.tensor_copy(x1[:], dx[k][:].indirect(pos1_sb[:]))
-            for c0, c1 in ((0, T),) if k < K // P - 1 else ((0, T // 2), (T // 2, T)):
-                nc.vector.tensor_tensor(
-                    total[:, c0:c1], dx[k][:].indirect(pos2_sb[:, c0 // 16 : c1 // 16]), x1[:, c0:c1], ADD
-                )
-                nc.sync.dma_start(out=out[k * P : (k + 1) * P, c0:c1], in_=total[:, c0:c1])
+        first = {}
+
+        def fetch_first(k):
+            first[k] = pair.tile([P, T], F32, name="x1")
+            nc.vector.tensor_copy(first[k][:], dx[k][:].indirect(pos1_sb[:]))
+
+        def add_second(k, c0, c1):
+            total = stage.tile([P, c1 - c0], F32, name="total")
+            nc.vector.tensor_tensor(total[:], dx[k][:].indirect(pos2_sb[:, c0 // 16 : c1 // 16]), first[k][:, c0:c1], ADD)
+            nc.sync.dma_start(out=out[k * P : (k + 1) * P, c0:c1], in_=total[:])
+
+        fetch_first(0)
+        add_second(0, 0, T)
+        fetch_first(1)
+        fetch_first(2)
+        add_second(1, 0, T)
+        fetch_first(3)
+        add_second(2, 0, T)
+        add_second(3, 0, 512)
+        add_second(3, 512, T)

@@ -25,17 +25,18 @@ COPY = mybir.ActivationFunctionType.Copy
 
 GATES = ((0, 512), (512, 512), (1024, 512))
 GROUPS = ((0, 512, 0), (0, 512, 1), (512, 512, 0), (512, 512, 1), (1024, 512, 0), (1024, 384, 1), (1408, 128, 1))
-ON_GPSIMD = (0, 1)
+ON_GPSIMD = (0, 1, 2, 3)
 KB = 1024
-G_AT = {0: 0, 5: 7 * KB, 6: 17 * KB, 2: 21 * KB, 3: 30 * KB, 4: 38 * KB, 1: 52 * KB}
-ROUNDED_AT = {3: 8 * KB, 4: 14 * KB, 0: 24 * KB, 1: 30 * KB, 2: 38 * KB, 6: 46 * KB}
-SLOPE_AT = {0: 0, 1: 2, 2: 4, 3: 6, 4: 18, 7: 52, 8: 54, 9: 56, 10: 58, 11: 60}
-DH_COPY_AT = 24 * KB
-SHARED_DA_AT = 46 * KB
-DY3_AT = 49 * KB
-DY2_AT = 62 * KB
+EDGE = 64
+G_AT = {0: 8 * KB, 2: 8 * KB, 4: 16 * KB - EDGE, 6: 2 * KB, 1: 24 * KB, 3: 24 * KB, 5: 24 * KB}
+ROUNDED_AT = {4: 32 * KB, 6: 36 * KB}
+MIDDLE_SLOPES_AT = EDGE
+MIDDLE_DA_AT = 18 * KB
+SHARED_DA_AT = {0: ROUNDED_AT[6], 1: ROUNDED_AT[4]}
+DY2_AT = 38 * KB
+DH_COPY_AT = 41 * KB
 DH_BANK = (0, 1, 2, 3, 0, 1, 2, 3, 4, 5, 0, 1)
-TURN_BANK = {2: 6, 3: 7, 4: 6, 5: 7, 6: 6, 7: 7, 8: 6, 0: 7, 9: 3, 10: 6, 1: 7, 11: 4}
+TURN_BANK = {4: 6, 5: 7, 6: 6, 7: 7, 2: 2, 3: 3, 8: 6, 9: 7, 0: 3, 10: 4, 11: 5, 1: 6}
 BANK = 2 * KB
 BLOCKS = S // P
 
@@ -61,17 +62,14 @@ def tile_moe_bdx_mlp_relu2_kernel(
         w1_sc = keep.tile([P, E, K], U8, name="w1_sc", align_bytes=64)
         w2 = [keep.tile([P, 2, 2 * H], U8, name=f"w2_{e}", align_bytes=64) for e in range(E)]
         w1 = [keep.tile([P, 2 * K], U8, name=f"w1_{e}", align_bytes=64) for e in range(E)]
-        dy = [keep.tile([P, T], F32, name=f"dy_{m}") for m in range(N // P) if m not in (2, 3)]
-        dy[2:2] = [
-            rooms.tile([P, T], F32, name="dy_2", offset=DY2_AT),
-            rooms.tile([P, T], F32, name="dy_3", offset=DY3_AT),
-        ]
+        dy = [keep.tile([P, T], F32, name=f"dy_{m}") for m in range(N // P) if m != 2]
+        dy[2:2] = [rooms.tile([P, T], F32, name="dy_2", offset=DY2_AT)]
         gates = [keep.tile([P, n], F32, name=f"gate_{c0}") for c0, n in GATES]
         saved = [keep.tile([P, PACK, n], F32, name=f"saved_{c0}") for c0, n in GATES]
 
         slope = {}
         da_packed = [keep.tile([P, C, 2], F32, name=f"da_packed_{e}", align_bytes=64) for e in range(E)]
-        da_codes = {e: keep.tile([P, C], U32, name=f"da_codes_{e}", align_bytes=64) for e in range(E) if e != 3}
+        da_codes = {e: keep.tile([P, C], U32, name=f"da_codes_{e}", align_bytes=64) for e in (0, 2, 3, 5)}
         dh_copy = {}
         da_scales = [keep.tile([P, C], U8, name=f"da_scales_{e}", align_bytes=64) for e in range(E)]
         dx = [keep.tile([P, S], F32, name=f"dx_{k}") for k in range(K // P)]
@@ -126,8 +124,8 @@ def tile_moe_bdx_mlp_relu2_kernel(
         rounded = {}
         g_codes = {}
         dh = {}
-        shared_da = []
-        early_da = []
+        shared_da = {}
+        made = {}
 
         def gather(k):
             c0, n, s = GROUPS[k]
@@ -143,7 +141,7 @@ def tile_moe_bdx_mlp_relu2_kernel(
             if k in ROUNDED_AT:
                 rounded[k] = rooms.tile([P, n, PACK], BF16, name=f"g_bf16_{k}", align_bytes=64, offset=ROUNDED_AT[k])
             else:
-                rounded[k] = keep.tile([P, n, PACK], BF16, name=f"g_bf16_{k}", align_bytes=64)
+                rounded[k] = stage.tile([P, n, PACK], BF16, name="g_bf16", align_bytes=64)
             nc.scalar.copy(
                 out=rounded[k][:].rearrange("p (c i) j -> p c j i", i=4), in_=g[:].rearrange("p j (c i) -> p c j i", i=4)
             )
@@ -172,10 +170,10 @@ def tile_moe_bdx_mlp_relu2_kernel(
 
         def make_slope(b):
             if b == 4:
-                slopes = rooms.tile([P, 3, H], F32, name="slope_4", align_bytes=64, offset=SLOPE_AT[b] * KB)
-                slope.update({4 + h: slopes[:, h, :] for h in range(3)})
-            elif b in SLOPE_AT:
-                slope[b] = rooms.tile([P, H], F32, name=f"slope_{b}", align_bytes=64, offset=SLOPE_AT[b] * KB)[:]
+                slopes = rooms.tile([P, 4, H], F32, name="slope_4", align_bytes=64, offset=MIDDLE_SLOPES_AT)
+                slope.update({4 + h: slopes[:, h, :] for h in range(4)})
+            elif b not in slope:
+                slope[b] = keep.tile([P, H], F32, name=f"slope_{b}")[:]
             turned = psum.tile([P, PACK, P], F32, name=f"a_turned_{b}", offset=(4 + b % 4) * BANK)
             col = b % 4 * P
             for t in range(PACK):
@@ -213,17 +211,15 @@ def tile_moe_bdx_mlp_relu2_kernel(
         def make_da(b):
             e, h = divmod(b, C // P)
             if b in ON_GPSIMD:
-                if not shared_da:
-                    shared_da.append(
-                        rooms.tile([P, len(ON_GPSIMD) * H], BF16, name="shared_da", align_bytes=64, offset=SHARED_DA_AT)
-                    )
-                da = shared_da[0][:, b * H : (b + 1) * H]
+                if h == 0:
+                    shared_da[e] = rooms.tile([P, 2 * H], BF16, name=f"shared_da_{e}", align_bytes=64, offset=SHARED_DA_AT[e])
+                da = shared_da[e][:, h * H : (h + 1) * H]
                 nc.gpsimd.tensor_tensor(da, dh_copy[b], slope[b], MULT)
             else:
-                if b == 2:
-                    early_da.append(rooms.tile([P, 2 * H], BF16, name="early_da", align_bytes=64, offset=DY3_AT))
-                if b < 4:
-                    da = early_da[0][:, (b - 2) * H : (b - 1) * H]
+                if b == 4:
+                    shared_da[2] = rooms.tile([P, 4 * H], BF16, name="middle_da", align_bytes=64, offset=MIDDLE_DA_AT)
+                if b < 8:
+                    da = shared_da[2][:, (b - 4) * H : (b - 3) * H]
                 else:
                     da = stage.tile([P, H], BF16, name="da", align_bytes=64)[:]
                 nc.vector.tensor_tensor(
@@ -232,15 +228,19 @@ def tile_moe_bdx_mlp_relu2_kernel(
                     slope[b].rearrange("s (u p e) -> s u p e", u=2, e=2),
                     MULT,
                 )
-            pairs = da.bitcast(F32)
+            made[b] = da
+
+        def turn_da(b):
+            e, h = divmod(b, C // P)
+            pairs = made[b].bitcast(F32)
             turned = psum.tile([P, 2, P], F32, name=f"da_turned_{b}", offset=TURN_BANK[b] * BANK)
             for u in range(2):
                 nc.tensor.transpose(turned[:, u, :], pairs[:, u * P : (u + 1) * P], ident[:])
             nc.scalar.copy(out=da_packed[e][:, h * P : (h + 1) * P, :], in_=turned[:].rearrange("p u s -> p s u"))
 
         def quantise_da(e):
-            if e == 3:
-                da_codes[e] = rooms.tile([P, C], U32, name="da_codes_3", align_bytes=64, offset=SLOPE_AT[10] * KB)
+            if e not in da_codes:
+                da_codes[e] = rooms.tile([P, C], U32, name=f"da_codes_{e}", align_bytes=64, offset=DH_COPY_AT + e * KB)
             flat = da_packed[e][:].rearrange("p c u -> p (c u)").bitcast(BF16)
             nc.vector.quantize_mx(out=da_codes[e][:].bitcast(FP8X4), scales=da_scales[e][:], in_=flat)
 
@@ -267,6 +267,8 @@ def tile_moe_bdx_mlp_relu2_kernel(
             c0, n, s = GROUPS[k]
             for b in after:
                 make_da(b)
+                if b not in ON_GPSIMD:
+                    turn_da(b)
             for b in range(c0 // P, (c0 + n) // P):
                 product_dh(b, s)
 
@@ -278,40 +280,35 @@ def tile_moe_bdx_mlp_relu2_kernel(
         gather(2)
         first_layer(1)
         gather(3)
-        quantise(2)
-        for b in range(4, 6):
-            product_dh(b, 0)
+        first_layer(2)
         for b in range(4, 12):
             make_slope(b)
         gather(4)
-        quantise(3)
-        make_da(2)
-        make_da(3)
-        product_dh(6, 0)
-        product_dh(7, 0)
-        for b in range(4, 8):
-            product_dh(b, 1)
+        first_layer(3)
         gather(5)
-        first_layer(4, (4, 5, 6))
-        quantise_da(1)
+        first_layer(4, (4, 5, 2, 6, 7, 3))
         gather(6)
         first_layer(5)
         first_layer(6)
         quantise_da(2)
-        for b in (7, 8, 0, 9, 10, 1, 11):
-            make_da(b)
-        product_dx((1, 2), 0, 2)
         quantise_da(3)
-        product_dx((3,), 0, 5)
-        quantise_da(0)
-        product_dx((0,), 0, 0)
+        turn_da(2)
+        turn_da(3)
+        for b in (8, 9, 0, 10, 11, 1):
+            make_da(b)
+            turn_da(b)
+        product_dx((2, 3), 0, 2)
+        quantise_da(1)
         quantise_da(4)
+        product_dx((1,), 0, 7)
         product_dx((4,), 0, 3)
         quantise_da(5)
-        product_dx((5,), 0, 1, on_vector=True)
+        quantise_da(0)
+        product_dx((5,), 0, 0, on_vector=True)
+        product_dx((0,), 0, 1)
         for k in range(1, 4):
-            for m, experts in enumerate(((1, 2), (3, 4), (0,), (5,))):
-                product_dx(experts, k, (2, 6, 7, 4, 5, 0, 3, 1)[(4 * (k - 1) + m) % 8])
+            for m, experts in enumerate(((2, 3), (4, 5), (0, 1))):
+                product_dx(experts, k, (6, 5, 4, 2, 7, 3, 0, 1)[(3 * (k - 1) + m) % 8])
 
         first = {}
 

@@ -19,26 +19,38 @@ FP8X4 = mybir.dt.float8_e4m3fn_x4
 FP4X4 = mybir.dt.float4_e2m1fn_x4
 MULT = mybir.AluOpType.mult
 ADD = mybir.AluOpType.add
-MAX = mybir.AluOpType.max
 RELU = mybir.ActivationFunctionType.Relu
-COPY = mybir.ActivationFunctionType.Copy
 
-GATES = ((0, 512), (512, 512), (1024, 512))
-GROUPS = ((0, 512, 0), (0, 512, 1), (512, 512, 0), (512, 512, 1), (1024, 512, 0), (1024, 384, 1), (1408, 128, 1))
+CHUNK = 512
+CHUNK_BLOCKS = CHUNK // P
+GROUPS = (
+    (0, CHUNK, 0),
+    (0, CHUNK, 1),
+    (CHUNK, CHUNK, 0),
+    (CHUNK, CHUNK, 1),
+    (2 * CHUNK, CHUNK, 0),
+    (2 * CHUNK, CHUNK - P, 1),
+    (S - P, P, 1),
+)
 ON_GPSIMD = (0, 1, 2, 3)
+LAST_STORE = 256
+
 KB = 1024
 EDGE = 64
-G_AT = {0: 8 * KB, 2: 8 * KB, 4: 16 * KB - EDGE, 6: 2 * KB, 1: 24 * KB, 3: 24 * KB, 5: 24 * KB}
-ROUNDED_AT = {4: 32 * KB, 6: 36 * KB}
-MIDDLE_SLOPES_AT = EDGE
-MIDDLE_DA_AT = 18 * KB
-SHARED_DA_AT = {0: ROUNDED_AT[6], 1: ROUNDED_AT[4]}
-DY2_AT = 38 * KB
+EVEN_AT, ODD_AT = 8 * KB, 24 * KB
+MIDDLE_SLOPES_AT = EVEN_AT - 4 * KB + EDGE
+GROUP_AT = {0: EVEN_AT, 1: ODD_AT, 2: EVEN_AT, 3: ODD_AT, 4: EVEN_AT + 8 * KB - EDGE, 5: ODD_AT, 6: EVEN_AT - 3 * KB}
+ROUNDED_AT = {4: 32 * KB, 6: 59 * KB}
+DY_AT = {2: 38 * KB, 6: 49 * KB, 7: 52 * KB}
 DH_COPY_AT = 41 * KB
-DH_BANK = (0, 1, 2, 3, 0, 1, 2, 3, 4, 5, 0, 1)
-TURN_BANK = {4: 6, 5: 7, 6: 6, 7: 7, 2: 2, 3: 3, 8: 6, 9: 7, 0: 3, 10: 4, 11: 5, 1: 6}
+LAST_SLOPES_AT = 55 * KB
+SLOPES_AT = {4: MIDDLE_SLOPES_AT, 10: LAST_SLOPES_AT}
+DA_AT = {0: (3, DY_AT[7]), 3: (1, ROUNDED_AT[4]), 4: (2, EVEN_AT + 10 * KB), 6: (2, DY_AT[6]), 8: (3, ROUNDED_AT[6])}
+
 BANK = 2 * KB
-BLOCKS = S // P
+DH_BANK = (0, 1, 2, 3, 0, 1, 2, 3, 4, 5, 0, 1)
+TURN_BANK = {4: 6, 3: 7, 6: 6, 0: DH_BANK[8], 8: DH_BANK[6], 10: DH_BANK[7], 11: DH_BANK[9], 2: DH_BANK[11]}
+LATE_BANKS = (TURN_BANK[2], TURN_BANK[11], TURN_BANK[10], TURN_BANK[0], 7, 0, 2, 6)
 
 
 def tile_moe_bdx_mlp_relu2_kernel(
@@ -49,7 +61,7 @@ def tile_moe_bdx_mlp_relu2_kernel(
         lists = ctx.enter_context(tc.tile_pool(name="lists", bufs=1))
         keep = ctx.enter_context(tc.tile_pool(name="keep", bufs=1))
         stage = ctx.enter_context(tc.tile_pool(name="stage", bufs=3))
-        rooms = ctx.enter_context(tc.tile_pool(name="rooms", bufs=1))
+        shared = ctx.enter_context(tc.tile_pool(name="shared", bufs=1))
         pair = ctx.enter_context(tc.tile_pool(name="pair", bufs=2))
         psum = ctx.enter_context(tc.psum_pool(name="psum", bufs=1))
 
@@ -62,15 +74,12 @@ def tile_moe_bdx_mlp_relu2_kernel(
         w1_sc = keep.tile([P, E, K], U8, name="w1_sc", align_bytes=64)
         w2 = [keep.tile([P, 2, 2 * H], U8, name=f"w2_{e}", align_bytes=64) for e in range(E)]
         w1 = [keep.tile([P, 2 * K], U8, name=f"w1_{e}", align_bytes=64) for e in range(E)]
-        dy = [keep.tile([P, T], F32, name=f"dy_{m}") for m in range(N // P) if m != 2]
-        dy[2:2] = [rooms.tile([P, T], F32, name="dy_2", offset=DY2_AT)]
-        gates = [keep.tile([P, n], F32, name=f"gate_{c0}") for c0, n in GATES]
-        saved = [keep.tile([P, PACK, n], F32, name=f"saved_{c0}") for c0, n in GATES]
-
-        slope = {}
+        dy = {m: keep.tile([P, T], F32, name=f"dy_{m}") for m in range(N // P) if m not in DY_AT}
+        dy.update({m: shared.tile([P, T], F32, name=f"dy_{m}", offset=at) for m, at in DY_AT.items()})
+        gates = [keep.tile([P, CHUNK], F32, name=f"gate_{c}") for c in range(S // CHUNK)]
+        saved = [keep.tile([P, PACK, CHUNK], F32, name=f"saved_{c}") for c in range(S // CHUNK)]
         da_packed = [keep.tile([P, C, 2], F32, name=f"da_packed_{e}", align_bytes=64) for e in range(E)]
-        da_codes = {e: keep.tile([P, C], U32, name=f"da_codes_{e}", align_bytes=64) for e in (0, 2, 3, 5)}
-        dh_copy = {}
+        da_codes = {e: keep.tile([P, C], U32, name=f"da_codes_{e}", align_bytes=64) for e in (1, 2, 5)}
         da_scales = [keep.tile([P, C], U8, name=f"da_scales_{e}", align_bytes=64) for e in range(E)]
         dx = [keep.tile([P, S], F32, name=f"dx_{k}") for k in range(K // P)]
 
@@ -80,16 +89,17 @@ def tile_moe_bdx_mlp_relu2_kernel(
 
         dy_rows = dyT.rearrange("(s p j) t -> s j p t", s=2, j=PACK)
         a_rows = a.rearrange("(t p) c -> p t c", p=P)
-        w2_rows = w2_scales.bitcast(I32).rearrange("e s f i -> f (e s) i")
-        w1_rows = w1_scales.bitcast(I32).rearrange("e s f i -> f (e s) i")
 
         def load_gate(c):
-            c0, n = GATES[c]
-            nc.sync.dma_start(out=gates[c][:], in_=gate[0:P, c0 : c0 + n])
+            nc.sync.dma_start(out=gates[c][:], in_=gate[0:P, c * CHUNK : (c + 1) * CHUNK])
 
         def load_saved(c):
-            c0, n = GATES[c]
-            nc.sync.dma_start(out=saved[c][:], in_=a_rows[:, :, c0 : c0 + n])
+            nc.sync.dma_start(out=saved[c][:], in_=a_rows[:, :, c * CHUNK : (c + 1) * CHUNK])
+
+        def load_scales(plane, scales):
+            rows = scales.bitcast(I32).rearrange("e s f i -> f (e s) i")
+            for q in range(4):
+                nc.sync.dma_start(out=plane[32 * q : 32 * q + 4].bitcast(I32), in_=rows[4 * q : 4 * q + 4])
 
         def load_w2(e):
             nc.sync.dma_start(out=w2[e][:].bitcast(I32), in_=w2_words[e].rearrange("s p b -> p s b").bitcast(I32))
@@ -103,8 +113,7 @@ def tile_moe_bdx_mlp_relu2_kernel(
             nc.sync.dma_start(out=dy[m][:], in_=dy_rows[m // PACK, m % PACK])
         load_gate(1)
         load_saved(0)
-        for q in range(4):
-            nc.sync.dma_start(out=w2_sc[32 * q : 32 * q + 4].bitcast(I32), in_=w2_rows[4 * q : 4 * q + 4])
+        load_scales(w2_sc, w2_scales)
         load_w2(0)
         load_w2(1)
         load_saved(1)
@@ -114,46 +123,49 @@ def tile_moe_bdx_mlp_relu2_kernel(
         load_saved(2)
         load_w2(4)
         load_w2(5)
-        for q in range(4):
-            nc.sync.dma_start(out=w1_sc[32 * q : 32 * q + 4].bitcast(I32), in_=w1_rows[4 * q : 4 * q + 4])
+        load_scales(w1_sc, w1_scales)
         for e in range(E):
             load_w1(e)
         nc.sync.dma_start(pos1_sb[:], pos1)
         nc.sync.dma_start(pos2_sb[:], pos2)
 
-        rounded = {}
-        g_codes = {}
-        dh = {}
-        shared_da = {}
-        made = {}
+        rounded, g_codes, slope, dh, dh_copy, da, first = {}, {}, {}, {}, {}, {}, {}
 
-        def gather(k):
-            c0, n, s = GROUPS[k]
-            g = rooms.tile([P, PACK, n], F32, name=f"g_{k}", align_bytes=64, offset=G_AT[k])
-            first = c0 % 512
+        def by_pairs(columns):
+            return columns.rearrange("s (u p e) -> s u p e", u=2, e=2)
+
+        def into_pairs(columns):
+            return columns.rearrange("s (p u e) -> s u p e", u=2, e=2)
+
+        def gather(group):
+            c0, n, s = GROUPS[group]
+            g = shared.tile([P, PACK, n], F32, name=f"g_{group}", align_bytes=64, offset=GROUP_AT[group])
+            chunk, col = divmod(c0, CHUNK)
             for j in range(PACK):
                 nc.vector.tensor_tensor(
                     g[:, j, :],
                     dy[PACK * s + j][:].indirect(offs_sb[:, c0 // 16 : (c0 + n) // 16]),
-                    gates[c0 // 512][:, first : first + n],
+                    gates[chunk][:, col : col + n],
                     MULT,
                 )
-            if k in ROUNDED_AT:
-                rounded[k] = rooms.tile([P, n, PACK], BF16, name=f"g_bf16_{k}", align_bytes=64, offset=ROUNDED_AT[k])
+            if group in ROUNDED_AT:
+                at = ROUNDED_AT[group]
+                rounded[group] = shared.tile([P, n, PACK], BF16, name=f"g_bf16_{group}", align_bytes=64, offset=at)
             else:
-                rounded[k] = stage.tile([P, n, PACK], BF16, name="g_bf16", align_bytes=64)
+                rounded[group] = stage.tile([P, n, PACK], BF16, name="g_bf16", align_bytes=64)
             nc.scalar.copy(
-                out=rounded[k][:].rearrange("p (c i) j -> p c j i", i=4), in_=g[:].rearrange("p j (c i) -> p c j i", i=4)
+                out=rounded[group][:].rearrange("p (c i) j -> p c j i", i=4),
+                in_=g[:].rearrange("p j (c i) -> p c j i", i=4),
             )
 
-        def quantise(k):
-            c0, n, s = GROUPS[k]
-            if k == 3:
-                codes = rooms.tile([P, n], U32, name="g_codes_3", align_bytes=64, offset=DY2_AT)
+        def quantise_g(group):
+            c0, n, s = GROUPS[group]
+            if group == 3:
+                codes = shared.tile([P, n], U32, name="g_codes_3", align_bytes=64, offset=DY_AT[2])
             else:
                 codes = stage.tile([P, n], U32, name="g_codes", align_bytes=64)
             scales = stage.tile([P, n], U8, name="g_scales", align_bytes=64)
-            flat = rounded[k][:].rearrange("p c j -> p (c j)")
+            flat = rounded[group][:].rearrange("p c j -> p (c j)")
             done = 0
             for width in (512, 256, 128):
                 if n - done >= width:
@@ -164,25 +176,22 @@ def tile_moe_bdx_mlp_relu2_kernel(
                         in_=flat[:, PACK * done : PACK * (done + width)],
                     )
                     done += width
-            for b in range(n // P):
-                cols = slice(b * P, (b + 1) * P)
-                g_codes[c0 // P + b, s] = (codes[:, cols], scales[:, cols])
+            for h in range(n // P):
+                cols = slice(h * P, (h + 1) * P)
+                g_codes[c0 // P + h, s] = (codes[:, cols], scales[:, cols])
 
         def make_slope(b):
-            if b == 4:
-                slopes = rooms.tile([P, 4, H], F32, name="slope_4", align_bytes=64, offset=MIDDLE_SLOPES_AT)
-                slope.update({4 + h: slopes[:, h, :] for h in range(4)})
+            if b in SLOPES_AT:
+                both = shared.tile([P, 2, H], F32, name=f"slope_{b}", align_bytes=64, offset=SLOPES_AT[b])
+                slope.update({b + h: both[:, h, :] for h in range(2)})
             elif b not in slope:
                 slope[b] = keep.tile([P, H], F32, name=f"slope_{b}")[:]
-            turned = psum.tile([P, PACK, P], F32, name=f"a_turned_{b}", offset=(4 + b % 4) * BANK)
-            col = b % 4 * P
+            chunk, h = divmod(b, CHUNK_BLOCKS)
+            turned = psum.tile([P, PACK, P], F32, name=f"a_turned_{b}", offset=(4 + h) * BANK)
             for t in range(PACK):
-                nc.tensor.transpose(turned[:, t, :], saved[b // 4][:, t, col : col + P], ident[:])
+                nc.tensor.transpose(turned[:, t, :], saved[chunk][:, t, h * P : (h + 1) * P], ident[:])
             nc.scalar.activation(
-                out=slope[b].rearrange("s (u p e) -> s u p e", u=2, e=2),
-                in_=turned[:].rearrange("s t q -> s (t q)").rearrange("s (p u e) -> s u p e", u=2, e=2),
-                func=RELU,
-                scale=2.0,
+                out=by_pairs(slope[b]), in_=into_pairs(turned[:].rearrange("s t q -> s (t q)")), func=RELU, scale=2.0
             )
 
         def product_dh(b, s):
@@ -201,50 +210,43 @@ def tile_moe_bdx_mlp_relu2_kernel(
             )
             if s == 1 and b in ON_GPSIMD:
                 if not dh_copy:
-                    copies = rooms.tile([P, len(ON_GPSIMD), H], F32, name="dh_copy", align_bytes=64, offset=DH_COPY_AT)
+                    copies = shared.tile([P, len(ON_GPSIMD), H], F32, name="dh_copy", align_bytes=64, offset=DH_COPY_AT)
                     dh_copy.update({h: copies[:, h, :] for h in ON_GPSIMD})
-                nc.scalar.copy(
-                    out=dh_copy[b].rearrange("s (u p e) -> s u p e", u=2, e=2),
-                    in_=dh[b][:].rearrange("s (p u e) -> s u p e", u=2, e=2),
-                )
+                nc.scalar.copy(out=by_pairs(dh_copy[b]), in_=into_pairs(dh[b][:]))
 
         def make_da(b):
-            e, h = divmod(b, C // P)
+            if b in DA_AT:
+                count, at = DA_AT[b]
+                several = shared.tile([P, count * H], BF16, name=f"da_{b}", align_bytes=64, offset=at)
+                da.update({b + h: several[:, h * H : (h + 1) * H] for h in range(count)})
+            elif b not in da:
+                da[b] = keep.tile([P, H], BF16, name=f"da_{b}", align_bytes=64)[:]
             if b in ON_GPSIMD:
-                if h == 0:
-                    shared_da[e] = rooms.tile([P, 2 * H], BF16, name=f"shared_da_{e}", align_bytes=64, offset=SHARED_DA_AT[e])
-                da = shared_da[e][:, h * H : (h + 1) * H]
-                nc.gpsimd.tensor_tensor(da, dh_copy[b], slope[b], MULT)
+                nc.gpsimd.tensor_tensor(da[b], dh_copy[b], slope[b], MULT)
             else:
-                if b == 4:
-                    shared_da[2] = rooms.tile([P, 4 * H], BF16, name="middle_da", align_bytes=64, offset=MIDDLE_DA_AT)
-                if b < 8:
-                    da = shared_da[2][:, (b - 4) * H : (b - 3) * H]
-                else:
-                    da = stage.tile([P, H], BF16, name="da", align_bytes=64)[:]
-                nc.vector.tensor_tensor(
-                    da.rearrange("s (u p e) -> s u p e", u=2, e=2),
-                    dh[b][:].rearrange("s (p u e) -> s u p e", u=2, e=2),
-                    slope[b].rearrange("s (u p e) -> s u p e", u=2, e=2),
-                    MULT,
-                )
-            made[b] = da
+                nc.vector.tensor_tensor(by_pairs(da[b]), into_pairs(dh[b][:]), by_pairs(slope[b]), MULT)
 
-        def turn_da(b):
-            e, h = divmod(b, C // P)
-            pairs = made[b].bitcast(F32)
-            turned = psum.tile([P, 2, P], F32, name=f"da_turned_{b}", offset=TURN_BANK[b] * BANK)
-            for u in range(2):
-                nc.tensor.transpose(turned[:, u, :], pairs[:, u * P : (u + 1) * P], ident[:])
-            nc.scalar.copy(out=da_packed[e][:, h * P : (h + 1) * P, :], in_=turned[:].rearrange("p u s -> p s u"))
+        def turn_da(*blocks):
+            e, h = divmod(blocks[0], C // P)
+            bank = TURN_BANK[blocks[0]]
+            turned = psum.tile([P, len(blocks), 2, P], F32, name=f"da_turned_{blocks[0]}", offset=bank * BANK)
+            for m, b in enumerate(blocks):
+                words = da[b].bitcast(F32)
+                for u in range(2):
+                    nc.tensor.transpose(turned[:, m, u, :], words[:, u * P : (u + 1) * P], ident[:])
+            nc.scalar.copy(
+                out=da_packed[e][:, h * P : (h + len(blocks)) * P, :].rearrange("p (m s) u -> p m s u", s=P),
+                in_=turned[:].rearrange("p m u s -> p m s u"),
+            )
 
         def quantise_da(e):
             if e not in da_codes:
-                da_codes[e] = rooms.tile([P, C], U32, name=f"da_codes_{e}", align_bytes=64, offset=DH_COPY_AT + e * KB)
+                at = LAST_SLOPES_AT + e // 2 * KB
+                da_codes[e] = shared.tile([P, C], U32, name=f"da_codes_{e}", align_bytes=64, offset=at)
             flat = da_packed[e][:].rearrange("p c u -> p (c u)").bitcast(BF16)
             nc.vector.quantize_mx(out=da_codes[e][:].bitcast(FP8X4), scales=da_scales[e][:], in_=flat)
 
-        def product_dx(experts, k, bank, on_vector=False):
+        def product_dx(experts, k, bank, copy=nc.scalar.copy):
             acc = psum.tile([P, len(experts), C], F32, name=f"dx_{experts[0]}_{k}", offset=bank * BANK)
             for h, e in enumerate(experts):
                 nc.tensor.matmul_mx(
@@ -256,77 +258,72 @@ def tile_moe_bdx_mlp_relu2_kernel(
                     start=True,
                     stop=True,
                 )
-            slots = dx[k][:, experts[0] * C : (experts[-1] + 1) * C]
-            if on_vector:
-                nc.vector.tensor_copy(slots, acc[:].rearrange("p h c -> p (h c)"))
-            else:
-                nc.scalar.copy(out=slots, in_=acc[:].rearrange("p h c -> p (h c)"))
+            copy(dx[k][:, experts[0] * C : (experts[-1] + 1) * C], acc[:].rearrange("p h c -> p (h c)"))
 
-        def first_layer(k, after=()):
-            quantise(k)
-            c0, n, s = GROUPS[k]
-            for b in after:
+        def first_layer(group, freeing=()):
+            quantise_g(group)
+            c0, n, s = GROUPS[group]
+            for b in freeing:
                 make_da(b)
-                if b not in ON_GPSIMD:
-                    turn_da(b)
             for b in range(c0 // P, (c0 + n) // P):
                 product_dh(b, s)
+
+        def fetch_first(k):
+            first[k] = pair.tile([P, T], F32, name="first")
+            nc.vector.tensor_copy(first[k][:], dx[k][:].indirect(pos1_sb[:]))
+
+        def add_second(k, t0=0, t1=T):
+            total = stage.tile([P, t1 - t0], F32, name="total")
+            second = dx[k][:].indirect(pos2_sb[:, t0 // 16 : t1 // 16])
+            nc.vector.tensor_tensor(total[:], second, first[k][:, t0:t1], ADD)
+            nc.sync.dma_start(out=out[k * P : (k + 1) * P, t0:t1], in_=total[:])
 
         gather(0)
         gather(1)
         first_layer(0)
-        for b in range(0, 4):
+        for b in range(CHUNK_BLOCKS):
             make_slope(b)
         gather(2)
         first_layer(1)
         gather(3)
         first_layer(2)
-        for b in range(4, 12):
+        for b in range(CHUNK_BLOCKS, S // P):
             make_slope(b)
         gather(4)
         first_layer(3)
         gather(5)
-        first_layer(4, (4, 5, 2, 6, 7, 3))
+        first_layer(4, freeing=(4, 5, 3))
+        turn_da(4, 5)
         gather(6)
         first_layer(5)
         first_layer(6)
+
         quantise_da(2)
-        quantise_da(3)
-        turn_da(2)
         turn_da(3)
-        for b in (8, 9, 0, 10, 11, 1):
-            make_da(b)
-            turn_da(b)
-        product_dx((2, 3), 0, 2)
-        quantise_da(1)
+        for blocks in ((6, 7), (0, 1), (8, 9), (10,), (11,), (2,)):
+            for b in blocks:
+                make_da(b)
+            turn_da(*blocks)
+
+        product_dx((2,), 0, 6)
+        quantise_da(3)
         quantise_da(4)
-        product_dx((1,), 0, 7)
-        product_dx((4,), 0, 3)
-        quantise_da(5)
+        product_dx((3, 4), 0, 7)
         quantise_da(0)
-        product_dx((5,), 0, 0, on_vector=True)
-        product_dx((0,), 0, 1)
-        for k in range(1, 4):
+        product_dx((0,), 0, DH_BANK[10])
+        quantise_da(5)
+        product_dx((5,), 0, TURN_BANK[8])
+        quantise_da(1)
+        product_dx((1,), 0, 6, copy=nc.vector.tensor_copy)
+        for k in range(1, K // P):
             for m, experts in enumerate(((2, 3), (4, 5), (0, 1))):
-                product_dx(experts, k, (6, 5, 4, 2, 7, 3, 0, 1)[(3 * (k - 1) + m) % 8])
-
-        first = {}
-
-        def fetch_first(k):
-            first[k] = pair.tile([P, T], F32, name="x1")
-            nc.vector.tensor_copy(first[k][:], dx[k][:].indirect(pos1_sb[:]))
-
-        def add_second(k, c0, c1):
-            total = stage.tile([P, c1 - c0], F32, name="total")
-            nc.vector.tensor_tensor(total[:], dx[k][:].indirect(pos2_sb[:, c0 // 16 : c1 // 16]), first[k][:, c0:c1], ADD)
-            nc.sync.dma_start(out=out[k * P : (k + 1) * P, c0:c1], in_=total[:])
+                product_dx(experts, k, LATE_BANKS[(3 * (k - 1) + m) % len(LATE_BANKS)])
 
         fetch_first(0)
-        add_second(0, 0, T)
+        add_second(0)
         fetch_first(1)
-        fetch_first(2)
-        add_second(1, 0, T)
-        fetch_first(3)
-        add_second(2, 0, T)
-        add_second(3, 0, 512)
-        add_second(3, 512, T)
+        for k in range(2, K // P):
+            fetch_first(k)
+            add_second(k - 1)
+        add_second(K // P - 1, 0, T - LAST_STORE)
+        add_second(K // P - 1, T - LAST_STORE, T)

@@ -20,6 +20,7 @@ FP4X4 = mybir.dt.float4_e2m1fn_x4
 MULT = mybir.AluOpType.mult
 ADD = mybir.AluOpType.add
 RELU = mybir.ActivationFunctionType.Relu
+COPY = mybir.ActivationFunctionType.Copy
 
 CHUNK = 512
 CHUNK_BLOCKS = CHUNK // P
@@ -33,24 +34,32 @@ GROUPS = (
     (S - P, P, 1),
 )
 ON_GPSIMD = (0, 1, 2, 3)
-LAST_STORE = 256
+LAST_STORES = (448, 192, 128)
 
 KB = 1024
 EDGE = 64
 EVEN_AT, ODD_AT = 8 * KB, 24 * KB
 MIDDLE_SLOPES_AT = EVEN_AT - 4 * KB + EDGE
 GROUP_AT = {0: EVEN_AT, 1: ODD_AT, 2: EVEN_AT, 3: ODD_AT, 4: EVEN_AT + 8 * KB - EDGE, 5: ODD_AT, 6: EVEN_AT - 3 * KB}
-ROUNDED_AT = {4: 32 * KB, 6: 59 * KB}
+ROUNDED_AT = {4: 32 * KB, 5: 0, 6: 59 * KB}
 DY_AT = {2: 38 * KB, 6: 49 * KB, 7: 52 * KB}
 DH_COPY_AT = 41 * KB
 LAST_SLOPES_AT = 55 * KB
-SLOPES_AT = {4: MIDDLE_SLOPES_AT, 10: LAST_SLOPES_AT}
-DA_AT = {0: (3, DY_AT[7]), 3: (1, ROUNDED_AT[4]), 4: (2, EVEN_AT + 10 * KB), 6: (2, DY_AT[6]), 8: (3, ROUNDED_AT[6])}
+SLOPES_AT = {4: (2, MIDDLE_SLOPES_AT), 10: (1, LAST_SLOPES_AT)}
+DA_AT = {
+    0: (1, DY_AT[7]),
+    1: (2, ROUNDED_AT[6] - 2 * KB + EDGE),
+    3: (1, ROUNDED_AT[4]),
+    4: (2, EVEN_AT + 10 * KB),
+    6: (1, DY_AT[6]),
+    7: (1, ROUNDED_AT[5]),
+    8: (3, ROUNDED_AT[6] + EDGE),
+}
 
 BANK = 2 * KB
 DH_BANK = (0, 1, 2, 3, 0, 1, 2, 3, 4, 5, 0, 1)
-TURN_BANK = {4: 6, 3: 7, 6: 6, 0: DH_BANK[8], 8: DH_BANK[6], 10: DH_BANK[7], 11: DH_BANK[9], 2: DH_BANK[11]}
-LATE_BANKS = (TURN_BANK[2], TURN_BANK[11], TURN_BANK[10], TURN_BANK[0], 7, 0, 2, 6)
+TURN_BANK = {4: 6, 3: 7, 6: DH_BANK[6], 8: DH_BANK[7], 0: DH_BANK[9], 2: DH_BANK[10], 10: 6}
+LATE_BANKS = ((3, 4, 1), (1, 3, 5), (4, 5, 0))
 
 
 def tile_moe_bdx_mlp_relu2_kernel(
@@ -79,7 +88,7 @@ def tile_moe_bdx_mlp_relu2_kernel(
         gates = [keep.tile([P, CHUNK], F32, name=f"gate_{c}") for c in range(S // CHUNK)]
         saved = [keep.tile([P, PACK, CHUNK], F32, name=f"saved_{c}") for c in range(S // CHUNK)]
         da_packed = [keep.tile([P, C, 2], F32, name=f"da_packed_{e}", align_bytes=64) for e in range(E)]
-        da_codes = {e: keep.tile([P, C], U32, name=f"da_codes_{e}", align_bytes=64) for e in (1, 2, 5)}
+        da_codes = {e: keep.tile([P, C], U32, name=f"da_codes_{e}", align_bytes=64) for e in range(E) if e != 2}
         da_scales = [keep.tile([P, C], U8, name=f"da_scales_{e}", align_bytes=64) for e in range(E)]
         dx = [keep.tile([P, S], F32, name=f"dx_{k}") for k in range(K // P)]
 
@@ -108,9 +117,10 @@ def tile_moe_bdx_mlp_relu2_kernel(
             nc.sync.dma_start(out=w1[e][:].bitcast(I32), in_=w1_words[e, 0].bitcast(I32))
 
         nc.sync.dma_start(offs_sb[:], offs)
-        load_gate(0)
         for m in range(N // P):
             nc.sync.dma_start(out=dy[m][:], in_=dy_rows[m // PACK, m % PACK])
+            if m == 1:
+                load_gate(0)
         load_gate(1)
         load_saved(0)
         load_scales(w2_sc, w2_scales)
@@ -158,6 +168,49 @@ def tile_moe_bdx_mlp_relu2_kernel(
                 in_=g[:].rearrange("p j (c i) -> p c j i", i=4),
             )
 
+        def gather_plain(group, first_bank):
+            c0, n, s = GROUPS[group]
+            g = shared.tile([P, PACK, n], F32, name=f"g_{group}", align_bytes=64, offset=GROUP_AT[group])
+            chunk, col = divmod(c0, CHUNK)
+            blocks = n // P
+            gate_turned = psum.tile([P, blocks, P], F32, name=f"gate_turned_{group}", offset=(first_bank + 6) * BANK)
+            for h in range(blocks):
+                nc.tensor.transpose(gate_turned[:, h, :], gates[chunk][:, col + h * P : col + (h + 1) * P], ident[:])
+            gate_col = keep.tile([P, blocks], F32, name=f"gate_col_{group}")
+            nc.scalar.copy(out=gate_col[:], in_=gate_turned[:, :, 0])
+            pairs = keep.tile([P, blocks, 2, P, 2], BF16, name=f"g_pairs_{group}", align_bytes=64)
+            for u in range(2):
+                for e in range(2):
+                    nc.vector.tensor_copy(
+                        g[:, 2 * u + e, :], dy[PACK * s + 2 * u + e][:].indirect(offs_sb[:, c0 // 16 : (c0 + n) // 16])
+                    )
+                for h0 in range(0, blocks, 2):
+                    bank = first_bank + 2 * u + h0 // 2
+                    turned = psum.tile([P, 2, 2, P], F32, name=f"g_turned_{group}_{u}_{h0}", offset=bank * BANK)
+                    for h in range(h0, h0 + 2):
+                        for e in range(2):
+                            nc.tensor.transpose(turned[:, h - h0, e, :], g[:, 2 * u + e, h * P : (h + 1) * P], ident[:])
+                    for h in range(h0, h0 + 2):
+                        nc.scalar.activation(
+                            out=pairs[:, h, u, :, :],
+                            in_=turned[:, h - h0, :, :].rearrange("s e p -> s p e"),
+                            func=COPY,
+                            scale=gate_col[:, h : h + 1],
+                        )
+            rounded[group] = stage.tile([P, n, PACK], BF16, name="g_bf16", align_bytes=64)
+            words = rounded[group][:].rearrange("p c j -> p (c j)").bitcast(F32).rearrange("p (c u) -> p c u", u=2)
+            for h0 in range(0, blocks, 2):
+                bank = first_bank + 4 + h0 // 2
+                back = psum.tile([P, 2, 2, P], F32, name=f"g_back_{group}_{h0}", offset=bank * BANK)
+                for h in range(h0, h0 + 2):
+                    for u in range(2):
+                        pair_words = pairs[:, h, u, :, :].rearrange("s p e -> s (p e)").bitcast(F32)
+                        nc.tensor.transpose(back[:, h - h0, u, :], pair_words, ident[:])
+                nc.scalar.copy(
+                    out=words[:, h0 * P : (h0 + 2) * P, :].rearrange("p (m s) u -> p m s u", s=P),
+                    in_=back[:].rearrange("p m u s -> p m s u"),
+                )
+
         def quantise_g(group):
             c0, n, s = GROUPS[group]
             if group == 3:
@@ -182,8 +235,9 @@ def tile_moe_bdx_mlp_relu2_kernel(
 
         def make_slope(b):
             if b in SLOPES_AT:
-                both = shared.tile([P, 2, H], F32, name=f"slope_{b}", align_bytes=64, offset=SLOPES_AT[b])
-                slope.update({b + h: both[:, h, :] for h in range(2)})
+                count, at = SLOPES_AT[b]
+                both = shared.tile([P, count, H], F32, name=f"slope_{b}", align_bytes=64, offset=at)
+                slope.update({b + h: both[:, h, :] for h in range(count)})
             elif b not in slope:
                 slope[b] = keep.tile([P, H], F32, name=f"slope_{b}")[:]
             chunk, h = divmod(b, CHUNK_BLOCKS)
@@ -241,8 +295,7 @@ def tile_moe_bdx_mlp_relu2_kernel(
 
         def quantise_da(e):
             if e not in da_codes:
-                at = LAST_SLOPES_AT + e // 2 * KB
-                da_codes[e] = shared.tile([P, C], U32, name=f"da_codes_{e}", align_bytes=64, offset=at)
+                da_codes[e] = shared.tile([P, C], U32, name=f"da_codes_{e}", align_bytes=64, offset=LAST_SLOPES_AT)
             flat = da_packed[e][:].rearrange("p c u -> p (c u)").bitcast(BF16)
             nc.vector.quantize_mx(out=da_codes[e][:].bitcast(FP8X4), scales=da_scales[e][:], in_=flat)
 
@@ -268,9 +321,10 @@ def tile_moe_bdx_mlp_relu2_kernel(
             for b in range(c0 // P, (c0 + n) // P):
                 product_dh(b, s)
 
-        def fetch_first(k):
-            first[k] = pair.tile([P, T], F32, name="first")
-            nc.vector.tensor_copy(first[k][:], dx[k][:].indirect(pos1_sb[:]))
+        def fetch_first(k, t0=0, t1=T):
+            if t0 == 0:
+                first[k] = pair.tile([P, T], F32, name="first")
+            nc.vector.tensor_copy(first[k][:, t0:t1], dx[k][:].indirect(pos1_sb[:, t0 // 16 : t1 // 16]))
 
         def add_second(k, t0=0, t1=T):
             total = stage.tile([P, t1 - t0], F32, name="total")
@@ -278,7 +332,7 @@ def tile_moe_bdx_mlp_relu2_kernel(
             nc.vector.tensor_tensor(total[:], second, first[k][:, t0:t1], ADD)
             nc.sync.dma_start(out=out[k * P : (k + 1) * P, t0:t1], in_=total[:])
 
-        gather(0)
+        gather_plain(0, 0)
         gather(1)
         first_layer(0)
         for b in range(CHUNK_BLOCKS):
@@ -293,37 +347,40 @@ def tile_moe_bdx_mlp_relu2_kernel(
         first_layer(3)
         gather(5)
         first_layer(4, freeing=(4, 5, 3))
-        turn_da(4, 5)
         gather(6)
         first_layer(5)
         first_layer(6)
+        turn_da(4, 5)
 
-        quantise_da(2)
         turn_da(3)
-        for blocks in ((6, 7), (0, 1), (8, 9), (10,), (11,), (2,)):
+        for blocks in ((6, 7), (8, 9), (0, 1), (2,), (10, 11)):
             for b in blocks:
                 make_da(b)
             turn_da(*blocks)
 
-        product_dx((2,), 0, 6)
+        quantise_da(2)
         quantise_da(3)
+        product_dx((2, 3), 0, 7)
         quantise_da(4)
-        product_dx((3, 4), 0, 7)
+        product_dx((4,), 0, 2)
         quantise_da(0)
-        product_dx((0,), 0, DH_BANK[10])
-        quantise_da(5)
-        product_dx((5,), 0, TURN_BANK[8])
         quantise_da(1)
-        product_dx((1,), 0, 6, copy=nc.vector.tensor_copy)
+        product_dx((0, 1), 0, 3)
+        quantise_da(5)
+        product_dx((5,), 0, 4, copy=nc.vector.tensor_copy)
         for k in range(1, K // P):
-            for m, experts in enumerate(((2, 3), (4, 5), (0, 1))):
-                product_dx(experts, k, LATE_BANKS[(3 * (k - 1) + m) % len(LATE_BANKS)])
+            for m, experts in enumerate(((2, 3), (0, 1), (4, 5))):
+                product_dx(experts, k, LATE_BANKS[k - 1][m])
 
-        fetch_first(0)
-        add_second(0)
+        fetch_first(0, 0, T // 2)
+        fetch_first(0, T // 2, T)
+        add_second(0, 0, T // 2)
+        add_second(0, T // 2, T)
         fetch_first(1)
         for k in range(2, K // P):
             fetch_first(k)
             add_second(k - 1)
-        add_second(K // P - 1, 0, T - LAST_STORE)
-        add_second(K // P - 1, T - LAST_STORE, T)
+        done = 0
+        for width in LAST_STORES:
+            add_second(K // P - 1, done, done + width)
+            done += width

@@ -32,34 +32,35 @@ GROUPS = (
     (2 * CHUNK, CHUNK, 0),
     (2 * CHUNK, CHUNK - P, 1),
     (S - P, P, 1),
+    (2 * CHUNK, CHUNK, 1),
 )
 ON_GPSIMD = (0, 1, 2, 3)
 LAST_STORES = (448, 192, 128)
 
+SAVED_PARTS = ((0, 2), (2, 4), (4, 8), (8, 12))
 KB = 1024
 EDGE = 64
 EVEN_AT, ODD_AT = 8 * KB, 24 * KB
-MIDDLE_SLOPES_AT = EVEN_AT - 4 * KB + EDGE
-GROUP_AT = {0: EVEN_AT, 1: ODD_AT, 2: EVEN_AT, 3: ODD_AT, 4: EVEN_AT + 8 * KB - EDGE, 5: ODD_AT, 6: EVEN_AT - 3 * KB}
-ROUNDED_AT = {4: 32 * KB, 5: 0, 6: 59 * KB}
-DY_AT = {2: 38 * KB, 6: 49 * KB, 7: 52 * KB}
+MIDDLE_SLOPES_AT = EVEN_AT - 4 * KB
+GROUP_AT = {0: EVEN_AT, 1: ODD_AT, 2: EVEN_AT, 3: ODD_AT, 4: EVEN_AT + 8 * KB - EDGE, 5: ODD_AT, 6: ODD_AT - 2 * KB}
+LAST_ROUNDED_AT = 2 * KB
+W2_1_AT = 32 * KB
+DY_AT = {2: 38 * KB, 7: 52 * KB}
 DH_COPY_AT = 41 * KB
-LAST_SLOPES_AT = 55 * KB
-SLOPES_AT = {4: (2, MIDDLE_SLOPES_AT), 10: (1, LAST_SLOPES_AT)}
+LAST_SLOPES_AT = 49 * KB
+SLOPES_AT = {10: (1, LAST_SLOPES_AT)}
 DA_AT = {
-    0: (1, DY_AT[7]),
-    1: (2, ROUNDED_AT[6] - 2 * KB + EDGE),
-    3: (1, ROUNDED_AT[4]),
+    0: (3, LAST_ROUNDED_AT + 3 * KB),
+    3: (1, DY_AT[7]),
     4: (2, EVEN_AT + 10 * KB),
-    6: (1, DY_AT[6]),
-    7: (1, ROUNDED_AT[5]),
-    8: (3, ROUNDED_AT[6] + EDGE),
+    6: (2, LAST_ROUNDED_AT),
 }
 
 BANK = 2 * KB
-DH_BANK = (0, 1, 2, 3, 0, 1, 2, 3, 4, 5, 0, 1)
-TURN_BANK = {4: 6, 3: 7, 6: DH_BANK[6], 8: DH_BANK[7], 0: DH_BANK[9], 2: DH_BANK[10], 10: 6}
-LATE_BANKS = ((3, 4, 1), (1, 3, 5), (4, 5, 0))
+SLOPE_BANK = (7, 6, 4, 5, 7, 6, 4, 5, 0, 1, 2, 3)
+DH_BANK = (0, 1, 2, 3, 0, 1, 2, 3, 4, 5, 6, 7)
+TURN_BANK = {4: 0, 3: 1, 6: DH_BANK[6], 0: DH_BANK[8], 8: DH_BANK[7], 10: 0, 11: 1, 2: DH_BANK[11]}
+LATE_BANKS = ((4, 3, 6), (5, 6, 0), (4, 3, 1))
 
 
 def tile_moe_bdx_mlp_relu2_kernel(
@@ -81,12 +82,13 @@ def tile_moe_bdx_mlp_relu2_kernel(
         ident = keep.tile([P, P], F32, name="ident")
         w2_sc = keep.tile([P, 2 * E, H], U8, name="w2_sc", align_bytes=64)
         w1_sc = keep.tile([P, E, K], U8, name="w1_sc", align_bytes=64)
-        w2 = [keep.tile([P, 2, 2 * H], U8, name=f"w2_{e}", align_bytes=64) for e in range(E)]
+        w2 = {e: keep.tile([P, 2, 2 * H], U8, name=f"w2_{e}", align_bytes=64) for e in range(E) if e != 1}
+        w2[1] = shared.tile([P, 2, 2 * H], U8, name="w2_1", align_bytes=64, offset=W2_1_AT)
         w1 = [keep.tile([P, 2 * K], U8, name=f"w1_{e}", align_bytes=64) for e in range(E)]
         dy = {m: keep.tile([P, T], F32, name=f"dy_{m}") for m in range(N // P) if m not in DY_AT}
         dy.update({m: shared.tile([P, T], F32, name=f"dy_{m}", offset=at) for m, at in DY_AT.items()})
         gates = [keep.tile([P, CHUNK], F32, name=f"gate_{c}") for c in range(S // CHUNK)]
-        saved = [keep.tile([P, PACK, CHUNK], F32, name=f"saved_{c}") for c in range(S // CHUNK)]
+        saved = {b0: keep.tile([P, PACK, (b1 - b0) * P], F32, name=f"saved_{b0}") for b0, b1 in SAVED_PARTS}
         da_packed = [keep.tile([P, C, 2], F32, name=f"da_packed_{e}", align_bytes=64) for e in range(E)]
         da_codes = {e: keep.tile([P, C], U32, name=f"da_codes_{e}", align_bytes=64) for e in range(E) if e != 2}
         da_scales = [keep.tile([P, C], U8, name=f"da_scales_{e}", align_bytes=64) for e in range(E)]
@@ -103,7 +105,8 @@ def tile_moe_bdx_mlp_relu2_kernel(
             nc.sync.dma_start(out=gates[c][:], in_=gate[0:P, c * CHUNK : (c + 1) * CHUNK])
 
         def load_saved(c):
-            nc.sync.dma_start(out=saved[c][:], in_=a_rows[:, :, c * CHUNK : (c + 1) * CHUNK])
+            b0, b1 = SAVED_PARTS[c]
+            nc.sync.dma_start(out=saved[b0][:], in_=a_rows[:, :, b0 * P : b1 * P])
 
         def load_scales(plane, scales):
             rows = scales.bitcast(I32).rearrange("e s f i -> f (e s) i")
@@ -121,16 +124,17 @@ def tile_moe_bdx_mlp_relu2_kernel(
             nc.sync.dma_start(out=dy[m][:], in_=dy_rows[m // PACK, m % PACK])
             if m == 1:
                 load_gate(0)
-        load_gate(1)
         load_saved(0)
+        load_gate(1)
+        load_saved(1)
+        load_saved(2)
         load_scales(w2_sc, w2_scales)
         load_w2(0)
         load_w2(1)
-        load_saved(1)
+        load_saved(3)
+        load_gate(2)
         load_w2(2)
         load_w2(3)
-        load_gate(2)
-        load_saved(2)
         load_w2(4)
         load_w2(5)
         load_scales(w1_sc, w1_scales)
@@ -158,10 +162,12 @@ def tile_moe_bdx_mlp_relu2_kernel(
                     gates[chunk][:, col : col + n],
                     MULT,
                 )
-            if group in ROUNDED_AT:
-                at = ROUNDED_AT[group]
-                rounded[group] = shared.tile([P, n, PACK], BF16, name=f"g_bf16_{group}", align_bytes=64, offset=at)
-            else:
+            if group == 5:
+                both = shared.tile([P, CHUNK, PACK], BF16, name="g_bf16_last", align_bytes=64, offset=LAST_ROUNDED_AT)
+                rounded.update({5: both[:, :n, :], 6: both[:, n:, :], 7: both})
+            elif group == 3:
+                rounded[group] = shared.tile([P, n, PACK], BF16, name="g_bf16_3", align_bytes=64, offset=W2_1_AT)
+            elif group != 6:
                 rounded[group] = stage.tile([P, n, PACK], BF16, name="g_bf16", align_bytes=64)
             nc.scalar.copy(
                 out=rounded[group][:].rearrange("p (c i) j -> p c j i", i=4),
@@ -240,10 +246,11 @@ def tile_moe_bdx_mlp_relu2_kernel(
                 slope.update({b + h: both[:, h, :] for h in range(count)})
             elif b not in slope:
                 slope[b] = keep.tile([P, H], F32, name=f"slope_{b}")[:]
-            chunk, h = divmod(b, CHUNK_BLOCKS)
-            turned = psum.tile([P, PACK, P], F32, name=f"a_turned_{b}", offset=(4 + h) * BANK)
+            b0 = max(first for first, last in SAVED_PARTS if first <= b)
+            h = b - b0
+            turned = psum.tile([P, PACK, P], F32, name=f"a_turned_{b}", offset=SLOPE_BANK[b] * BANK)
             for t in range(PACK):
-                nc.tensor.transpose(turned[:, t, :], saved[chunk][:, t, h * P : (h + 1) * P], ident[:])
+                nc.tensor.transpose(turned[:, t, :], saved[b0][:, t, h * P : (h + 1) * P], ident[:])
             nc.scalar.activation(
                 out=by_pairs(slope[b]), in_=into_pairs(turned[:].rearrange("s t q -> s (t q)")), func=RELU, scale=2.0
             )
@@ -333,43 +340,49 @@ def tile_moe_bdx_mlp_relu2_kernel(
             nc.sync.dma_start(out=out[k * P : (k + 1) * P, t0:t1], in_=total[:])
 
         gather_plain(0, 0)
+        make_slope(0)
+        make_slope(1)
         gather(1)
         first_layer(0)
-        for b in range(CHUNK_BLOCKS):
+        for b in range(2, 7):
             make_slope(b)
         gather(2)
         first_layer(1)
+        make_slope(7)
         gather(3)
-        first_layer(2)
-        for b in range(CHUNK_BLOCKS, S // P):
+        quantise_g(2)
+        for b in range(8, 12):
             make_slope(b)
         gather(4)
+        for b in range(CHUNK_BLOCKS, 2 * CHUNK_BLOCKS):
+            product_dh(b, 0)
         first_layer(3)
         gather(5)
-        first_layer(4, freeing=(4, 5, 3))
+        first_layer(4)
         gather(6)
-        first_layer(5)
-        first_layer(6)
+        for b in (4, 5, 3):
+            make_da(b)
+        first_layer(7)
         turn_da(4, 5)
 
         turn_da(3)
-        for blocks in ((6, 7), (8, 9), (0, 1), (2,), (10, 11)):
+        for blocks in ((6, 7), (0, 1), (8, 9), (10,), (11,), (2,)):
             for b in blocks:
                 make_da(b)
             turn_da(*blocks)
 
         quantise_da(2)
         quantise_da(3)
-        product_dx((2, 3), 0, 7)
-        quantise_da(4)
-        product_dx((4,), 0, 2)
+        product_dx((2, 3), 0, 2)
         quantise_da(0)
-        quantise_da(1)
-        product_dx((0, 1), 0, 3)
+        quantise_da(4)
         quantise_da(5)
-        product_dx((5,), 0, 4, copy=nc.vector.tensor_copy)
+        product_dx((4, 5), 0, 3)
+        quantise_da(1)
+        product_dx((0,), 0, 4, copy=nc.vector.tensor_copy)
+        product_dx((1,), 0, 5, copy=nc.vector.tensor_copy)
         for k in range(1, K // P):
-            for m, experts in enumerate(((2, 3), (0, 1), (4, 5))):
+            for m, experts in enumerate(((2, 3), (4, 5), (0, 1))):
                 product_dx(experts, k, LATE_BANKS[k - 1][m])
 
         fetch_first(0, 0, T // 2)

@@ -48,7 +48,9 @@ W2_1_AT = 32 * KB
 DY_AT = {2: 38 * KB, 7: 52 * KB}
 DH_COPY_AT = 41 * KB
 LAST_SLOPES_AT = 49 * KB
-SLOPES_AT = {10: (1, LAST_SLOPES_AT)}
+FIRST_SLOPES_AT = 55 * KB
+SHORT_SHARE = 384
+SLOPES_AT = {0: (2, FIRST_SLOPES_AT), 10: (1, LAST_SLOPES_AT)}
 DA_AT = {
     0: (3, LAST_ROUNDED_AT + 3 * KB),
     3: (1, DY_AT[7]),
@@ -143,6 +145,7 @@ def tile_moe_bdx_mlp_relu2_kernel(
         nc.sync.dma_start(pos1_sb[:], pos1)
         nc.sync.dma_start(pos2_sb[:], pos2)
 
+        whole = {}
         rounded, g_codes, slope, dh, dh_copy, da, first = {}, {}, {}, {}, {}, {}, {}
 
         def by_pairs(columns):
@@ -244,6 +247,7 @@ def tile_moe_bdx_mlp_relu2_kernel(
                 count, at = SLOPES_AT[b]
                 both = shared.tile([P, count, H], F32, name=f"slope_{b}", align_bytes=64, offset=at)
                 slope.update({b + h: both[:, h, :] for h in range(count)})
+                whole["slope", b] = both[:].rearrange("s h i -> s (h i)")
             elif b not in slope:
                 slope[b] = keep.tile([P, H], F32, name=f"slope_{b}")[:]
             b0 = max(first for first, last in SAVED_PARTS if first <= b)
@@ -273,6 +277,7 @@ def tile_moe_bdx_mlp_relu2_kernel(
                 if not dh_copy:
                     copies = shared.tile([P, len(ON_GPSIMD), H], F32, name="dh_copy", align_bytes=64, offset=DH_COPY_AT)
                     dh_copy.update({h: copies[:, h, :] for h in ON_GPSIMD})
+                    whole["dh", 0] = copies[:].rearrange("s h i -> s (h i)")
                 nc.scalar.copy(out=by_pairs(dh_copy[b]), in_=into_pairs(dh[b][:]))
 
         def make_da(b):
@@ -280,10 +285,17 @@ def tile_moe_bdx_mlp_relu2_kernel(
                 count, at = DA_AT[b]
                 several = shared.tile([P, count * H], BF16, name=f"da_{b}", align_bytes=64, offset=at)
                 da.update({b + h: several[:, h * H : (h + 1) * H] for h in range(count)})
+                whole["da", b] = several[:]
             elif b not in da:
                 da[b] = keep.tile([P, H], BF16, name=f"da_{b}", align_bytes=64)[:]
-            if b in ON_GPSIMD:
-                nc.gpsimd.tensor_tensor(da[b], dh_copy[b], slope[b], MULT)
+            if b == 0:
+                both = slice(0, 2 * H)
+                nc.gpsimd.tensor_tensor(whole["da", 0][:, both], whole["dh", 0][:, both], whole["slope", 0], MULT)
+            elif b == 1:
+                return
+            elif b in ON_GPSIMD:
+                cols = slice(0, SHORT_SHARE if b == 3 else H)
+                nc.gpsimd.tensor_tensor(da[b][:, cols], dh_copy[b][:, cols], slope[b][:, cols], MULT)
             else:
                 nc.vector.tensor_tensor(by_pairs(da[b]), into_pairs(dh[b][:]), by_pairs(slope[b]), MULT)
 
@@ -363,6 +375,7 @@ def tile_moe_bdx_mlp_relu2_kernel(
         for b in (4, 5, 3):
             make_da(b)
         first_layer(7)
+        nc.vector.tensor_tensor(da[3][:, SHORT_SHARE:], dh_copy[3][:, SHORT_SHARE:], slope[3][:, SHORT_SHARE:], MULT)
         turn_da(4, 5)
 
         turn_da(3)

@@ -50,10 +50,12 @@ DH_COPY_AT = 41 * KB
 LAST_SLOPES_AT = 49 * KB
 FIRST_SLOPES_AT = 55 * KB
 SHORT_SHARE = 384
+PACKED = ((0, 2), (2, 1), (3, 1), (4, 2), (6, 2), (8, 2), (10, 2))
 SLOPES_AT = {0: (2, FIRST_SLOPES_AT), 10: (1, LAST_SLOPES_AT)}
 DA_AT = {
-    0: (3, LAST_ROUNDED_AT + 3 * KB),
-    3: (1, DY_AT[7]),
+    0: (2, LAST_ROUNDED_AT + 3 * KB),
+    2: (1, DY_AT[7]),
+    3: (1, LAST_ROUNDED_AT + 2 * KB),
     4: (2, EVEN_AT + 10 * KB),
     6: (2, LAST_ROUNDED_AT),
 }
@@ -61,7 +63,7 @@ DA_AT = {
 BANK = 2 * KB
 SLOPE_BANK = (7, 6, 4, 5, 7, 6, 4, 5, 0, 1, 2, 3)
 DH_BANK = (0, 1, 2, 3, 0, 1, 2, 3, 4, 5, 6, 7)
-TURN_BANK = {4: 0, 3: 1, 6: DH_BANK[6], 0: DH_BANK[8], 8: DH_BANK[7], 10: 0, 11: 1, 2: DH_BANK[11]}
+TURN_BANK = {4: 0, 2: 1, 6: DH_BANK[6], 0: DH_BANK[8], 8: DH_BANK[7], 10: 0, 11: 1, 3: DH_BANK[11]}
 LATE_BANKS = ((4, 3, 6), (5, 6, 0), (4, 3, 1))
 
 
@@ -91,14 +93,14 @@ def tile_moe_bdx_mlp_relu2_kernel(
         dy.update({m: shared.tile([P, T], F32, name=f"dy_{m}", offset=at) for m, at in DY_AT.items()})
         gates = [keep.tile([P, CHUNK], F32, name=f"gate_{c}") for c in range(S // CHUNK)]
         saved = {b0: keep.tile([P, PACK, (b1 - b0) * P], F32, name=f"saved_{b0}") for b0, b1 in SAVED_PARTS}
-        da_packed = [keep.tile([P, C, 2], F32, name=f"da_packed_{e}", align_bytes=64) for e in range(E)]
-        da_codes = {e: keep.tile([P, C], U32, name=f"da_codes_{e}", align_bytes=64) for e in range(E) if e != 2}
+        da_packed = {b0: keep.tile([P, n * P, 2], F32, name=f"da_packed_{b0}", align_bytes=64) for b0, n in PACKED}
+        da_codes = {e: keep.tile([P, C], U32, name=f"da_codes_{e}", align_bytes=64) for e in range(E) if e not in (1, 2)}
         da_scales = [keep.tile([P, C], U8, name=f"da_scales_{e}", align_bytes=64) for e in range(E)]
         dx = [keep.tile([P, S], F32, name=f"dx_{k}") for k in range(K // P)]
 
+        make_identity(nc, ident[:])
         nc.gpsimd.memset(w2_sc[:].rearrange("p g i -> p (g i)").bitcast(I32), 0)
         nc.gpsimd.memset(w1_sc[:].rearrange("p g i -> p (g i)").bitcast(I32), 0)
-        make_identity(nc, ident[:])
 
         dy_rows = dyT.rearrange("(s p j) t -> s j p t", s=2, j=PACK)
         a_rows = a.rearrange("(t p) c -> p t c", p=P)
@@ -121,9 +123,10 @@ def tile_moe_bdx_mlp_relu2_kernel(
         def load_w1(e):
             nc.sync.dma_start(out=w1[e][:].bitcast(I32), in_=w1_words[e, 0].bitcast(I32))
 
-        nc.sync.dma_start(offs_sb[:], offs)
         for m in range(N // P):
             nc.sync.dma_start(out=dy[m][:], in_=dy_rows[m // PACK, m % PACK])
+            if m == 0:
+                nc.sync.dma_start(offs_sb[:], offs)
             if m == 1:
                 load_gate(0)
         load_saved(0)
@@ -145,7 +148,7 @@ def tile_moe_bdx_mlp_relu2_kernel(
         nc.sync.dma_start(pos1_sb[:], pos1)
         nc.sync.dma_start(pos2_sb[:], pos2)
 
-        whole = {}
+        whole, total = {}, {}
         rounded, g_codes, slope, dh, dh_copy, da, first = {}, {}, {}, {}, {}, {}, {}
 
         def by_pairs(columns):
@@ -294,13 +297,14 @@ def tile_moe_bdx_mlp_relu2_kernel(
             elif b == 1:
                 return
             elif b in ON_GPSIMD:
-                cols = slice(0, SHORT_SHARE if b == 3 else H)
+                cols = slice(0, SHORT_SHARE if b == 2 else H)
                 nc.gpsimd.tensor_tensor(da[b][:, cols], dh_copy[b][:, cols], slope[b][:, cols], MULT)
             else:
                 nc.vector.tensor_tensor(by_pairs(da[b]), into_pairs(dh[b][:]), by_pairs(slope[b]), MULT)
 
         def turn_da(*blocks):
-            e, h = divmod(blocks[0], C // P)
+            b0 = blocks[0] if blocks[0] in da_packed else blocks[0] - 1
+            h = blocks[0] - b0
             bank = TURN_BANK[blocks[0]]
             turned = psum.tile([P, len(blocks), 2, P], F32, name=f"da_turned_{blocks[0]}", offset=bank * BANK)
             for m, b in enumerate(blocks):
@@ -308,29 +312,34 @@ def tile_moe_bdx_mlp_relu2_kernel(
                 for u in range(2):
                     nc.tensor.transpose(turned[:, m, u, :], words[:, u * P : (u + 1) * P], ident[:])
             nc.scalar.copy(
-                out=da_packed[e][:, h * P : (h + len(blocks)) * P, :].rearrange("p (m s) u -> p m s u", s=P),
+                out=da_packed[b0][:, h * P : (h + len(blocks)) * P, :].rearrange("p (m s) u -> p m s u", s=P),
                 in_=turned[:].rearrange("p m u s -> p m s u"),
             )
 
-        def quantise_da(e):
+        def quantise_da(b0):
+            e, h = divmod(b0, C // P)
             if e not in da_codes:
-                da_codes[e] = shared.tile([P, C], U32, name=f"da_codes_{e}", align_bytes=64, offset=LAST_SLOPES_AT)
-            flat = da_packed[e][:].rearrange("p c u -> p (c u)").bitcast(BF16)
-            nc.vector.quantize_mx(out=da_codes[e][:].bitcast(FP8X4), scales=da_scales[e][:], in_=flat)
+                at = LAST_SLOPES_AT + (e - 1) * KB
+                da_codes[e] = shared.tile([P, C], U32, name=f"da_codes_{e}", align_bytes=64, offset=at)
+            cols = slice(h * P, h * P + da_packed[b0].shape[1])
+            flat = da_packed[b0][:].rearrange("p c u -> p (c u)").bitcast(BF16)
+            nc.vector.quantize_mx(out=da_codes[e][:, cols].bitcast(FP8X4), scales=da_scales[e][:, cols], in_=flat)
 
-        def product_dx(experts, k, bank, copy=nc.scalar.copy):
-            acc = psum.tile([P, len(experts), C], F32, name=f"dx_{experts[0]}_{k}", offset=bank * BANK)
-            for h, e in enumerate(experts):
+        def product_dx(b0, b1, k, bank, copy=nc.scalar.copy):
+            c0, c1 = b0 * P, b1 * P
+            acc = psum.tile([P, c1 - c0], F32, name=f"dx_{b0}_{k}", offset=bank * BANK)
+            for e in range(c0 // C, (c1 - 1) // C + 1):
+                lo, hi = max(c0, e * C), min(c1, (e + 1) * C)
                 nc.tensor.matmul_mx(
-                    out=acc[:, h, :],
+                    out=acc[:, lo - c0 : hi - c0],
                     lhsT=w1[e][:, 2 * k * P : 2 * (k + 1) * P].bitcast(FP4X4),
                     lhsT_scale=w1_sc[:, e, k * P : (k + 1) * P],
-                    rhs=da_codes[e][:].bitcast(FP8X4),
-                    rhs_scale=da_scales[e][:],
+                    rhs=da_codes[e][:, lo - e * C : hi - e * C].bitcast(FP8X4),
+                    rhs_scale=da_scales[e][:, lo - e * C : hi - e * C],
                     start=True,
                     stop=True,
                 )
-            copy(dx[k][:, experts[0] * C : (experts[-1] + 1) * C], acc[:].rearrange("p h c -> p (h c)"))
+            copy(dx[k][:, c0:c1], acc[:])
 
         def first_layer(group, freeing=()):
             quantise_g(group)
@@ -346,10 +355,11 @@ def tile_moe_bdx_mlp_relu2_kernel(
             nc.vector.tensor_copy(first[k][:, t0:t1], dx[k][:].indirect(pos1_sb[:, t0 // 16 : t1 // 16]))
 
         def add_second(k, t0=0, t1=T):
-            total = stage.tile([P, t1 - t0], F32, name="total")
+            if t0 == 0:
+                total[k] = stage.tile([P, T], F32, name="total")
             second = dx[k][:].indirect(pos2_sb[:, t0 // 16 : t1 // 16])
-            nc.vector.tensor_tensor(total[:], second, first[k][:, t0:t1], ADD)
-            nc.sync.dma_start(out=out[k * P : (k + 1) * P, t0:t1], in_=total[:])
+            nc.vector.tensor_tensor(total[k][:, t0:t1], second, first[k][:, t0:t1], ADD)
+            nc.sync.dma_start(out=out[k * P : (k + 1) * P, t0:t1], in_=total[k][:, t0:t1])
 
         gather_plain(0, 0)
         make_slope(0)
@@ -372,31 +382,33 @@ def tile_moe_bdx_mlp_relu2_kernel(
         gather(5)
         first_layer(4)
         gather(6)
-        for b in (4, 5, 3):
+        for b in (4, 5, 2):
             make_da(b)
         first_layer(7)
-        nc.vector.tensor_tensor(da[3][:, SHORT_SHARE:], dh_copy[3][:, SHORT_SHARE:], slope[3][:, SHORT_SHARE:], MULT)
+        nc.vector.tensor_tensor(da[2][:, SHORT_SHARE:], dh_copy[2][:, SHORT_SHARE:], slope[2][:, SHORT_SHARE:], MULT)
         turn_da(4, 5)
 
-        turn_da(3)
-        for blocks in ((6, 7), (0, 1), (8, 9), (10,), (11,), (2,)):
+        turn_da(2)
+        for blocks in ((6, 7), (0, 1), (8, 9), (10,), (11,), (3,)):
             for b in blocks:
                 make_da(b)
             turn_da(*blocks)
 
-        quantise_da(2)
-        quantise_da(3)
-        product_dx((2, 3), 0, 2)
-        quantise_da(0)
         quantise_da(4)
-        quantise_da(5)
-        product_dx((4, 5), 0, 3)
-        quantise_da(1)
-        product_dx((0,), 0, 4, copy=nc.vector.tensor_copy)
-        product_dx((1,), 0, 5, copy=nc.vector.tensor_copy)
+        quantise_da(6)
+        product_dx(4, 8, 0, 2)
+        quantise_da(0)
+        quantise_da(2)
+        quantise_da(8)
+        product_dx(8, 10, 0, 3)
+        quantise_da(10)
+        product_dx(10, 12, 0, 6)
+        quantise_da(3)
+        product_dx(0, 3, 0, 4, copy=nc.vector.tensor_copy)
+        product_dx(3, 4, 0, 5, copy=nc.vector.tensor_copy)
         for k in range(1, K // P):
-            for m, experts in enumerate(((2, 3), (4, 5), (0, 1))):
-                product_dx(experts, k, LATE_BANKS[k - 1][m])
+            for m, b0 in enumerate((4, 8, 0)):
+                product_dx(b0, b0 + CHUNK_BLOCKS, k, LATE_BANKS[k - 1][m])
 
         fetch_first(0, 0, T // 2)
         fetch_first(0, T // 2, T)

@@ -1,7 +1,6 @@
 from contextlib import ExitStack
 
 import concourse.mybir as mybir
-from concourse.masks import make_identity
 
 N, T, E, C, H, K = 1024, 768, 6, 256, 512, 512
 S = E * C
@@ -19,52 +18,38 @@ FP8X4 = mybir.dt.float8_e4m3fn_x4
 FP4X4 = mybir.dt.float4_e2m1fn_x4
 MULT = mybir.AluOpType.mult
 ADD = mybir.AluOpType.add
-RELU = mybir.ActivationFunctionType.Relu
+MAX = mybir.AluOpType.max
+MIN = mybir.AluOpType.min
+FLOAT_MAX = (2.0 - 2.0**-23) * 2.0**127
 COPY = mybir.ActivationFunctionType.Copy
+RELU = mybir.ActivationFunctionType.Relu
 
 CHUNK = 512
-CHUNK_BLOCKS = CHUNK // P
-GROUPS = (
-    (0, CHUNK, 0),
-    (0, CHUNK, 1),
-    (CHUNK, CHUNK, 0),
-    (CHUNK, CHUNK, 1),
-    (2 * CHUNK, CHUNK, 0),
-    (2 * CHUNK, CHUNK - P, 1),
-    (S - P, P, 1),
-    (2 * CHUNK, CHUNK, 1),
-)
-ON_GPSIMD = (0, 1, 2, 3)
+BLOCKS = S // P
+KB = 1024
+BANK = 2 * KB
+GROUPS = {
+    "c0s0": (0, 512, 0),
+    "c0s1": (0, 512, 1),
+    "c1s0": (512, 512, 0),
+    "c1s1": (512, 512, 1),
+    "e4s0": (1024, 256, 0),
+    "e4s1": (1024, 256, 1),
+    "e5s0": (1280, 256, 0),
+    "e5s1": (1280, 256, 1),
+}
 LAST_STORES = (448, 192, 128)
 
-SAVED_PARTS = ((0, 2), (2, 4), (4, 8), (8, 12))
-KB = 1024
-EDGE = 64
-EVEN_AT, ODD_AT = 8 * KB, 24 * KB
-MIDDLE_SLOPES_AT = EVEN_AT - 4 * KB
-GROUP_AT = {0: EVEN_AT, 1: ODD_AT, 2: EVEN_AT, 3: ODD_AT, 4: EVEN_AT + 8 * KB - EDGE, 5: ODD_AT, 6: ODD_AT - 2 * KB}
-LAST_ROUNDED_AT = 2 * KB
-W2_1_AT = 32 * KB
-DY_AT = {2: 38 * KB, 7: 52 * KB}
-DH_COPY_AT = 41 * KB
-LAST_SLOPES_AT = 49 * KB
-FIRST_SLOPES_AT = 55 * KB
-SHORT_SHARE = 384
-PACKED = ((0, 2), (2, 1), (3, 1), (4, 2), (6, 2), (8, 2), (10, 2))
-SLOPES_AT = {0: (2, FIRST_SLOPES_AT), 10: (1, LAST_SLOPES_AT)}
-DA_AT = {
-    0: (2, LAST_ROUNDED_AT + 3 * KB),
-    2: (1, DY_AT[7]),
-    3: (1, LAST_ROUNDED_AT + 2 * KB),
-    4: (2, EVEN_AT + 10 * KB),
-    6: (2, LAST_ROUNDED_AT),
-}
-
-BANK = 2 * KB
-SLOPE_BANK = (7, 6, 4, 5, 7, 6, 4, 5, 0, 1, 2, 3)
-DH_BANK = (0, 1, 2, 3, 0, 1, 2, 3, 4, 5, 6, 7)
-TURN_BANK = {4: 0, 2: 1, 6: DH_BANK[6], 0: DH_BANK[8], 8: DH_BANK[7], 10: 0, 11: 1, 3: DH_BANK[11]}
-LATE_BANKS = ((4, 3, 6), (5, 6, 0), (4, 3, 1))
+PICKED_AT = {"c0s0": 24, "c0s1": 32, "c1s1": 40, "e4s1": 48, "c1s0": 52, "e4s0": 60, "e5s0": 24, "e5s1": 32}
+DH_AT = (24, 26, 28, 30, 32, 34, 36, 38, 52, 54, 56, 58)
+FIRST_AT, TOTAL_AT = 40, 52
+SAVED_AT = 64
+ROUNDED_AT = {"c0s0": 90, "c0s1": 100, "e4s0": 110, "c1s0": 88, "c1s1": 110, "e4s1": 92, "e5s0": 88, "e5s1": 110}
+DA_AT = (92, 112, 114, 116, 126, 128)
+SLOPE_AT = (118, 94, 102)
+SCALES_AT = {"c0s0": 0, "c0s1": 1, "e4s0": 2, "c1s0": 16, "c1s1": 17, "e4s1": 18, "e5s0": 19, "e5s1": 20}
+DH_BANK = (3, 4, 5, 6, 3, 4, 5, 6, 3, 4, 2, 3)
+TURN_BANK = (7, 0, 1, 7, 0, 1, 7, 0, 1, 7, 0, 1)
 
 
 def tile_moe_bdx_mlp_relu2_kernel(
@@ -74,9 +59,7 @@ def tile_moe_bdx_mlp_relu2_kernel(
     with ExitStack() as ctx:
         lists = ctx.enter_context(tc.tile_pool(name="lists", bufs=1))
         keep = ctx.enter_context(tc.tile_pool(name="keep", bufs=1))
-        stage = ctx.enter_context(tc.tile_pool(name="stage", bufs=3))
         shared = ctx.enter_context(tc.tile_pool(name="shared", bufs=1))
-        pair = ctx.enter_context(tc.tile_pool(name="pair", bufs=2))
         psum = ctx.enter_context(tc.psum_pool(name="psum", bufs=1))
 
         offs_sb = lists.tile([P, S // 16], U16, name="offs_sb")
@@ -84,341 +67,245 @@ def tile_moe_bdx_mlp_relu2_kernel(
         pos2_sb = lists.tile([P, T // 16], U16, name="pos2_sb")
 
         ident = keep.tile([P, P], F32, name="ident")
+        gate_col = keep.tile([P, S // CHUNK, PACK], F32, name="gate_col")
         w2_sc = keep.tile([P, 2 * E, H], U8, name="w2_sc", align_bytes=64)
         w1_sc = keep.tile([P, E, K], U8, name="w1_sc", align_bytes=64)
-        w2 = {e: keep.tile([P, 2, 2 * H], U8, name=f"w2_{e}", align_bytes=64) for e in range(E) if e != 1}
-        w2[1] = shared.tile([P, 2, 2 * H], U8, name="w2_1", align_bytes=64, offset=W2_1_AT)
-        w1 = [keep.tile([P, 2 * K], U8, name=f"w1_{e}", align_bytes=64) for e in range(E)]
-        dy = {m: keep.tile([P, T], F32, name=f"dy_{m}") for m in range(N // P) if m not in DY_AT}
-        dy.update({m: shared.tile([P, T], F32, name=f"dy_{m}", offset=at) for m, at in DY_AT.items()})
-        gates = [keep.tile([P, CHUNK], F32, name=f"gate_{c}") for c in range(S // CHUNK)]
-        saved = {b0: keep.tile([P, PACK, (b1 - b0) * P], F32, name=f"saved_{b0}") for b0, b1 in SAVED_PARTS}
-        da_packed = {b0: keep.tile([P, n * P, 2], F32, name=f"da_packed_{b0}", align_bytes=64) for b0, n in PACKED}
-        da_codes = {e: keep.tile([P, C], U32, name=f"da_codes_{e}", align_bytes=64) for e in range(E) if e not in (1, 2)}
-        da_scales = [keep.tile([P, C], U8, name=f"da_scales_{e}", align_bytes=64) for e in range(E)]
-        dx = [keep.tile([P, S], F32, name=f"dx_{k}") for k in range(K // P)]
+        w2 = [keep.tile([P, 2, 2 * H], U8, name=f"w2_{e}", align_bytes=64) for e in range(E)]
+        w1 = keep.tile([P, E, 2 * K], U8, name="w1", align_bytes=64)
+        dy = [shared.tile([P, T], F32, name=f"dy_{m}", align_bytes=64, offset=(m % 4 * 6 + m // 4 * 3) * KB) for m in range(N // P)]
+        saved, slope = [], []
+        for c in range(S // CHUNK):
+            at = (SAVED_AT + c * 8) * KB
+            saved.append(shared.tile([P, PACK, CHUNK], F32, name=f"saved_{c}", align_bytes=64, offset=at))
+            slope.append(shared.tile([P, PACK, CHUNK], F32, name=f"slope_{c}", align_bytes=64, offset=SLOPE_AT[c] * KB))
 
-        make_identity(nc, ident[:])
+        apart = keep.tile([P, P], F32, name="apart")
+        apart_squared = shared.tile([P, 7 * KB], F32, name="apart_squared", align_bytes=64, offset=24 * KB)[:, :P]
+        nc.gpsimd.iota(apart[:], pattern=[[1, P]], base=0, channel_multiplier=-1, allow_small_or_imprecise_dtypes=True)
+        nc.gpsimd.tensor_tensor(apart_squared, apart[:], apart[:], MULT)
+        nc.scalar.activation(ident[:], apart_squared, RELU, bias=1.0, scale=-1.0)
         nc.gpsimd.memset(w2_sc[:].rearrange("p g i -> p (g i)").bitcast(I32), 0)
         nc.gpsimd.memset(w1_sc[:].rearrange("p g i -> p (g i)").bitcast(I32), 0)
 
         dy_rows = dyT.rearrange("(s p j) t -> s j p t", s=2, j=PACK)
-        a_rows = a.rearrange("(t p) c -> p t c", p=P)
-
-        def load_gate(c):
-            nc.sync.dma_start(out=gates[c][:], in_=gate[0:P, c * CHUNK : (c + 1) * CHUNK])
-
-        def load_saved(c):
-            b0, b1 = SAVED_PARTS[c]
-            nc.sync.dma_start(out=saved[b0][:], in_=a_rows[:, :, b0 * P : b1 * P])
+        a_rows = a.rearrange("(p t) c -> p t c", t=PACK)
 
         def load_scales(plane, scales):
             rows = scales.bitcast(I32).rearrange("e s f i -> f (e s) i")
             for q in range(4):
                 nc.sync.dma_start(out=plane[32 * q : 32 * q + 4].bitcast(I32), in_=rows[4 * q : 4 * q + 4])
 
-        def load_w2(e):
-            nc.sync.dma_start(out=w2[e][:].bitcast(I32), in_=w2_words[e].rearrange("s p b -> p s b").bitcast(I32))
-
-        def load_w1(e):
-            nc.sync.dma_start(out=w1[e][:].bitcast(I32), in_=w1_words[e, 0].bitcast(I32))
-
+        nc.sync.dma_start(offs_sb[:], offs)
         for m in range(N // P):
             nc.sync.dma_start(out=dy[m][:], in_=dy_rows[m // PACK, m % PACK])
             if m == 0:
-                nc.sync.dma_start(offs_sb[:], offs)
-            if m == 1:
-                load_gate(0)
-        load_saved(0)
-        load_gate(1)
-        load_saved(1)
-        load_saved(2)
+                nc.sync.dma_start(out=gate_col[:], in_=gate[0].rearrange("(q n b) -> n q b", n=P, b=PACK))
+        nc.sync.dma_start(out=saved[0][:], in_=a_rows[:, :, :CHUNK])
         load_scales(w2_sc, w2_scales)
-        load_w2(0)
-        load_w2(1)
-        load_saved(3)
-        load_gate(2)
-        load_w2(2)
-        load_w2(3)
-        load_w2(4)
-        load_w2(5)
-        load_scales(w1_sc, w1_scales)
         for e in range(E):
-            load_w1(e)
+            nc.sync.dma_start(out=w2[e][:].bitcast(I32), in_=w2_words[e].rearrange("s p b -> p s b").bitcast(I32))
+            if e == 1:
+                nc.sync.dma_start(out=saved[1][:], in_=a_rows[:, :, CHUNK : 2 * CHUNK])
+                nc.sync.dma_start(out=saved[2][:], in_=a_rows[:, :, 2 * CHUNK :])
+        load_scales(w1_sc, w1_scales)
+        nc.sync.dma_start(out=w1[:].bitcast(I32), in_=w1_words.rearrange("e s p b -> p (e s) b").bitcast(I32))
         nc.sync.dma_start(pos1_sb[:], pos1)
         nc.sync.dma_start(pos2_sb[:], pos2)
 
-        whole, total = {}, {}
-        rounded, g_codes, slope, dh, dh_copy, da, first = {}, {}, {}, {}, {}, {}, {}
+        spread = [psum.tile([P, PACK, P], F32, name=f"spread_{q}", offset=q * BANK) for q in range(S // CHUNK)]
+        for q in range(S // CHUNK):
+            for b in range(PACK):
+                nc.tensor.transpose(spread[q][:, b, :], gate_col[:, q, b : b + 1].to_broadcast([P, P]), ident[:])
 
-        def by_pairs(columns):
-            return columns.rearrange("s (u p e) -> s u p e", u=2, e=2)
+        picked, rounded, g_codes, dh_sb, turned, da, da_codes = {}, {}, {}, {}, {}, {}, {}
 
-        def into_pairs(columns):
-            return columns.rearrange("s (p u e) -> s u p e", u=2, e=2)
-
-        def gather(group):
+        def gather(group, j, on_vector):
             c0, n, s = GROUPS[group]
-            g = shared.tile([P, PACK, n], F32, name=f"g_{group}", align_bytes=64, offset=GROUP_AT[group])
-            chunk, col = divmod(c0, CHUNK)
+            if j == 0:
+                at = PICKED_AT[group] * KB
+                picked[group] = shared.tile([P, PACK, n], F32, name=f"picked_{group}", align_bytes=64, offset=at)
+            window = dy[PACK * s + j][:].indirect(offs_sb[:, c0 // 16 : (c0 + n) // 16])
+            if on_vector:
+                nc.vector.tensor_copy(picked[group][:, j, :], window)
+            else:
+                nc.scalar.activation(picked[group][:, j, :], window, COPY)
+
+        def gather_on_scalar(group):
             for j in range(PACK):
-                nc.vector.tensor_tensor(
-                    g[:, j, :],
-                    dy[PACK * s + j][:].indirect(offs_sb[:, c0 // 16 : (c0 + n) // 16]),
-                    gates[chunk][:, col : col + n],
-                    MULT,
-                )
-            if group == 5:
-                both = shared.tile([P, CHUNK, PACK], BF16, name="g_bf16_last", align_bytes=64, offset=LAST_ROUNDED_AT)
-                rounded.update({5: both[:, :n, :], 6: both[:, n:, :], 7: both})
-            elif group == 3:
-                rounded[group] = shared.tile([P, n, PACK], BF16, name="g_bf16_3", align_bytes=64, offset=W2_1_AT)
-            elif group != 6:
-                rounded[group] = stage.tile([P, n, PACK], BF16, name="g_bf16", align_bytes=64)
-            nc.scalar.copy(
-                out=rounded[group][:].rearrange("p (c i) j -> p c j i", i=4),
-                in_=g[:].rearrange("p j (c i) -> p c j i", i=4),
-            )
+                gather(group, j, False)
 
-        def gather_plain(group, first_bank):
+        def apply_gate(group):
             c0, n, s = GROUPS[group]
-            g = shared.tile([P, PACK, n], F32, name=f"g_{group}", align_bytes=64, offset=GROUP_AT[group])
-            chunk, col = divmod(c0, CHUNK)
-            blocks = n // P
-            gate_turned = psum.tile([P, blocks, P], F32, name=f"gate_turned_{group}", offset=(first_bank + 6) * BANK)
-            for h in range(blocks):
-                nc.tensor.transpose(gate_turned[:, h, :], gates[chunk][:, col + h * P : col + (h + 1) * P], ident[:])
-            gate_col = keep.tile([P, blocks], F32, name=f"gate_col_{group}")
-            nc.scalar.copy(out=gate_col[:], in_=gate_turned[:, :, 0])
-            pairs = keep.tile([P, blocks, 2, P, 2], BF16, name=f"g_pairs_{group}", align_bytes=64)
-            for u in range(2):
-                for e in range(2):
-                    nc.vector.tensor_copy(
-                        g[:, 2 * u + e, :], dy[PACK * s + 2 * u + e][:].indirect(offs_sb[:, c0 // 16 : (c0 + n) // 16])
-                    )
-                for h0 in range(0, blocks, 2):
-                    bank = first_bank + 2 * u + h0 // 2
-                    turned = psum.tile([P, 2, 2, P], F32, name=f"g_turned_{group}_{u}_{h0}", offset=bank * BANK)
-                    for h in range(h0, h0 + 2):
-                        for e in range(2):
-                            nc.tensor.transpose(turned[:, h - h0, e, :], g[:, 2 * u + e, h * P : (h + 1) * P], ident[:])
-                    for h in range(h0, h0 + 2):
-                        nc.scalar.activation(
-                            out=pairs[:, h, u, :, :],
-                            in_=turned[:, h - h0, :, :].rearrange("s e p -> s p e"),
-                            func=COPY,
-                            scale=gate_col[:, h : h + 1],
-                        )
-            rounded[group] = stage.tile([P, n, PACK], BF16, name="g_bf16", align_bytes=64)
-            words = rounded[group][:].rearrange("p c j -> p (c j)").bitcast(F32).rearrange("p (c u) -> p c u", u=2)
-            for h0 in range(0, blocks, 2):
-                bank = first_bank + 4 + h0 // 2
-                back = psum.tile([P, 2, 2, P], F32, name=f"g_back_{group}_{h0}", offset=bank * BANK)
-                for h in range(h0, h0 + 2):
-                    for u in range(2):
-                        pair_words = pairs[:, h, u, :, :].rearrange("s p e -> s (p e)").bitcast(F32)
-                        nc.tensor.transpose(back[:, h - h0, u, :], pair_words, ident[:])
-                nc.scalar.copy(
-                    out=words[:, h0 * P : (h0 + 2) * P, :].rearrange("p (m s) u -> p m s u", s=P),
-                    in_=back[:].rearrange("p m u s -> p m s u"),
-                )
+            q, col = divmod(c0, CHUNK)
+            rounded[group] = shared.tile(
+                [P, n, PACK], BF16, name=f"rounded_{group}", align_bytes=64, offset=ROUNDED_AT[group] * KB
+            )
+            factor = spread[q][:, :, col // 4 : (col + n) // 4].rearrange("p i c -> p c i")
+            nc.vector.tensor_tensor(
+                rounded[group][:].rearrange("p (c i) j -> p c j i", i=4),
+                picked[group][:].rearrange("p j (c i) -> p c j i", i=4),
+                factor.unsqueeze(2).to_broadcast([P, n // 4, PACK, 4]),
+                MULT,
+            )
 
         def quantise_g(group):
             c0, n, s = GROUPS[group]
-            if group == 3:
-                codes = shared.tile([P, n], U32, name="g_codes_3", align_bytes=64, offset=DY_AT[2])
-            else:
-                codes = stage.tile([P, n], U32, name="g_codes", align_bytes=64)
-            scales = stage.tile([P, n], U8, name="g_scales", align_bytes=64)
-            flat = rounded[group][:].rearrange("p c j -> p (c j)")
-            done = 0
-            for width in (512, 256, 128):
-                if n - done >= width:
-                    cols = slice(done, done + width)
-                    nc.vector.quantize_mx(
-                        out=codes[:, cols].bitcast(FP8X4),
-                        scales=scales[:, cols],
-                        in_=flat[:, PACK * done : PACK * (done + width)],
-                    )
-                    done += width
+            codes = keep.tile([P, n], U32, name=f"g_codes_{group}", align_bytes=64)
+            at = (SAVED_AT + SCALES_AT[group]) * KB
+            scales = shared.tile([P, n], U8, name=f"g_scales_{group}", align_bytes=64, offset=at)
+            nc.vector.quantize_mx(
+                out=codes[:].bitcast(FP8X4), scales=scales[:], in_=rounded[group][:].rearrange("p c j -> p (c j)")
+            )
             for h in range(n // P):
                 cols = slice(h * P, (h + 1) * P)
                 g_codes[c0 // P + h, s] = (codes[:, cols], scales[:, cols])
 
-        def make_slope(b):
-            if b in SLOPES_AT:
-                count, at = SLOPES_AT[b]
-                both = shared.tile([P, count, H], F32, name=f"slope_{b}", align_bytes=64, offset=at)
-                slope.update({b + h: both[:, h, :] for h in range(count)})
-                whole["slope", b] = both[:].rearrange("s h i -> s (h i)")
-            elif b not in slope:
-                slope[b] = keep.tile([P, H], F32, name=f"slope_{b}")[:]
-            b0 = max(first for first, last in SAVED_PARTS if first <= b)
-            h = b - b0
-            turned = psum.tile([P, PACK, P], F32, name=f"a_turned_{b}", offset=SLOPE_BANK[b] * BANK)
-            for t in range(PACK):
-                nc.tensor.transpose(turned[:, t, :], saved[b0][:, t, h * P : (h + 1) * P], ident[:])
-            nc.scalar.activation(
-                out=by_pairs(slope[b]), in_=into_pairs(turned[:].rearrange("s t q -> s (t q)")), func=RELU, scale=2.0
-            )
-
-        def product_dh(b, s):
+        def product_dh(b):
             e = b * P // C
-            if s == 0:
-                dh[b] = psum.tile([P, H], F32, name=f"dh_{b}", offset=DH_BANK[b] * BANK)
-            codes, scales = g_codes[b, s]
-            nc.tensor.matmul_mx(
-                out=dh[b][:],
-                lhsT=codes.bitcast(FP8X4),
-                lhsT_scale=scales,
-                rhs=w2[e][:, s, :].bitcast(FP4X4),
-                rhs_scale=w2_sc[:, 2 * e + s, :],
-                start=(s == 0),
-                stop=(s == 1),
-            )
-            if s == 1 and b in ON_GPSIMD:
-                if not dh_copy:
-                    copies = shared.tile([P, len(ON_GPSIMD), H], F32, name="dh_copy", align_bytes=64, offset=DH_COPY_AT)
-                    dh_copy.update({h: copies[:, h, :] for h in ON_GPSIMD})
-                    whole["dh", 0] = copies[:].rearrange("s h i -> s (h i)")
-                nc.scalar.copy(out=by_pairs(dh_copy[b]), in_=into_pairs(dh[b][:]))
+            dh = psum.tile([P, H], F32, name=f"dh_{b}", offset=DH_BANK[b] * BANK)
+            for s in range(2):
+                codes, scales = g_codes[b, s]
+                nc.tensor.matmul_mx(
+                    out=dh[:],
+                    lhsT=codes.bitcast(FP8X4),
+                    lhsT_scale=scales,
+                    rhs=w2[e][:, s, :].bitcast(FP4X4),
+                    rhs_scale=w2_sc[:, 2 * e + s, :],
+                    start=(s == 0),
+                    stop=(s == 1),
+                )
+            dh_sb[b] = shared.tile([P, PACK, P], F32, name=f"dh_sb_{b}", align_bytes=64, offset=DH_AT[b] * KB)
+            nc.scalar.activation(dh_sb[b][:], dh[:].rearrange("s (m t) -> s t m", t=PACK), COPY, scale=2.0)
+
+        def turn_dh(b):
+            turned[b] = psum.tile([P, PACK, P], F32, name=f"turned_{b}", offset=TURN_BANK[b] * BANK)
+            for t in range(PACK):
+                nc.tensor.transpose(turned[b][:, t, :], dh_sb[b][:, t, :], ident[:])
 
         def make_da(b):
-            if b in DA_AT:
-                count, at = DA_AT[b]
-                several = shared.tile([P, count * H], BF16, name=f"da_{b}", align_bytes=64, offset=at)
-                da.update({b + h: several[:, h * H : (h + 1) * H] for h in range(count)})
-                whole["da", b] = several[:]
-            elif b not in da:
-                da[b] = keep.tile([P, H], BF16, name=f"da_{b}", align_bytes=64)[:]
-            if b == 0:
-                both = slice(0, 2 * H)
-                nc.gpsimd.tensor_tensor(whole["da", 0][:, both], whole["dh", 0][:, both], whole["slope", 0], MULT)
-            elif b == 1:
-                return
-            elif b in ON_GPSIMD:
-                cols = slice(0, SHORT_SHARE if b == 2 else H)
-                nc.gpsimd.tensor_tensor(da[b][:, cols], dh_copy[b][:, cols], slope[b][:, cols], MULT)
-            else:
-                nc.vector.tensor_tensor(by_pairs(da[b]), into_pairs(dh[b][:]), by_pairs(slope[b]), MULT)
-
-        def turn_da(*blocks):
-            b0 = blocks[0] if blocks[0] in da_packed else blocks[0] - 1
-            h = blocks[0] - b0
-            bank = TURN_BANK[blocks[0]]
-            turned = psum.tile([P, len(blocks), 2, P], F32, name=f"da_turned_{blocks[0]}", offset=bank * BANK)
-            for m, b in enumerate(blocks):
-                words = da[b].bitcast(F32)
-                for u in range(2):
-                    nc.tensor.transpose(turned[:, m, u, :], words[:, u * P : (u + 1) * P], ident[:])
-            nc.scalar.copy(
-                out=da_packed[b0][:, h * P : (h + len(blocks)) * P, :].rearrange("p (m s) u -> p m s u", s=P),
-                in_=turned[:].rearrange("p m u s -> p m s u"),
+            e, h = divmod(b, C // P)
+            if h == 0:
+                da[e] = shared.tile([P, C, PACK], BF16, name=f"da_{e}", align_bytes=64, offset=DA_AT[e] * KB)
+            nc.vector.tensor_tensor(
+                da[e][:, h * P : (h + 1) * P, :].rearrange("p (c i) t -> p c t i", i=4),
+                turned[b][:].rearrange("p t (c i) -> p c t i", i=4),
+                slope[b // 4][:, :, b % 4 * P : (b % 4 + 1) * P].rearrange("p t (c i) -> p c t i", i=4),
+                MULT,
             )
 
-        def quantise_da(b0):
-            e, h = divmod(b0, C // P)
-            if e not in da_codes:
-                at = LAST_SLOPES_AT + (e - 1) * KB
-                da_codes[e] = shared.tile([P, C], U32, name=f"da_codes_{e}", align_bytes=64, offset=at)
-            cols = slice(h * P, h * P + da_packed[b0].shape[1])
-            flat = da_packed[b0][:].rearrange("p c u -> p (c u)").bitcast(BF16)
-            nc.vector.quantize_mx(out=da_codes[e][:, cols].bitcast(FP8X4), scales=da_scales[e][:, cols], in_=flat)
+        def quantise_da(e):
+            codes = keep.tile([P, C], U32, name=f"da_codes_{e}", align_bytes=64)
+            scales = keep.tile([P, C], U8, name=f"da_scales_{e}", align_bytes=64)
+            nc.vector.quantize_mx(
+                out=codes[:].bitcast(FP8X4), scales=scales[:], in_=da[e][:].rearrange("p c t -> p (c t)")
+            )
+            da_codes[e] = (codes, scales)
 
-        def product_dx(b0, b1, k, bank, copy=nc.scalar.copy):
-            c0, c1 = b0 * P, b1 * P
-            acc = psum.tile([P, c1 - c0], F32, name=f"dx_{b0}_{k}", offset=bank * BANK)
-            for e in range(c0 // C, (c1 - 1) // C + 1):
-                lo, hi = max(c0, e * C), min(c1, (e + 1) * C)
+        dx = {}
+
+        def product_dx(e0, e1, k, bank, copy):
+            if k not in dx:
+                dx[k] = shared.tile([P, S], F32, name=f"dx_{k}", align_bytes=64, offset=k * 6 * KB)
+            acc = psum.tile([P, (e1 - e0) * C], F32, name=f"dx_{e0}_{k}", offset=bank * BANK)
+            for e in range(e0, e1):
+                codes, scales = da_codes[e]
                 nc.tensor.matmul_mx(
-                    out=acc[:, lo - c0 : hi - c0],
-                    lhsT=w1[e][:, 2 * k * P : 2 * (k + 1) * P].bitcast(FP4X4),
+                    out=acc[:, (e - e0) * C : (e - e0 + 1) * C],
+                    lhsT=w1[:, e, 2 * k * P : 2 * (k + 1) * P].bitcast(FP4X4),
                     lhsT_scale=w1_sc[:, e, k * P : (k + 1) * P],
-                    rhs=da_codes[e][:, lo - e * C : hi - e * C].bitcast(FP8X4),
-                    rhs_scale=da_scales[e][:, lo - e * C : hi - e * C],
+                    rhs=codes[:].bitcast(FP8X4),
+                    rhs_scale=scales[:],
                     start=True,
                     stop=True,
                 )
-            copy(dx[k][:, c0:c1], acc[:])
+            copy(dx[k][:, e0 * C : e1 * C], acc[:])
 
-        def first_layer(group, freeing=()):
-            quantise_g(group)
-            c0, n, s = GROUPS[group]
-            for b in freeing:
-                make_da(b)
-            for b in range(c0 // P, (c0 + n) // P):
-                product_dh(b, s)
+        first, total = {}, {}
 
         def fetch_first(k, t0=0, t1=T):
             if t0 == 0:
-                first[k] = pair.tile([P, T], F32, name="first")
-            nc.vector.tensor_copy(first[k][:, t0:t1], dx[k][:].indirect(pos1_sb[:, t0 // 16 : t1 // 16]))
+                first[k] = shared.tile([P, T], F32, name=f"first_{k}", align_bytes=64, offset=(FIRST_AT + 3 * k) * KB)
+            nc.scalar.activation(first[k][:, t0:t1], dx[k][:].indirect(pos1_sb[:, t0 // 16 : t1 // 16]), COPY)
 
         def add_second(k, t0=0, t1=T):
             if t0 == 0:
-                total[k] = stage.tile([P, T], F32, name="total")
+                total[k] = shared.tile([P, T], F32, name=f"total_{k}", align_bytes=64, offset=(TOTAL_AT + 3 * k) * KB)
             second = dx[k][:].indirect(pos2_sb[:, t0 // 16 : t1 // 16])
             nc.vector.tensor_tensor(total[k][:, t0:t1], second, first[k][:, t0:t1], ADD)
             nc.sync.dma_start(out=out[k * P : (k + 1) * P, t0:t1], in_=total[k][:, t0:t1])
 
-        gather_plain(0, 0)
+        def first_layer(b0, b1):
+            for b in range(b0, b1):
+                product_dh(b)
+            for b in range(b0, b1):
+                turn_dh(b)
+
+        for j in range(PACK):
+            gather("c1s0", j, True)
+            gather("e4s0", j, True)
+        for group in ("c0s0", "c0s1", "c1s1", "e4s1"):
+            gather_on_scalar(group)
+
+        def make_slope(c):
+            nc.gpsimd.tensor_scalar(slope[c][:], saved[c][:], FLOAT_MAX, 0.0, MIN, MAX)
+
         make_slope(0)
+        for group in ("c0s0", "e4s0", "c0s1"):
+            apply_gate(group)
+        for group in ("c0s0", "e4s0", "c0s1"):
+            quantise_g(group)
         make_slope(1)
-        gather(1)
-        first_layer(0)
-        for b in range(2, 7):
-            make_slope(b)
-        gather(2)
-        first_layer(1)
-        make_slope(7)
-        gather(3)
-        quantise_g(2)
-        for b in range(8, 12):
-            make_slope(b)
-        gather(4)
-        for b in range(CHUNK_BLOCKS, 2 * CHUNK_BLOCKS):
-            product_dh(b, 0)
-        first_layer(3)
-        gather(5)
-        first_layer(4)
-        gather(6)
-        for b in (4, 5, 2):
+        make_slope(2)
+        first_layer(0, 4)
+        gather_on_scalar("e5s0")
+        for group in ("c1s0", "c1s1", "e4s1"):
+            apply_gate(group)
+        for group in ("c1s0", "c1s1", "e4s1"):
+            quantise_g(group)
+        first_layer(4, 8)
+        gather_on_scalar("e5s1")
+        for b in range(0, 3):
             make_da(b)
-        first_layer(7)
-        nc.vector.tensor_tensor(da[2][:, SHORT_SHARE:], dh_copy[2][:, SHORT_SHARE:], slope[2][:, SHORT_SHARE:], MULT)
-        turn_da(4, 5)
-
-        turn_da(2)
-        for blocks in ((6, 7), (0, 1), (8, 9), (10,), (11,), (3,)):
-            for b in blocks:
-                make_da(b)
-            turn_da(*blocks)
-
-        quantise_da(4)
-        quantise_da(6)
-        product_dx(4, 8, 0, 2)
+        apply_gate("e5s0")
+        for b in range(3, 6):
+            make_da(b)
         quantise_da(0)
+        quantise_da(1)
+        first_layer(8, 10)
+        make_da(6)
+        apply_gate("e5s1")
+        quantise_g("e5s0")
+        quantise_g("e5s1")
+        for k in range(2):
+            product_dx(0, 2, k, 5 + k, nc.scalar.copy)
+        first_layer(10, 12)
+        make_da(7)
         quantise_da(2)
-        quantise_da(8)
-        product_dx(8, 10, 0, 3)
-        quantise_da(10)
-        product_dx(10, 12, 0, 6)
+        make_da(8)
         quantise_da(3)
-        product_dx(0, 3, 0, 4, copy=nc.vector.tensor_copy)
-        product_dx(3, 4, 0, 5, copy=nc.vector.tensor_copy)
-        for k in range(1, K // P):
-            for m, b0 in enumerate((4, 8, 0)):
-                product_dx(b0, b0 + CHUNK_BLOCKS, k, LATE_BANKS[k - 1][m])
+        for k in range(2, 4):
+            product_dx(0, 2, k, 3 + k, nc.scalar.copy)
+        for b in range(9, 12):
+            make_da(b)
+        for k in range(K // P):
+            product_dx(2, 4, k, (4, 2, 5, 6)[k], nc.scalar.copy)
+        quantise_da(4)
+        quantise_da(5)
 
+        product_dx(4, 6, 0, 3, nc.vector.tensor_copy)
+        product_dx(4, 6, 1, 7, nc.vector.tensor_copy)
+        product_dx(4, 6, 2, 0, nc.vector.tensor_copy)
         fetch_first(0, 0, T // 2)
         fetch_first(0, T // 2, T)
         add_second(0, 0, T // 2)
         add_second(0, T // 2, T)
         fetch_first(1)
-        for k in range(2, K // P):
-            fetch_first(k)
-            add_second(k - 1)
+        add_second(1)
+        product_dx(4, 6, 3, 1, nc.scalar.copy)
+        fetch_first(2)
+        add_second(2)
         done = 0
         for width in LAST_STORES:
+            fetch_first(K // P - 1, done, done + width)
             add_second(K // P - 1, done, done + width)
             done += width

@@ -28,28 +28,34 @@ CHUNK = 512
 BLOCKS = S // P
 KB = 1024
 BANK = 2 * KB
-GROUPS = {
+GATHERS = {
     "c0s0": (0, 512, 0),
-    "c0s1": (0, 512, 1),
     "c1s0": (512, 512, 0),
-    "c1s1": (512, 512, 1),
     "e4s0": (1024, 256, 0),
-    "e4s1": (1024, 256, 1),
     "e5s0": (1280, 256, 0),
-    "e5s1": (1280, 256, 1),
+    "e0s1": (0, 256, 1),
+    "e1s1": (256, 256, 1),
+    "e2s1": (512, 256, 1),
+    "e3s1": (768, 256, 1),
+    "e4s1": (1024, 256, 1),
+    "b10s1": (1280, 128, 1),
+    "b11s1": (1408, 128, 1),
 }
-LAST_STORES = (448, 192, 128)
+LAST_STORES = (384, 256, 128)
 
-PICKED_AT = {"c0s0": 24, "c0s1": 32, "c1s1": 40, "e4s1": 48, "c1s0": 52, "e4s0": 60, "e5s0": 24, "e5s1": 32}
-DH_AT = (24, 26, 28, 30, 32, 34, 36, 38, 52, 54, 56, 58)
-FIRST_AT, TOTAL_AT = 40, 52
-SAVED_AT = 64
-ROUNDED_AT = {"c0s0": 90, "c0s1": 100, "e4s0": 110, "c1s0": 88, "c1s1": 110, "e4s1": 92, "e5s0": 88, "e5s1": 110}
-DA_AT = (92, 112, 114, 116, 126, 128)
-SLOPE_AT = (118, 94, 102)
-SCALES_AT = {"c0s0": 0, "c0s1": 1, "e4s0": 2, "c1s0": 16, "c1s1": 17, "e4s1": 18, "e5s0": 19, "e5s1": 20}
-DH_BANK = (3, 4, 5, 6, 3, 4, 5, 6, 3, 4, 2, 3)
-TURN_BANK = (7, 0, 1, 7, 0, 1, 7, 0, 1, 7, 0, 1)
+PICKED_AT = {
+    "c0s0": 24, "e0s1": 32, "e1s1": 36, "e2s1": 40, "c1s0": 44, "e4s0": 52,
+    "e3s1": 56, "e4s1": 60, "e5s0": 64, "b10s1": 68, "b11s1": 70,
+}
+CODES_AT = {(0, 1): 56, (256, 1): 60, (512, 1): 64, (768, 1): 69.5}
+DH_AT = 24
+FIRST_AT, TOTAL_AT = 48, 60
+SAVED_AT = 72
+SLOPE_AT = 96
+ROUNDED_AT = {(256, 1): 96, (512, 1): 103, **{(e * C, 0): 120 for e in range(E)}}
+DA_AT = {0: 111, 1: 116}
+DH_BANK = (3, 4, 5, 6, 3, 4, 5, 6, 3, 4, 5, 3)
+TURN_BANK = (7, 0, 7, 0, 1, 7, 0, 1, 7, 0, 1, 7)
 
 
 def tile_moe_bdx_mlp_relu2_kernel(
@@ -73,19 +79,18 @@ def tile_moe_bdx_mlp_relu2_kernel(
         w2 = [keep.tile([P, 2, 2 * H], U8, name=f"w2_{e}", align_bytes=64) for e in range(E)]
         w1 = keep.tile([P, E, 2 * K], U8, name="w1", align_bytes=64)
         dy = [shared.tile([P, T], F32, name=f"dy_{m}", align_bytes=64, offset=(m % 4 * 6 + m // 4 * 3) * KB) for m in range(N // P)]
-        saved, slope = [], []
-        for c in range(S // CHUNK):
-            at = (SAVED_AT + c * 8) * KB
-            saved.append(shared.tile([P, PACK, CHUNK], F32, name=f"saved_{c}", align_bytes=64, offset=at))
-            slope.append(shared.tile([P, PACK, CHUNK], F32, name=f"slope_{c}", align_bytes=64, offset=SLOPE_AT[c] * KB))
+        saved = [
+            shared.tile([P, PACK, CHUNK], F32, name=f"saved_{c}", align_bytes=64, offset=(SAVED_AT + 8 * c) * KB)
+            for c in range(S // CHUNK)
+        ]
 
         apart = keep.tile([P, P], F32, name="apart")
-        apart_squared = shared.tile([P, 7 * KB], F32, name="apart_squared", align_bytes=64, offset=24 * KB)[:, :P]
+        apart_squared = shared.tile([P, 5 * KB], F32, name="apart_squared", align_bytes=64, offset=24 * KB)[:, :P]
         nc.gpsimd.iota(apart[:], pattern=[[1, P]], base=0, channel_multiplier=-1, allow_small_or_imprecise_dtypes=True)
         nc.gpsimd.tensor_tensor(apart_squared, apart[:], apart[:], MULT)
         nc.scalar.activation(ident[:], apart_squared, RELU, bias=1.0, scale=-1.0)
-        nc.gpsimd.memset(w2_sc[:].rearrange("p g i -> p (g i)").bitcast(I32), 0)
-        nc.gpsimd.memset(w1_sc[:].rearrange("p g i -> p (g i)").bitcast(I32), 0)
+        nc.vector.memset(w2_sc[:].rearrange("p g i -> p (g i)").bitcast(I32), 0)
+        nc.vector.memset(w1_sc[:].rearrange("p g i -> p (g i)").bitcast(I32), 0)
 
         dy_rows = dyT.rearrange("(s p j) t -> s j p t", s=2, j=PACK)
         a_rows = a.rearrange("(p t) c -> p t c", t=PACK)
@@ -100,13 +105,12 @@ def tile_moe_bdx_mlp_relu2_kernel(
             nc.sync.dma_start(out=dy[m][:], in_=dy_rows[m // PACK, m % PACK])
             if m == 0:
                 nc.sync.dma_start(out=gate_col[:], in_=gate[0].rearrange("(q n b) -> n q b", n=P, b=PACK))
-        nc.sync.dma_start(out=saved[0][:], in_=a_rows[:, :, :CHUNK])
         load_scales(w2_sc, w2_scales)
         for e in range(E):
             nc.sync.dma_start(out=w2[e][:].bitcast(I32), in_=w2_words[e].rearrange("s p b -> p s b").bitcast(I32))
-            if e == 1:
-                nc.sync.dma_start(out=saved[1][:], in_=a_rows[:, :, CHUNK : 2 * CHUNK])
-                nc.sync.dma_start(out=saved[2][:], in_=a_rows[:, :, 2 * CHUNK :])
+            if e in (1, 2, 5):
+                c = (1, 2, 5).index(e)
+                nc.sync.dma_start(out=saved[c][:], in_=a_rows[:, :, c * CHUNK : (c + 1) * CHUNK])
         load_scales(w1_sc, w1_scales)
         nc.sync.dma_start(out=w1[:].bitcast(I32), in_=w1_words.rearrange("e s p b -> p (e s) b").bitcast(I32))
         nc.sync.dma_start(pos1_sb[:], pos1)
@@ -117,13 +121,17 @@ def tile_moe_bdx_mlp_relu2_kernel(
             for b in range(PACK):
                 nc.tensor.transpose(spread[q][:, b, :], gate_col[:, q, b : b + 1].to_broadcast([P, P]), ident[:])
 
-        picked, rounded, g_codes, dh_sb, turned, da, da_codes = {}, {}, {}, {}, {}, {}, {}
+        picked, rounded, g_codes, slope, dh, dh_sb, turned, da, da_codes = {}, {}, {}, {}, {}, {}, {}, {}, {}
+
+        def placed(shape, dtype, name, at):
+            if at is None:
+                return keep.tile(shape, dtype, name=name, align_bytes=64)
+            return shared.tile(shape, dtype, name=name, align_bytes=64, offset=int(at * KB))
 
         def gather(group, j, on_vector):
-            c0, n, s = GROUPS[group]
+            c0, n, s = GATHERS[group]
             if j == 0:
-                at = PICKED_AT[group] * KB
-                picked[group] = shared.tile([P, PACK, n], F32, name=f"picked_{group}", align_bytes=64, offset=at)
+                picked[group] = placed([P, PACK, n], F32, f"picked_{group}", PICKED_AT[group])
             window = dy[PACK * s + j][:].indirect(offs_sb[:, c0 // 16 : (c0 + n) // 16])
             if on_vector:
                 nc.vector.tensor_copy(picked[group][:, j, :], window)
@@ -134,48 +142,51 @@ def tile_moe_bdx_mlp_relu2_kernel(
             for j in range(PACK):
                 gather(group, j, False)
 
-        def apply_gate(group):
-            c0, n, s = GROUPS[group]
+        def apply_gate(c0, s, n=C):
+            group = [g for g, (first, count, where) in GATHERS.items() if where == s and first <= c0 < first + count][0]
+            h = c0 - GATHERS[group][0]
             q, col = divmod(c0, CHUNK)
-            rounded[group] = shared.tile(
-                [P, n, PACK], BF16, name=f"rounded_{group}", align_bytes=64, offset=ROUNDED_AT[group] * KB
-            )
+            rounded[c0, s] = placed([P, n, PACK], BF16, f"rounded_{c0}_{s}", ROUNDED_AT.get((c0, s)))
             factor = spread[q][:, :, col // 4 : (col + n) // 4].rearrange("p i c -> p c i")
             nc.vector.tensor_tensor(
-                rounded[group][:].rearrange("p (c i) j -> p c j i", i=4),
-                picked[group][:].rearrange("p j (c i) -> p c j i", i=4),
+                rounded[c0, s][:].rearrange("p (c i) j -> p c j i", i=4),
+                picked[group][:, :, h : h + n].rearrange("p j (c i) -> p c j i", i=4),
                 factor.unsqueeze(2).to_broadcast([P, n // 4, PACK, 4]),
                 MULT,
             )
 
-        def quantise_g(group):
-            c0, n, s = GROUPS[group]
-            codes = keep.tile([P, n], U32, name=f"g_codes_{group}", align_bytes=64)
-            at = (SAVED_AT + SCALES_AT[group]) * KB
-            scales = shared.tile([P, n], U8, name=f"g_scales_{group}", align_bytes=64, offset=at)
+        def quantise_g(c0, s):
+            n = rounded[c0, s].shape[1]
+            codes = placed([P, n], U32, f"g_codes_{c0}_{s}", CODES_AT.get((c0, s)))
+            scales = keep.tile([P, n], U8, name=f"g_scales_{c0}_{s}", align_bytes=64)
             nc.vector.quantize_mx(
-                out=codes[:].bitcast(FP8X4), scales=scales[:], in_=rounded[group][:].rearrange("p c j -> p (c j)")
+                out=codes[:].bitcast(FP8X4), scales=scales[:], in_=rounded[c0, s][:].rearrange("p c j -> p (c j)")
             )
             for h in range(n // P):
                 cols = slice(h * P, (h + 1) * P)
                 g_codes[c0 // P + h, s] = (codes[:, cols], scales[:, cols])
 
-        def product_dh(b):
+        def make_slope(e):
+            slope[e] = placed([P, PACK, C], F32, f"slope_{e}", SLOPE_AT + 4 * e)
+            nc.gpsimd.tensor_scalar(slope[e][:], saved[e // 2][:, :, e % 2 * C : (e % 2 + 1) * C], FLOAT_MAX, 0.0, MIN, MAX)
+
+        def product_dh(b, s):
             e = b * P // C
-            dh = psum.tile([P, H], F32, name=f"dh_{b}", offset=DH_BANK[b] * BANK)
-            for s in range(2):
-                codes, scales = g_codes[b, s]
-                nc.tensor.matmul_mx(
-                    out=dh[:],
-                    lhsT=codes.bitcast(FP8X4),
-                    lhsT_scale=scales,
-                    rhs=w2[e][:, s, :].bitcast(FP4X4),
-                    rhs_scale=w2_sc[:, 2 * e + s, :],
-                    start=(s == 0),
-                    stop=(s == 1),
-                )
-            dh_sb[b] = shared.tile([P, PACK, P], F32, name=f"dh_sb_{b}", align_bytes=64, offset=DH_AT[b] * KB)
-            nc.scalar.activation(dh_sb[b][:], dh[:].rearrange("s (m t) -> s t m", t=PACK), COPY, scale=2.0)
+            if s == 0:
+                dh[b] = psum.tile([P, H], F32, name=f"dh_{b}", offset=DH_BANK[b] * BANK)
+            codes, scales = g_codes[b, s]
+            nc.tensor.matmul_mx(
+                out=dh[b][:],
+                lhsT=codes.bitcast(FP8X4),
+                lhsT_scale=scales,
+                rhs=w2[e][:, s, :].bitcast(FP4X4),
+                rhs_scale=w2_sc[:, 2 * e + s, :],
+                start=(s == 0),
+                stop=(s == 1),
+            )
+            if s == 1:
+                dh_sb[b] = placed([P, PACK, P], F32, f"dh_sb_{b}", DH_AT + 2 * b)
+                nc.scalar.activation(dh_sb[b][:], dh[b][:].rearrange("s (m t) -> s t m", t=PACK), COPY, scale=2.0)
 
         def turn_dh(b):
             turned[b] = psum.tile([P, PACK, P], F32, name=f"turned_{b}", offset=TURN_BANK[b] * BANK)
@@ -185,40 +196,42 @@ def tile_moe_bdx_mlp_relu2_kernel(
         def make_da(b):
             e, h = divmod(b, C // P)
             if h == 0:
-                da[e] = shared.tile([P, C, PACK], BF16, name=f"da_{e}", align_bytes=64, offset=DA_AT[e] * KB)
+                da[e] = placed([P, C, PACK], BF16, f"da_{e}", DA_AT.get(e))
             nc.vector.tensor_tensor(
                 da[e][:, h * P : (h + 1) * P, :].rearrange("p (c i) t -> p c t i", i=4),
                 turned[b][:].rearrange("p t (c i) -> p c t i", i=4),
-                slope[b // 4][:, :, b % 4 * P : (b % 4 + 1) * P].rearrange("p t (c i) -> p c t i", i=4),
+                slope[e][:, :, h * P : (h + 1) * P].rearrange("p t (c i) -> p c t i", i=4),
                 MULT,
             )
 
-        def quantise_da(e):
-            codes = keep.tile([P, C], U32, name=f"da_codes_{e}", align_bytes=64)
-            scales = keep.tile([P, C], U8, name=f"da_scales_{e}", align_bytes=64)
-            nc.vector.quantize_mx(
-                out=codes[:].bitcast(FP8X4), scales=scales[:], in_=da[e][:].rearrange("p c t -> p (c t)")
-            )
-            da_codes[e] = (codes, scales)
+        def quantise_da(b0, blocks=2):
+            e, h = divmod(b0, C // P)
+            codes = keep.tile([P, blocks * P], U32, name=f"da_codes_{b0}", align_bytes=64)
+            scales = keep.tile([P, blocks * P], U8, name=f"da_scales_{b0}", align_bytes=64)
+            values = da[e][:, h * P : (h + blocks) * P, :].rearrange("p c t -> p (c t)")
+            nc.vector.quantize_mx(out=codes[:].bitcast(FP8X4), scales=scales[:], in_=values)
+            da_codes[b0] = (codes, scales, blocks)
 
         dx = {}
 
-        def product_dx(e0, e1, k, bank, copy):
+        def product_dx(b0, b1, k, bank, copy):
             if k not in dx:
                 dx[k] = shared.tile([P, S], F32, name=f"dx_{k}", align_bytes=64, offset=k * 6 * KB)
-            acc = psum.tile([P, (e1 - e0) * C], F32, name=f"dx_{e0}_{k}", offset=bank * BANK)
-            for e in range(e0, e1):
-                codes, scales = da_codes[e]
-                nc.tensor.matmul_mx(
-                    out=acc[:, (e - e0) * C : (e - e0 + 1) * C],
-                    lhsT=w1[:, e, 2 * k * P : 2 * (k + 1) * P].bitcast(FP4X4),
-                    lhsT_scale=w1_sc[:, e, k * P : (k + 1) * P],
-                    rhs=codes[:].bitcast(FP8X4),
-                    rhs_scale=scales[:],
-                    start=True,
-                    stop=True,
-                )
-            copy(dx[k][:, e0 * C : e1 * C], acc[:])
+            acc = psum.tile([P, (b1 - b0) * P], F32, name=f"dx_{b0}_{k}", offset=bank * BANK)
+            for b in range(b0, b1):
+                if b in da_codes:
+                    codes, scales, blocks = da_codes[b]
+                    e = b * P // C
+                    nc.tensor.matmul_mx(
+                        out=acc[:, (b - b0) * P : (b - b0 + blocks) * P],
+                        lhsT=w1[:, e, 2 * k * P : 2 * (k + 1) * P].bitcast(FP4X4),
+                        lhsT_scale=w1_sc[:, e, k * P : (k + 1) * P],
+                        rhs=codes[:].bitcast(FP8X4),
+                        rhs_scale=scales[:],
+                        start=True,
+                        stop=True,
+                    )
+            copy(dx[k][:, b0 * P : b1 * P], acc[:])
 
         first, total = {}, {}
 
@@ -236,74 +249,75 @@ def tile_moe_bdx_mlp_relu2_kernel(
 
         def first_layer(b0, b1):
             for b in range(b0, b1):
-                product_dh(b)
+                if b not in dh:
+                    product_dh(b, 0)
+                product_dh(b, 1)
             for b in range(b0, b1):
                 turn_dh(b)
 
         for j in range(PACK):
             gather("c1s0", j, True)
             gather("e4s0", j, True)
-        for group in ("c0s0", "c0s1", "c1s1", "e4s1"):
+        for group in ("c0s0", "e0s1", "e1s1", "e2s1"):
             gather_on_scalar(group)
 
-        def make_slope(c):
-            nc.gpsimd.tensor_scalar(slope[c][:], saved[c][:], FLOAT_MAX, 0.0, MIN, MAX)
+        later = {0: ("e3s1",), 1: ("e4s1",), 2: ("e5s0",), 3: ("b10s1", "b11s1"), 4: ()}
+        slopes = {0: (), 1: (0,), 2: (1, 2), 3: (3, 4), 4: (5,)}
+        for e in range(E - 1):
+            if e >= 3:
+                make_da(2 * e - 6)
+                make_da(2 * e - 5)
+            apply_gate(e * C, 0)
+            apply_gate(e * C, 1)
+            quantise_g(e * C, 0)
+            quantise_g(e * C, 1)
+            if e >= 3:
+                quantise_da(2 * e - 6)
+            for m in slopes[e]:
+                make_slope(m)
+            first_layer(2 * e, 2 * e + 2)
+            for group in later[e]:
+                gather_on_scalar(group)
 
-        make_slope(0)
-        for group in ("c0s0", "e4s0", "c0s1"):
-            apply_gate(group)
-        for group in ("c0s0", "e4s0", "c0s1"):
-            quantise_g(group)
-        make_slope(1)
-        make_slope(2)
-        first_layer(0, 4)
-        gather_on_scalar("e5s0")
-        for group in ("c1s0", "c1s1", "e4s1"):
-            apply_gate(group)
-        for group in ("c1s0", "c1s1", "e4s1"):
-            quantise_g(group)
-        first_layer(4, 8)
-        gather_on_scalar("e5s1")
-        for b in range(0, 3):
-            make_da(b)
-        apply_gate("e5s0")
-        for b in range(3, 6):
-            make_da(b)
-        quantise_da(0)
-        quantise_da(1)
-        first_layer(8, 10)
+        last = (E - 1) * C
+        apply_gate(last, 0)
+        make_da(4)
+        quantise_g(last, 0)
+        product_dh(10, 0)
+        product_dx(0, 4, 0, 6, nc.scalar.copy)
+        apply_gate(last, 1, P)
+        make_da(5)
+        quantise_g(last, 1)
+        product_dh(11, 0)
+        first_layer(10, 11)
+        product_dx(0, 4, 1, 4, nc.scalar.copy)
+        product_dx(0, 4, 2, 6, nc.scalar.copy)
+        apply_gate(last + P, 1, P)
         make_da(6)
-        apply_gate("e5s1")
-        quantise_g("e5s0")
-        quantise_g("e5s1")
-        for k in range(2):
-            product_dx(0, 2, k, 5 + k, nc.scalar.copy)
-        first_layer(10, 12)
+        quantise_g(last + P, 1)
+        first_layer(11, 12)
+        product_dx(0, 4, 3, 2, nc.scalar.copy)
         make_da(7)
-        quantise_da(2)
-        make_da(8)
-        quantise_da(3)
-        for k in range(2, 4):
-            product_dx(0, 2, k, 3 + k, nc.scalar.copy)
-        for b in range(9, 12):
-            make_da(b)
-        for k in range(K // P):
-            product_dx(2, 4, k, (4, 2, 5, 6)[k], nc.scalar.copy)
         quantise_da(4)
-        quantise_da(5)
-
-        product_dx(4, 6, 0, 3, nc.vector.tensor_copy)
-        product_dx(4, 6, 1, 7, nc.vector.tensor_copy)
-        product_dx(4, 6, 2, 0, nc.vector.tensor_copy)
-        fetch_first(0, 0, T // 2)
-        fetch_first(0, T // 2, T)
-        add_second(0, 0, T // 2)
-        add_second(0, T // 2, T)
-        fetch_first(1)
-        add_second(1)
-        product_dx(4, 6, 3, 1, nc.scalar.copy)
-        fetch_first(2)
-        add_second(2)
+        quantise_da(6)
+        make_da(8)
+        make_da(9)
+        make_da(10)
+        quantise_da(8)
+        make_da(11)
+        quantise_da(10, 1)
+        for k in range(3):
+            product_dx(4, 8, k, (5, 4, 6)[k], nc.scalar.copy)
+        quantise_da(11, 1)
+        product_dx(8, 11, 0, 2, nc.scalar.copy)
+        product_dx(4, 8, 3, 3, nc.vector.tensor_copy)
+        product_dx(11, 12, 0, 0, nc.vector.tensor_copy)
+        for k in range(1, K // P):
+            product_dx(8, 12, k, (1, 5, 7)[k - 1], nc.vector.tensor_copy)
+        for k in range(K // P - 1):
+            for t0 in (0, T // 2):
+                fetch_first(k, t0, t0 + T // 2)
+                add_second(k, t0, t0 + T // 2)
         done = 0
         for width in LAST_STORES:
             fetch_first(K // P - 1, done, done + width)

from contextlib import ExitStack

import concourse.mybir as mybir

N, T, E, C, H, K = 1024, 768, 6, 256, 512, 512
S = E * C
P = 128
PACK = 4
FLOPS = 2 * S * (N * H + H * K)

F32 = mybir.dt.float32
BF16 = mybir.dt.bfloat16
I32 = mybir.dt.int32
U32 = mybir.dt.uint32
U16 = mybir.dt.uint16
U8 = mybir.dt.uint8
FP8X4 = mybir.dt.float8_e4m3fn_x4
FP4X4 = mybir.dt.float4_e2m1fn_x4
MULT = mybir.AluOpType.mult
ADD = mybir.AluOpType.add
MAX = mybir.AluOpType.max
MIN = mybir.AluOpType.min
FLOAT_MAX = (2.0 - 2.0**-23) * 2.0**127
COPY = mybir.ActivationFunctionType.Copy
RELU = mybir.ActivationFunctionType.Relu

CHUNK = 512
BLOCKS = S // P
KB = 1024
BANK = 2 * KB
GATHERS = {
    "c0s0": (0, 512, 0),
    "c1s0": (512, 512, 0),
    "e4s0": (1024, 256, 0),
    "e5s0": (1280, 256, 0),
    "e0s1": (0, 256, 1),
    "e1s1": (256, 256, 1),
    "e2s1": (512, 256, 1),
    "e3s1": (768, 256, 1),
    "e4s1": (1024, 256, 1),
    "b10s1": (1280, 128, 1),
    "b11s1": (1408, 128, 1),
}
LAST_STORES = (384, 256, 128)

PICKED_AT = {
    "c0s0": 24, "e0s1": 32, "e1s1": 36, "e2s1": 40, "c1s0": 44, "e4s0": 52,
    "e3s1": 56, "e4s1": 60, "e5s0": 64, "b10s1": 68, "b11s1": 70,
}
CODES_AT = {(0, 1): 56, (256, 1): 60, (512, 1): 64, (768, 1): 69.5}
DH_AT = 24
FIRST_AT, TOTAL_AT = 48, 60
SAVED_AT = 72
SLOPE_AT = 96
ROUNDED_AT = {(256, 1): 96, (512, 1): 103, **{(e * C, 0): 120 for e in range(E)}}
DA_AT = {0: 111, 1: 116}
DH_BANK = (3, 4, 5, 6, 3, 4, 5, 6, 3, 4, 5, 3)
TURN_BANK = (7, 0, 7, 0, 1, 7, 0, 1, 7, 0, 1, 7)


def tile_moe_bdx_mlp_relu2_kernel(
    tc, dyT, a, w2_words, w2_scales, w1_words, w1_scales, gate, offs, pos1, pos2, out
):
    nc = tc.nc
    with ExitStack() as ctx:
        lists = ctx.enter_context(tc.tile_pool(name="lists", bufs=1))
        keep = ctx.enter_context(tc.tile_pool(name="keep", bufs=1))
        shared = ctx.enter_context(tc.tile_pool(name="shared", bufs=1))
        psum = ctx.enter_context(tc.psum_pool(name="psum", bufs=1))

        offs_sb = lists.tile([P, S // 16], U16, name="offs_sb")
        pos1_sb = lists.tile([P, T // 16], U16, name="pos1_sb")
        pos2_sb = lists.tile([P, T // 16], U16, name="pos2_sb")

        ident = keep.tile([P, P], F32, name="ident")
        gate_col = keep.tile([P, S // CHUNK, PACK], F32, name="gate_col")
        w2_sc = keep.tile([P, 2 * E, H], U8, name="w2_sc", align_bytes=64)
        w1_sc = keep.tile([P, E, K], U8, name="w1_sc", align_bytes=64)
        w2 = [keep.tile([P, 2, 2 * H], U8, name=f"w2_{e}", align_bytes=64) for e in range(E)]
        w1 = keep.tile([P, E, 2 * K], U8, name="w1", align_bytes=64)
        dy = [shared.tile([P, T], F32, name=f"dy_{m}", align_bytes=64, offset=(m % 4 * 6 + m // 4 * 3) * KB) for m in range(N // P)]
        saved = [
            shared.tile([P, PACK, CHUNK], F32, name=f"saved_{c}", align_bytes=64, offset=(SAVED_AT + 8 * c) * KB)
            for c in range(S // CHUNK)
        ]

        apart = keep.tile([P, P], F32, name="apart")
        apart_squared = shared.tile([P, 5 * KB], F32, name="apart_squared", align_bytes=64, offset=24 * KB)[:, :P]
        nc.gpsimd.iota(apart[:], pattern=[[1, P]], base=0, channel_multiplier=-1, allow_small_or_imprecise_dtypes=True)
        nc.gpsimd.tensor_tensor(apart_squared, apart[:], apart[:], MULT)
        nc.scalar.activation(ident[:], apart_squared, RELU, bias=1.0, scale=-1.0)
        nc.vector.memset(w2_sc[:].rearrange("p g i -> p (g i)").bitcast(I32), 0)
        nc.vector.memset(w1_sc[:].rearrange("p g i -> p (g i)").bitcast(I32), 0)

        dy_rows = dyT.rearrange("(s p j) t -> s j p t", s=2, j=PACK)
        a_rows = a.rearrange("(p t) c -> p t c", t=PACK)

        def load_scales(plane, scales):
            rows = scales.bitcast(I32).rearrange("e s f i -> f (e s) i")
            for q in range(4):
                nc.sync.dma_start(out=plane[32 * q : 32 * q + 4].bitcast(I32), in_=rows[4 * q : 4 * q + 4])

        nc.sync.dma_start(offs_sb[:], offs)
        for m in range(N // P):
            nc.sync.dma_start(out=dy[m][:], in_=dy_rows[m // PACK, m % PACK])
            if m == 0:
                nc.sync.dma_start(out=gate_col[:], in_=gate[0].rearrange("(q n b) -> n q b", n=P, b=PACK))
        load_scales(w2_sc, w2_scales)
        for e in range(E):
            nc.sync.dma_start(out=w2[e][:].bitcast(I32), in_=w2_words[e].rearrange("s p b -> p s b").bitcast(I32))
            if e in (1, 2, 5):
                c = (1, 2, 5).index(e)
                nc.sync.dma_start(out=saved[c][:], in_=a_rows[:, :, c * CHUNK : (c + 1) * CHUNK])
        load_scales(w1_sc, w1_scales)
        nc.sync.dma_start(out=w1[:].bitcast(I32), in_=w1_words.rearrange("e s p b -> p (e s) b").bitcast(I32))
        nc.sync.dma_start(pos1_sb[:], pos1)
        nc.sync.dma_start(pos2_sb[:], pos2)

        spread = [psum.tile([P, PACK, P], F32, name=f"spread_{q}", offset=q * BANK) for q in range(S // CHUNK)]
        for q in range(S // CHUNK):
            for b in range(PACK):
                nc.tensor.transpose(spread[q][:, b, :], gate_col[:, q, b : b + 1].to_broadcast([P, P]), ident[:])

        picked, rounded, g_codes, slope, dh, dh_sb, turned, da, da_codes = {}, {}, {}, {}, {}, {}, {}, {}, {}

        def placed(shape, dtype, name, at):
            if at is None:
                return keep.tile(shape, dtype, name=name, align_bytes=64)
            return shared.tile(shape, dtype, name=name, align_bytes=64, offset=int(at * KB))

        def gather(group, j, on_vector):
            c0, n, s = GATHERS[group]
            if j == 0:
                picked[group] = placed([P, PACK, n], F32, f"picked_{group}", PICKED_AT[group])
            window = dy[PACK * s + j][:].indirect(offs_sb[:, c0 // 16 : (c0 + n) // 16])
            if on_vector:
                nc.vector.tensor_copy(picked[group][:, j, :], window)
            else:
                nc.scalar.activation(picked[group][:, j, :], window, COPY)

        def gather_on_scalar(group):
            for j in range(PACK):
                gather(group, j, False)

        def apply_gate(c0, s, n=C):
            group = [g for g, (first, count, where) in GATHERS.items() if where == s and first <= c0 < first + count][0]
            h = c0 - GATHERS[group][0]
            q, col = divmod(c0, CHUNK)
            rounded[c0, s] = placed([P, n, PACK], BF16, f"rounded_{c0}_{s}", ROUNDED_AT.get((c0, s)))
            factor = spread[q][:, :, col // 4 : (col + n) // 4].rearrange("p i c -> p c i")
            nc.vector.tensor_tensor(
                rounded[c0, s][:].rearrange("p (c i) j -> p c j i", i=4),
                picked[group][:, :, h : h + n].rearrange("p j (c i) -> p c j i", i=4),
                factor.unsqueeze(2).to_broadcast([P, n // 4, PACK, 4]),
                MULT,
            )

        def quantise_g(c0, s):
            n = rounded[c0, s].shape[1]
            codes = placed([P, n], U32, f"g_codes_{c0}_{s}", CODES_AT.get((c0, s)))
            scales = keep.tile([P, n], U8, name=f"g_scales_{c0}_{s}", align_bytes=64)
            nc.vector.quantize_mx(
                out=codes[:].bitcast(FP8X4), scales=scales[:], in_=rounded[c0, s][:].rearrange("p c j -> p (c j)")
            )
            for h in range(n // P):
                cols = slice(h * P, (h + 1) * P)
                g_codes[c0 // P + h, s] = (codes[:, cols], scales[:, cols])

        def make_slope(e):
            slope[e] = placed([P, PACK, C], F32, f"slope_{e}", SLOPE_AT + 4 * e)
            nc.gpsimd.tensor_scalar(slope[e][:], saved[e // 2][:, :, e % 2 * C : (e % 2 + 1) * C], FLOAT_MAX, 0.0, MIN, MAX)

        def product_dh(b, s):
            e = b * P // C
            if s == 0:
                dh[b] = psum.tile([P, H], F32, name=f"dh_{b}", offset=DH_BANK[b] * BANK)
            codes, scales = g_codes[b, s]
            nc.tensor.matmul_mx(
                out=dh[b][:],
                lhsT=codes.bitcast(FP8X4),
                lhsT_scale=scales,
                rhs=w2[e][:, s, :].bitcast(FP4X4),
                rhs_scale=w2_sc[:, 2 * e + s, :],
                start=(s == 0),
                stop=(s == 1),
            )
            if s == 1:
                dh_sb[b] = placed([P, PACK, P], F32, f"dh_sb_{b}", DH_AT + 2 * b)
                nc.scalar.activation(dh_sb[b][:], dh[b][:].rearrange("s (m t) -> s t m", t=PACK), COPY, scale=2.0)

        def turn_dh(b):
            turned[b] = psum.tile([P, PACK, P], F32, name=f"turned_{b}", offset=TURN_BANK[b] * BANK)
            for t in range(PACK):
                nc.tensor.transpose(turned[b][:, t, :], dh_sb[b][:, t, :], ident[:])

        def make_da(b):
            e, h = divmod(b, C // P)
            if h == 0:
                da[e] = placed([P, C, PACK], BF16, f"da_{e}", DA_AT.get(e))
            nc.vector.tensor_tensor(
                da[e][:, h * P : (h + 1) * P, :].rearrange("p (c i) t -> p c t i", i=4),
                turned[b][:].rearrange("p t (c i) -> p c t i", i=4),
                slope[e][:, :, h * P : (h + 1) * P].rearrange("p t (c i) -> p c t i", i=4),
                MULT,
            )

        def quantise_da(b0, blocks=2):
            e, h = divmod(b0, C // P)
            codes = keep.tile([P, blocks * P], U32, name=f"da_codes_{b0}", align_bytes=64)
            scales = keep.tile([P, blocks * P], U8, name=f"da_scales_{b0}", align_bytes=64)
            values = da[e][:, h * P : (h + blocks) * P, :].rearrange("p c t -> p (c t)")
            nc.vector.quantize_mx(out=codes[:].bitcast(FP8X4), scales=scales[:], in_=values)
            da_codes[b0] = (codes, scales, blocks)

        dx = {}

        def product_dx(b0, b1, k, bank, copy):
            if k not in dx:
                dx[k] = shared.tile([P, S], F32, name=f"dx_{k}", align_bytes=64, offset=k * 6 * KB)
            acc = psum.tile([P, (b1 - b0) * P], F32, name=f"dx_{b0}_{k}", offset=bank * BANK)
            for b in range(b0, b1):
                if b in da_codes:
                    codes, scales, blocks = da_codes[b]
                    e = b * P // C
                    nc.tensor.matmul_mx(
                        out=acc[:, (b - b0) * P : (b - b0 + blocks) * P],
                        lhsT=w1[:, e, 2 * k * P : 2 * (k + 1) * P].bitcast(FP4X4),
                        lhsT_scale=w1_sc[:, e, k * P : (k + 1) * P],
                        rhs=codes[:].bitcast(FP8X4),
                        rhs_scale=scales[:],
                        start=True,
                        stop=True,
                    )
            copy(dx[k][:, b0 * P : b1 * P], acc[:])

        first, total = {}, {}

        def fetch_first(k, t0=0, t1=T):
            if t0 == 0:
                first[k] = shared.tile([P, T], F32, name=f"first_{k}", align_bytes=64, offset=(FIRST_AT + 3 * k) * KB)
            nc.scalar.activation(first[k][:, t0:t1], dx[k][:].indirect(pos1_sb[:, t0 // 16 : t1 // 16]), COPY)

        def add_second(k, t0=0, t1=T):
            if t0 == 0:
                total[k] = shared.tile([P, T], F32, name=f"total_{k}", align_bytes=64, offset=(TOTAL_AT + 3 * k) * KB)
            second = dx[k][:].indirect(pos2_sb[:, t0 // 16 : t1 // 16])
            nc.vector.tensor_tensor(total[k][:, t0:t1], second, first[k][:, t0:t1], ADD)
            nc.sync.dma_start(out=out[k * P : (k + 1) * P, t0:t1], in_=total[k][:, t0:t1])

        def first_layer(b0, b1):
            for b in range(b0, b1):
                if b not in dh:
                    product_dh(b, 0)
                product_dh(b, 1)
            for b in range(b0, b1):
                turn_dh(b)

        for j in range(PACK):
            gather("c1s0", j, True)
            gather("e4s0", j, True)
        for group in ("c0s0", "e0s1", "e1s1", "e2s1"):
            gather_on_scalar(group)

        later = {0: ("e3s1",), 1: ("e4s1",), 2: ("e5s0",), 3: ("b10s1", "b11s1"), 4: ()}
        slopes = {0: (), 1: (0,), 2: (1, 2), 3: (3, 4), 4: (5,)}
        for e in range(E - 1):
            if e >= 3:
                make_da(2 * e - 6)
                make_da(2 * e - 5)
            apply_gate(e * C, 0)
            apply_gate(e * C, 1)
            quantise_g(e * C, 0)
            quantise_g(e * C, 1)
            if e >= 3:
                quantise_da(2 * e - 6)
            for m in slopes[e]:
                make_slope(m)
            first_layer(2 * e, 2 * e + 2)
            for group in later[e]:
                gather_on_scalar(group)

        last = (E - 1) * C
        apply_gate(last, 0)
        make_da(4)
        quantise_g(last, 0)
        product_dh(10, 0)
        product_dx(0, 4, 0, 6, nc.scalar.copy)
        apply_gate(last, 1, P)
        make_da(5)
        quantise_g(last, 1)
        product_dh(11, 0)
        first_layer(10, 11)
        product_dx(0, 4, 1, 4, nc.scalar.copy)
        product_dx(0, 4, 2, 6, nc.scalar.copy)
        apply_gate(last + P, 1, P)
        make_da(6)
        quantise_g(last + P, 1)
        first_layer(11, 12)
        product_dx(0, 4, 3, 2, nc.scalar.copy)
        make_da(7)
        quantise_da(4)
        quantise_da(6)
        make_da(8)
        make_da(9)
        make_da(10)
        quantise_da(8)
        make_da(11)
        quantise_da(10, 1)
        for k in range(3):
            product_dx(4, 8, k, (5, 4, 6)[k], nc.scalar.copy)
        quantise_da(11, 1)
        product_dx(8, 11, 0, 2, nc.scalar.copy)
        product_dx(4, 8, 3, 3, nc.vector.tensor_copy)
        product_dx(11, 12, 0, 0, nc.vector.tensor_copy)
        for k in range(1, K // P):
            product_dx(8, 12, k, (1, 5, 7)[k - 1], nc.vector.tensor_copy)
        for k in range(K // P - 1):
            for t0 in (0, T // 2):
                fetch_first(k, t0, t0 + T // 2)
                add_second(k, t0, t0 + T // 2)
        done = 0
        for width in LAST_STORES:
            fetch_first(K // P - 1, done, done + width)
            add_second(K // P - 1, done, done + width)
            done += width
